import numpy as np, ml_dtypes
CORES = [3,7,11,15,131,135,139,143]
N = 8
BF = ml_dtypes.bfloat16
def gentries(a):
    return np.ascontiguousarray(a.reshape(8, 16, -1).transpose(0, 2, 1)).reshape(8, -1)
def gtable(e):
    e = np.asarray(e); return np.ascontiguousarray(e.reshape(8, -1, 16).transpose(0, 2, 1)).reshape(128, -1).astype(np.int32)
V, NB, S0, T, RO = 896, 1792, 256, 256, 3
def dist(b, c, v):
    pk = np.take_along_axis(b, c.reshape(N, 8, 1, 16 * T), 3).reshape(N, 8, 16, 16, T)
    return np.add.reduce(np.abs(pk - v[:, :, :, None, :]), axis=2)
def parts(rng):
    c = rng.integers(0, NB, (N, 8, 16, V)); p = rng.integers(0, V, (N, 8, 16, V)); sh = rng.integers(0, S0, (N, 8, V))
    b = rng.integers(0, 256, (N, 8, 16, NB)); h = rng.integers(600, 1150, (N, 8, 1, S0)) + rng.integers(-100, 101, (N, 8, 16, S0))
    v = rng.integers(0, 256, (N, 8, 16, T)); o = rng.integers(0, V, (N, 8, T)); dr = rng.integers(0, 256, (N, 8, 16, RO))
    return c, p, sh, b, h, v, o, dr
def apart(rng, sh):
    o = np.ascontiguousarray(np.argsort(rng.random((N, 8, V)), axis=-1)[..., :T]); lab = np.ascontiguousarray(np.argsort(rng.random((N, 8, S0)), axis=-1)[..., :T])
    np.put_along_axis(sh, o, lab, 2)
    return o, lab
def back(a):
    return np.swapaxes(a.reshape(N, N, T // N), 0, 1).reshape(N, T)
def trail(rng, g, c, p, sh, b, h, v, o):
    k = rng.integers(0, 3, (N, 1, V)); at = np.zeros((RO, N, T), np.int64); j = np.arange(RO * T); i = np.arange(T); m1 = min(S0, 2 * T)
    for q in range(N):
        u = rng.permutation(V)[:RO * T]; m = rng.permutation(S0)[:m1]
        at[:, q] = u.reshape(RO, T); sh[q, g, u] = m[j % m1]; k[q, 0, u] = j // m1
        if S0 == T and q % 2:
            x = u[T:2 * T]; sh[q, g, x] = m[i % (T // 2)]; k[q, 0, x] = 1 + i // (T // 2)
            at[2, q, :T // 2] = x[T // 2:]; k[q, 0, at[2, q, T // 2:]] = 1
    for t in range(RO - 1):
        to = back(at[t + 1])
        for q in range(N): p[q, g][:, at[t, q]] = to[q]
    b[:, g] = rng.integers(0, 64, (N, 16, NB)) + 32 + 80 * (np.arange(NB) % 3)
    c[:, g] = 3 * rng.integers(0, NB // 3, (N, 16, V)) + k
    v[:, g] = v[:, g] >> 4; h[:, g] = 0; o[:, g] = at[0]
def pack(c, p, sh, b, h, v, o, dr):
    def bf(x): return np.ascontiguousarray(x.reshape(N, 128, -1)).astype(np.float32).astype(BF)
    return {"rec": (p * 4096 + c).reshape(N, 128, V).astype(np.int32), "shp": sh.astype(np.int32), "box": bf(b), "bound": h.reshape(N, 128, S0).astype(np.int32),
            "tv": bf(v), "ob": np.stack([gtable(a) for a in o]), "dr": bf(dr)}
def setup_inputs(rng):
    return pack(*parts(rng))
def setup_inputs_ties(rng):
    c, p, sh, b, h, v, o, dr = parts(rng); o, lab = apart(rng, sh)
    c[:, :, 8:] = c[:, :, 7::-1].copy()
    v[..., :1] = np.take_along_axis(b, np.take_along_axis(c[:, :, 5], o[..., :1], 2)[:, :, None, :], 3)
    e = dist(b, np.take_along_axis(c, o[:, :, None, :], 3), v)
    m = rng.integers(0, 4, (N, 8, 1, T)); row = np.arange(16)[:, None]
    hit = np.where(m == 1, rng.random(e.shape) < 0.2, np.where(m == 2, row == 15, (m == 3) & (row == 0)))
    np.put_along_axis(h, lab[:, :, None, :] + np.zeros((1, 1, 16, 1), np.int64), np.maximum(e - 1 + hit, 0), 3)
    return pack(c, p, sh, b, h, v, o, dr)
def setup_inputs_crowd(rng):
    c, p, sh, b, h, v, o, dr = parts(rng); k = rng.permutation(V)[:12].reshape(4, 3); k[0] = k[0, 0]
    for j in range(4):
        o[:, 2 * j] = k[j][rng.integers(0, 3, (N, T))]; p[:, 2 * j] = k[j][rng.integers(0, 3, (N, 16, V))]
    sh[:, 1::2] = rng.choice(np.array([0, S0 - 1, S0 // 2]), (N, 4, V)); sh[:, 3] = rng.integers(0, S0, (N, 1))
    z = [1, 5, 7]
    b[:, z] = b[:, z] >> 3; v[:, z] = v[:, z] >> rng.integers(0, 4, (N, 3, 1, T)); h[:, z] = h[:, z] // 8
    return pack(c, p, sh, b, h, v, o, dr)
def setup_inputs_thin(rng):
    c, p, sh, b, h, v, o, dr = parts(rng); s2 = sh.copy(); o2, lab = apart(rng, s2)
    o[:, 3] = o2[:, 3]; sh[:, 3] = s2[:, 3]
    b[:, 3] = np.maximum(b[:, 3], 1); v[:, 3] = 0
    h[:, 0] = 0; h[:, 1] = 4080; h[:, 2, :, ::2] = 0; h[:, 2, :, 1::2] = 4080; h[:, 3] = 0
    h[:, 4] = 0; h[:, 4, 15] = 4080; h[:, 5] = 0; h[:, 5, 0] = 4080
    b[:, 6] = b[:, 6] >> (3 + np.arange(N) % 5)[:, None, None]; v[:, 6] = 255 - (v[:, 6] >> rng.integers(3, 8, (N, 1, T)))
    trail(rng, 7, c, p, sh, b, h, v, o)
    return pack(c, p, sh, b, h, v, o, dr)
def setup_inputs_ends(rng):
    c, p, sh, b, h, v, o, dr = parts(rng)
    c[:, ::3] = rng.choice(np.array([0, NB - 1]), (N, 3, 16, V)); p[:, 1:6:2] = rng.choice(np.array([0, V - 1]), (N, 3, 16, V))
    sh[:, 2:6:3] = rng.choice(np.array([0, S0 - 1]), (N, 2, V)); o[:, :3] = rng.choice(np.array([0, V - 1]), (N, 3, T))
    b[:, 4] = 0; v[:, 4] = 255; h[:, 4] = rng.choice(np.array([4079, 4080]), (N, 16, S0), p=np.array([0.96, 0.04]))
    b[:, 7] = rng.choice(np.array([0, 255]), (N, 16, NB)); v[:, 7] = rng.choice(np.array([0, 255]), (N, 16, T)); h[:, 7] = rng.integers(1000, 2100, (N, 16, S0))
    dr[:, ::2] = rng.choice(np.array([0, 255]), (N, 4, 16, RO))
    return pack(c, p, sh, b, h, v, o, dr)
def setup_inputs_spread(rng):
    c, p, sh, b, h, v, o, dr = parts(rng)
    b = b >> rng.integers(0, 8, (N, 8, 1, NB)); v = v >> rng.integers(0, 8, (N, 8, 1, T)); dr = dr >> rng.integers(0, 8, (N, 8, 1, RO))
    h = np.minimum(np.exp2(12 * rng.random((N, 8, 1, S0))) * (0.5 + rng.random((N, 8, 16, S0))), 4080).astype(np.int64)
    c = (NB * rng.random(c.shape) ** 2).astype(np.int64); p = (V * rng.random(p.shape) ** 3).astype(np.int64)
    sh = (S0 * rng.random(sh.shape) ** 2).astype(np.int64); o = (V * rng.random(o.shape) ** 3).astype(np.int64)
    return pack(c, p, sh, b, h, v, o, dr)
def check_inputs(d):
    bad = []
    for k, lo, hi in (("rec", 0, 4096 * V - 1), ("shp", 0, S0 - 1), ("box", 0, 255), ("bound", 0, 4080), ("tv", 0, 255), ("ob", 0, V - 1), ("dr", 0, 255)):
        x = np.asarray(d[k]).astype(np.float64)
        if not (np.min(x) >= lo and np.max(x) <= hi and np.all(np.floor(x) == x)): bad.append("range of " + k)
    if np.max(np.asarray(d["rec"]).astype(np.int64) & 4095) >= NB: bad.append("box numbers of rec")
    return bad
def reference(rec, shp, box, bound, tv, ob, dr):
    w = rec.astype(np.int64).reshape(N, 8, 16, V); sh = shp.astype(np.int64)
    b = np.zeros((N, 8, 16, NB + RO * T), np.int64); b[..., :NB] = box.astype(np.float32).astype(np.int64).reshape(N, 8, 16, NB)
    h = np.zeros((N, 8, 16, S0 + RO * T), np.int64); h[..., :S0] = bound.astype(np.int64).reshape(N, 8, 16, S0)
    nx = np.tile(np.arange(S0 + RO * T), (N, 8, 1))
    v = tv.astype(np.float32).astype(np.int64).reshape(N, 8, 16, T); o = np.stack([gentries(a) for a in ob]).astype(np.int64)
    drift = dr.astype(np.float32).astype(np.int64).reshape(N, 8, 16, RO)
    for t in range(RO):
        s = np.take_along_axis(sh, o, 2); n = np.take_along_axis(nx, s, 2)
        x = np.take_along_axis(w, o[:, :, None, :], 3)
        x = np.where((n != s)[:, :, None, :], np.roll(x, -1, axis=2), x)
        c = x & 4095; p = x >> 12; e = dist(b, c, v)
        hn = np.take_along_axis(h, n[:, :, None, :], 3); fit = e <= hn; has = np.any(fit, axis=2)
        a = np.where(has, np.argmax(fit, axis=2), np.argmin(e, axis=2))[:, :, None, :]
        ba = np.take_along_axis(b, np.take_along_axis(c, a, 2), 3); go = np.take_along_axis(p, a, 2)[:, :, 0]; hs = has[:, :, None, :]
        y = np.where((np.arange(16)[:, None] == a) & hs, p * 4096 + NB + T * t + np.arange(T), x)
        b[..., NB + T * t:NB + T * (t + 1)] = np.where(hs, (ba + v) >> 1, 0)
        makes = ~has & (np.take_along_axis(nx, n, 2) == n); wider = np.maximum(hn, e)
        for q in range(N):
            for g in range(8):
                i = np.unique(o[q, g], return_index=True)[1]
                w[q, g][:, o[q, g, i]] = y[q, g][:, i]; sh[q, g, o[q, g, i]] = n[q, g, i]
                j = np.flatnonzero(makes[q, g]); j = j[np.unique(n[q, g, j], return_index=True)[1]]
                h[q, g][:, S0 + T * t + j] = wider[q, g][:, j]; nx[q, g, n[q, g, j]] = S0 + T * t + j
        v = np.where(hs, (ba + drift[..., t:t + 1]) & 255, v); o = go
        if t < RO - 1:
            v = np.swapaxes(v.reshape(N, 8, 16, N, T // N), 0, 3).reshape(N, 8, 16, T)
            o = np.swapaxes(o.reshape(N, 8, N, T // N), 0, 2).reshape(N, 8, T)
    return {"yr": w.reshape(N, 128, V).astype(np.float32), "yh": h[..., S0:].reshape(N, 128, RO * T).astype(np.float32), "yv": v.reshape(N, 128, T).astype(np.float32).astype(BF)}

@@ -1,0 +1,679 @@
+import math
+from concourse.bass import DstId, RemoteDMATransfer
+from concourse.mybir import AluOpType as OP, ActivationFunctionType as AF
+
+N, V, NB, S0, TH, RO = 8, 896, 1792, 256, 256, 3
+F32, BF, I32, U16 = "float32", "bfloat16", "int32", "uint16"
+SLOT, SENT = 40, 36
+SEG = 18
+HS = 8 * SEG
+RHO = 1.8
+MAGIC = 12582912.0
+TBD = 1032
+WIDTHS = {
+    I32: dict(obi=16, reci=V, shi=56, bdi=S0, pi=8, lei=16, lli=8, xi=TH, ci=TH, wi=16, a1=64),
+    U16: dict(le=16, ll=8, lj=8, ow=48, cu=TH, oru=TH, sl=16, ox=16, oo=16, osa=16, osb=16),
+    BF: dict(sh1=56, sh2=V, shb=V + TH, boxw=2816, v0=TH, drb=8, dg=2048, k256=256, one=128, em=512, idb=128, bo=128, bob=128,
+             idbig=128, ib=384, dk=256, g24=24, hi=432, lo=HS, kp=2 * HS, kz=HS, vt=256, bg=4096, da=4096, eq=4096,
+             dh=520, dl=520, ha=TH, hb=TH, ht=512, hw=TH, hm=128, hu=TH,
+             sg=TH, cb=TH, sr=3 * TH, rot=TH, na=TH, oh=256, ff=2 * HS, yy=TH, ym=TH, vout=TH, ohs=TH, fl=TH, vis=TH),
+    F32: dict(rf=V + TH, tb=1544, drc=16, io=V, pc=16, jm=128, dm=128, idf=128, nidf=128, m2=128, rmi=128, qm=8, thrs=8, vq=HS,
+              xu=HS, hq=HS, dmz=HS, tmpc=2 * HS, iw=16, kk=48, ww=18, thr=256, thw=16, lef=16, owf=48, xf=TH, sm=TH,
+              sk=48, hv=TH, hr=TH, es=256, p16=256, me=16, tt=2 * HS, mm=2 * HS, s2=2 * HS, lq=256, a2=128, mc=TH, yr2=512,
+              ysb=TH, esb=TH, nbf=TH, wa=16, yhs=3 * TH),
+}
+SCRATCH = {k: ("sbuf", [128, n], d) for d, w in WIDTHS.items() for k, n in w.items()}
+SCRATCH.update({k: ("sbuf", [128, 16, SEG], F32) for k in ("ps", "e3")})
+SCRATCH.update({k: ("sbuf", [128, 8, SLOT], BF) for k in ("snd0", "snd1", "rcv0", "rcv1")})
+SCRATCH.update({k: ("psum", [128, 512], F32) for k in ("pq0", "pq1", "pz", "pr", "pu0", "pu1", "pn", "py")})
+SEMAPHORES = ["sD", "sA", "sP", "sG", "arr0", "arr1", "sent", "l_ob", "l_rec", "l_box", "l_tv", "l_dr", "l_bd", "l_sh",
+              "o_yr", "o_yv", "o_h0", "o_h1", "o_h2"]
+
+MODES = ["ADDDADDD", "DADDADDD", "DADDADDD"]
+HOP, DEAL, ROUNDS, SEED, SHAKE = 100, 3500, 40, 1, 1000
+
+
+def masks_of(src, cores, topo):
+    dsts = [c for c in cores if c != src]
+    far = [c for c in dsts if c not in topo.cores_of(src)]
+    near = [c for c in dsts if c not in far]
+    pool = [e for e in topo.engines(src, far[0]) if all(e in topo.engines(src, c) for c in far)]
+    share = {c: 1 for c in far}
+    spare = len(pool) - len(far)
+    for c in [c for c in far if not topo.same_plane(src, c) and not topo.mates(src, c)] + far:
+        if spare >= 1 and share[c] == 1:
+            share[c] = 2
+            spare -= 1
+    out, used = {}, set(pool)
+    for c in sorted(far, key=lambda c: -share[c]):
+        out[c] = [pool.pop(0) for _ in range(share[c])]
+    for c in near:
+        free = [e for e in topo.engines(src, c) if e not in used]
+        k = 1
+        while 2 * k * len(near) <= len(free):
+            k *= 2
+        out[c] = free[:k]
+        used |= set(out[c])
+    return out
+
+
+def rank_program(g, core, T, topo):
+    rank = T.rank_of(core)
+    if rank is None:
+        return
+    cores = list(T.cores)
+    ops = []
+    psum = {k for k, s in SCRATCH.items() if s[0] == "psum"}
+
+    def S(name, lo=None, hi=None, step=1, p=None):
+        n = SCRATCH[name][1][1]
+        lo = 0 if lo is None else lo
+        hi = n if hi is None else hi
+        rows = slice(None) if p is None else slice(p[0], p[1])
+        ap = T[name][rows, lo:hi:step] if step != 1 else T[name][rows, lo:hi]
+        return (ap, [(name, lo, hi)], len(range(lo, hi, step)), SCRATCH[name][2] in (BF, U16))
+
+    def S3(name, q0, q1, c0, c1):
+        w = SCRATCH[name][1][2]
+        ap = T[name][:, q0, c0:c1] if q1 == q0 + 1 else T[name][:, q0:q1, c0:c1]
+        return (ap, [(name, q * w + c0, q * w + c1) for q in range(q0, q1)], (q1 - q0) * (c1 - c0), SCRATCH[name][2] == BF)
+
+    def H(name, h, w=128):
+        return S(name, w * h, w * h + w)
+
+    def col(name, j):
+        return S(name, j, j + 1)
+
+    def IND(win, off):
+        return (win[0].indirect(off[0]), win[1] + off[1], -16 * off[2], False)
+
+    def val(x):
+        return x[0] if isinstance(x, tuple) else x
+
+    def keys(*xs):
+        return [k for x in xs if isinstance(x, tuple) for k in x[1]]
+
+    def add(eng, fn, rd, wr, cost, sem=None, inc=None, late=0, after=None):
+        ops.append({"e": eng, "fn": fn, "rd": rd, "wr": wr, "sem": sem, "inc": inc, "cost": cost, "late": late, "after": after})
+
+    def ns(out, a, k=1.0):
+        if a[2] < 0:
+            return 55 + 1.3 * out[2]
+        return 30 + max(64, k * out[2] * (0.5 if out[3] and a[3] else 1.0))
+
+    def cp(out, in_):
+        add("D", lambda: g.vector.tensor_copy(out[0], in_[0]), keys(in_), keys(out), ns(out, in_))
+
+    def scat(win, off, in_):
+        add("D", lambda: g.vector.tensor_copy(win[0].indirect(off[0]), in_[0]), keys(in_, off), keys(win), 50 + 3.2 * in_[2])
+
+    def tt(out, a, b, op):
+        k = 1.0 if a[1][0][0] in psum or b[1][0][0] in psum else 2.0
+        add("D", lambda: g.vector.tensor_tensor(out[0], a[0], b[0], op), keys(a, b), keys(out), ns(out, a, k))
+
+    def ts(out, a, s1, op0, s2=None, op1=None):
+        if op1 is None:
+            add("D", lambda: g.vector.tensor_scalar(out[0], a[0], val(s1), None, op0), keys(a, s1), keys(out), ns(out, a))
+        else:
+            add("D", lambda: g.vector.tensor_scalar(out[0], a[0], val(s1), val(s2), op0, op1), keys(a, s1, s2), keys(out), ns(out, a))
+
+    def scan(out, d0, d1, init, op0, op1):
+        add("D", lambda: g.vector.tensor_tensor_scan(out[0], d0[0], d1[0], init, op0, op1), keys(d0, d1), keys(out), 30 + out[2])
+
+    def ms(out, c):
+        add("D", lambda: g.vector.memset(out[0], c), [], keys(out), ns(out, out))
+
+    def act(out, a, func=AF.Copy, bias=0.0, scale=1.0):
+        cost = 95 + 1.3 * out[2] if a[2] < 0 else 60 + max(64, out[2])
+        add("A", lambda: g.scalar.activation(out[0], a[0], func, bias=val(bias), scale=val(scale)), keys(a, bias, scale), keys(out), cost)
+
+    def mm(out, lhsT, rhs, start, stop):
+        add("P", lambda: g.tensor.matmul(out[0], lhsT[0], rhs[0], start, stop), keys(lhsT, rhs), keys(out),
+            0.5 * max(min(64, lhsT[2]), rhs[2]) * (1 if lhsT[3] else 4))
+
+    def iota(out, pattern, base, mult=0):
+        if SCRATCH[out[1][0][0]][2] == I32:
+            add("G", lambda: g.iota(out[0], pattern, base, mult), [], keys(out), 130 + 2 * out[2])
+        else:
+            add("G", lambda: g.iota(out[0], pattern, base, mult, allow_small_or_imprecise_dtypes=True), [], keys(out), 130 + 2 * out[2])
+
+    def pick(out, in_, pattern, base):
+        add("G", lambda: g.affine_select(out[0], in_[0], pattern, OP.is_equal, 0.0, base, 1), keys(in_), keys(out), 170 + 2 * out[2])
+
+    moved = [0]
+
+    def dma(q, out, in_, sem, nbytes):
+        eng = {"S": g.sync, "A": g.scalar, "G": g}[q]
+        moved[0] = moved[0] + nbytes if sem[0] == "l" else nbytes
+        add(q, lambda: eng.dma_start(val(out), val(in_)), keys(in_), keys(out), 60, sem, 16, 1800 + moved[0] / 180)
+
+    dma("S", S("obi"), T.ob[:], "l_ob", 8192)
+    dma("S", S("reci"), T.rec[:], "l_rec", 512 * V)
+    dma("A", S("v0"), T.tv[:], "l_tv", 65536)
+    dma("A", S("shi"), T.shp[:], "l_sh", 32 * V)
+    dma("S", S("boxw", 0, NB), T.box[:], "l_box", 256 * NB)
+    dma("A", S("drb", 0, 3), T.dr[:], "l_dr", 4096)
+    dma("S", S("bdi"), T.bound[:], "l_bd", 512 * S0)
+
+    iota(S("pi", 0, 1), [[0, 1]], 0, 1)
+    iota(S("one"), [[0, 128]], 1)
+    pick(S("idb"), S("one"), [[-1, 128]], 0)
+    iota(S("io", 0, 256), [[1, 256]], 0)
+    iota(S("jm"), [[0, 8], [1, 16]], 0)
+    iota(S("em"), [[1, 32], [0, 16]], 0)
+    iota(S("iw"), [[16, 16]], 0)
+    iota(S("lo"), [[0, 8], [1, SEG]], 15)
+    iota(S("hi", 0, HS), [[-1, 8], [0, SEG]], 7)
+    iota(S("lli"), [[SEG, 8]], SEG - 1)
+    iota(S("bo"), [[1, 8], [0, 16]], 0)
+    iota(S("io", 256, V), [[1, V - 256]], 256)
+    iota(S("hi", HS, 432), [[0, 432 - HS]], 0)
+    iota(S("tb", 0, 1), [[0, 1]], 0)
+    iota(S("dh", 0, 1), [[0, 1]], 0)
+    iota(S("dl", 0, 1), [[0, 1]], 0)
+    iota(S("dh", 1, 513), [[0, 2], [1, 16], [0, 16]], 0)
+    iota(S("dl", 1, 513), [[0, 32], [1, 16]], 0)
+    iota(S("boxw", NB, 2560), [[0, 2560 - NB]], 0)
+    iota(S("k256"), [[0, 256]], 256)
+    iota(S("tb", 513, TBD), [[0, TBD - 513]], 0)
+    pc = [col("pc", j) for j in range(11)]
+    J = S("io", 0, HS)
+    ts(col("pi", 1), col("pi", 0), 15, OP.bitwise_and)
+    ts(col("pi", 2), col("pi", 0), 4, OP.arith_shift_right)
+    ts(col("pi", 3), col("pi", 0), 31, OP.bitwise_and)
+    cp(S("pc", 0, 4), S("pi", 0, 4))
+    ts(S("em"), S("em"), pc[3], OP.is_equal, -1.0, OP.mult)
+    for j, sc in enumerate((16.0, 2.0 ** 20, 1.0)):
+        ts(H("g24", j, 8), S("io", 0, 8), pc[2], OP.is_equal, sc, OP.mult)
+    ts(S("dm"), S("jm"), pc[1], OP.is_equal)
+    ts(S("iw"), S("iw"), pc[1], OP.add)
+    ts(pc[4], pc[2], float(SEG), OP.mult, 1.0, OP.add)
+    tt(pc[4], pc[4], pc[1], OP.add)
+    ts(pc[6], pc[4], -1.0, OP.add)
+    ts(S("hi", 0, HS), S("hi", 0, HS), 65536.0, OP.mult)
+    ts(S("thrs"), S("hi", 1, HS, SEG), 15.5, OP.add)
+    ms(S("hi", 0, HS, SEG), 2.0 ** 22)
+    ms(S("hi", SEG - 1, HS, SEG), 2.0 ** 22)
+    top = 108 * math.log(2.0)
+    for h in range(2):
+        act(col("ww", 16 + h), pc[0], AF.Exp, bias=top - 128 * h * math.log(RHO), scale=-math.log(RHO))
+    act(S("ww", 0, 16), S("iw"), AF.Exp, bias=top, scale=-math.log(RHO))
+    act(S("thw"), S("iw"), AF.Exp, bias=top + math.log(2.5), scale=-math.log(RHO))
+    act(S("thr"), S("io", 0, 256), AF.Exp, bias=top + math.log(2.5), scale=-math.log(RHO))
+    for r in range(16):
+        act(H("dg", r), S("idb"), scale=col("dm", r))
+    ts(S("vq"), J, pc[4], OP.is_equal, -2.0 ** 20, OP.mult)
+    ts(H("tmpc", 0, HS), J, pc[6], OP.is_equal, 2.0 ** -22, OP.mult)
+    ts(S("dmz"), S("vq"), -2.0 ** -42, OP.mult)
+    tt(S("dmz"), S("dmz"), H("tmpc", 0, HS), OP.subtract)
+    ts(S("qm"), S("io", 0, 8), pc[2], OP.is_equal, 2.0 ** 22, OP.mult)
+    ts(S("lef"), S("iw"), -8.5, OP.add, 1.0 / SEG, OP.mult)
+    cp(S("lei"), S("lef"))
+    cp(S("le"), S("lei"))
+    cp(S("lj"), S("io", 0, 8))
+    cp(S("ll"), S("lli"))
+    for j, b in enumerate((2560.0, float(V), float(TBD))):
+        ts(H("kk", j, 16), S("iw"), b, OP.add)
+    ts(S("drc", 0, 3), S("drb", 0, 3), -1.0, OP.mult)
+    ts(S("drc", 4, 7), S("drb", 0, 3), -256.0, OP.add)
+    ts(S("drc", 8, 11), S("drb", 0, 3), -1.0, OP.mult, 256.0, OP.add)
+    cp(S("tb", 1, S0 + 1), S("bdi"))
+    ts(S("bo"), S("bo"), pc[2], OP.is_equal)
+    ts(S("sh1"), S("shi"), 1.0, OP.add)
+    ts(S("dh", 1, 513), S("dh", 1, 513), pc[1], OP.is_equal)
+    ts(S("dl", 1, 513), S("dl", 1, 513), pc[1], OP.is_equal)
+    for h, bank in enumerate(("py", "pz")):
+        for c in range(8):
+            mm(H(bank, c, 56), H("dg", 8 * h + c), S("sh1"), True, True)
+        act(H("sh2", h, 448), S(bank, 0, 448))
+        mm(S(bank, 0, 448), S("bo"), H("sh2", h, 448), True, True)
+        act(H("shb", h, 448), S(bank, 0, 448))
+    act(S("idf"), S("idb"))
+    act(S("nidf"), S("idb"), scale=-1.0)
+    act(S("m2"), S("idb"), scale=-2048.5)
+    act(S("bob"), S("bo"), scale=2.0 ** 99)
+    act(S("bob"), S("bob"), scale=2.0 ** 13)
+    act(S("idbig"), S("idb"), scale=2.0 ** 99)
+    act(S("idbig"), S("idbig"), scale=2.0 ** 13)
+    for t in range(RO):
+        act(H("ib", t), S("idb"), scale=float(NB + TH * t))
+    act(H("dk", 0), S("idb"), scale=pc[0])
+    tt(H("dk", 1), S("io", 128, 256), S("idb"), OP.mult)
+    ts(pc[9], pc[1], 0.0, OP.is_equal, 2.0, OP.mult)
+    ts(pc[8], pc[9], 8.0, OP.mult, -1.0, OP.add)
+    tt(pc[10], pc[0], pc[8], OP.add)
+    ts(pc[5], pc[1], 15.0, OP.is_equal, -16.0, OP.mult)
+    ts(pc[5], pc[5], pc[4], OP.add, 1.0, OP.add)
+    ts(pc[7], pc[4], 15.0, OP.add)
+    ts(S("xu"), J, pc[5], OP.is_equal, -2.0 ** 20, OP.mult)
+    tt(S("hq"), S("xu"), S("vq"), OP.subtract)
+    ts(H("kp", 0, HS), J, pc[4], OP.is_equal, pc[8], OP.mult)
+    ts(H("tmpc", 1, HS), S("vq"), -4096.0, OP.mult)
+    tt(H("kp", 1, HS), H("tmpc", 1, HS), S("xu"), OP.subtract)
+    ts(S("kz"), J, pc[7], OP.is_equal, pc[9], OP.mult)
+    ts(S("rmi"), S("io", 0, 128), pc[10], OP.is_equal)
+    tt(S("rmi"), S("rmi"), S("idf"), OP.subtract)
+
+    def vall(t):
+        return S("v0") if t == 0 else S3("rcv%d" % (t - 1), 0, 8, 0, 32)
+
+    def vblock(t, u):
+        return H("v0", u, 32) if t == 0 else S3("rcv%d" % (t - 1), u, u + 1, 0, 32)
+
+    def OW(t, a=0, b=16):
+        return S("ow", 16 * t + a, 16 * t + b)
+
+    def OWF(t, a=0, b=16):
+        return S("owf", 16 * t + a, 16 * t + b)
+
+    def SK(t, a=0, b=16):
+        return S("sk", 16 * t + a, 16 * t + b)
+
+    def A2(j):
+        return H("a2", j, 16)
+
+    def wrap(bank, o, row, c0):
+        for r in range(16):
+            mm(S(bank, o, o + 16), H("dg", r), S(row, c0 + r, c0 + TH, 16), r == 0, r == 15)
+
+    def pre(t):
+        if t == 0:
+            cp(OW(0), S("obi"))
+            cp(OWF(0), S("obi"))
+        else:
+            r = "rcv%d" % (t - 1)
+            tt(OWF(t), S3(r, 0, 8, 32, 34), S3(r, 0, 8, 34, 36), OP.add)
+            cp(OW(t), OWF(t))
+        for u in range(8):
+            k = 32 * (u % 4)
+            mm(S("pu1", 128 * (u // 4), 128 * (u // 4) + 128, p=(k, k + 32)), vblock(t, u), S("idb"), True, True)
+        act(S("vt"), S("pu1", 0, 256))
+        act(S("boxw", 2560, 2816), vall(t), AF.Identity, bias=col("drc", t))
+
+    def boxlist(t, h):
+        if t == 0:
+            ts(H("ci", h), IND(S("reci"), OW(t, 8 * h, 8 * h + 8)), 4095, OP.bitwise_and)
+        else:
+            cp(H("xi", h), IND(S("rf", 0, V), OW(t, 8 * h, 8 * h + 8)))
+            ts(H("ci", h), H("xi", h), 4095, OP.bitwise_and)
+        cp(H("cu", h), H("ci", h))
+
+    def chunk(t, u):
+        src = IND(S("boxw", 0, NB + TH * t), H("cu", u, 32))
+        dst = H("bg", u, 512)
+        if MODES[t][u] == "D":
+            cp(dst, src)
+        else:
+            act(dst, src)
+        b, h, k = "pu%d" % (u % 2), u // 4, 32 * (u % 4)
+        mm(S(b), S("idb"), dst, True, False)
+        mm(S(b), S("vt", 128 * h, 128 * h + 128, p=(k, k + 32)), S("em", p=(k, k + 32)), False, True)
+        act(H("da", u, 512), S(b), AF.Abs)
+
+    def red(h, last):
+        for a in range(16):
+            mm(S("pq%d" % h, 1 + a, 432, SEG), S("da", 2048 * h + a, 2048 * h + 2048, 16), S("g24"), False, last and a == 15)
+
+    def shapes(t):
+        W = S("pr", 304, 320)
+        act(H("sr", t, TH), IND(S("shb", 0, V), OW(t)), AF.Abs if t < 2 else AF.Copy)
+        wrap("pr", 304, "sr", TH * t)
+        if t < 2:
+            cp(S("sl"), W)
+            act(SK(t), W)
+        else:
+            act(SK(t), W, AF.Abs)
+            ts(A2(6), W, 0.0, OP.is_lt, 256.0, OP.mult)
+            tt(A2(6), A2(6), SK(t), OP.add)
+            cp(S("sl"), A2(6))
+        act(S("hv"), IND(S("tb", 0, 257 if t < 2 else 513), S("sl")))
+        if t:
+            act(S("hr"), S("hv"), AF.Relu, bias=-4096.0)
+            act(S("rot"), S("hr"), AF.Sign)
+        if t == 2:
+            act(S("na"), IND(S("tb", 512, 1025), S("sl")), AF.Sign)
+
+    def keys_init(t):
+        for h in range(2):
+            q = "pq%d" % h
+            mm(S(q, 0, 432), S("idb"), S("hi"), True, False)
+            mm(S(q, 0, HS), S("idb"), S("lo"), False, False)
+        for h in range(2):
+            o = H("pr", h, HS)
+            mm(o, S("idb"), S("hi", 0, HS), h == 0, False)
+            mm(o, S("idb"), S("lo"), False, t == 0 and h == 1)
+            if t:
+                mm(o, H("rot", h), H("kp", 0, HS), False, h == 1)
+        act(S3("ps", 0, 16, 0, SEG), S("pr", 0, 2 * HS), AF.Identity, bias=-16.0)
+        act(S("p16"), S3("ps", 0, 16, 1, 17))
+        for h in range(2):
+            mm(H("pz", h, HS), H("xf", h), S("dmz"), h == 0, t == 0 and h == 1)
+            if t == 1:
+                mm(H("pz", h, HS), H("rot", h), S("kz"), False, h == 1)
+            if t == 2:
+                mm(H("pz", h, HS), H("na", h), S("kz"), False, h == 1)
+
+    def bounds(t, h, last):
+        q = "pq%d" % h
+        if t:
+            mm(H(q, 1, HS), H("hr", h), S("hq"), False, False)
+            mm(S(q, 0, 2 * HS), H("rot", h), S("kp"), False, False)
+        mm(H(q, 1, HS), H("hv", h), S("vq"), False, last)
+
+    def objects(t):
+        cp(S("oru"), IND(S("io"), OW(t)))
+        for q in range(16):
+            e = S("eq", 272 * q, 256 * q + 256)
+            ts(e, S("oru", 16 * q, TH), OWF(t, q, q + 1), OP.is_equal, col("ww", q), OP.mult)
+            mm(S("pn", 16 * q, 256), S("bo"), e, q == 0, q == 15)
+        act(S("cb"), S("pn", 0, 256))
+        wrap("pn", 0, "cb", 0)
+        tt(A2(1), S("pn", 0, 16), S("thw"), OP.is_ge)
+        tt(A2(1), A2(1), H("kk", 1, 16), OP.mult)
+        tt(A2(1), A2(1), OWF(t), OP.max)
+        cp(S("oo"), A2(1))
+
+    def choose(h):
+        q, o = "pq%d" % h, HS * h
+        M, E = H("mm", h, HS), H("me", h, 8)
+        tt(H("tt", h, HS), H(q, 1, HS), S3("ps", 8 * h, 8 * h + 8, 0, SEG), OP.max)
+        scan(M, H("tt", h, HS), H(q, 0, HS), 2.0 ** 23, OP.min, OP.min)
+        cp(E, S("mm", o + SEG - 1, o + HS, SEG))
+        tt(S("pz", o + SEG - 1, o + HS, SEG), E, S("thrs"), OP.is_ge)
+        act(S3("e3", 8 * h, 8 * h + 8, 0, SEG), H(q, 2, HS))
+        act(H("es", h), S3("e3", 8 * h, 8 * h + 8, 1, 17))
+        tt(H("ff", h, HS), IND(E, S("le", 0, 9)), M, OP.is_equal)
+        scan(H("s2", h, HS), H("pz", h, HS), H("ff", h, HS), 0.0, OP.add, OP.mult)
+        tt(H("lq", h), IND(H("s2", h, HS), S("ll")), S("dm"), OP.mult)
+        mm(S("pr", 288 + 8 * h, 296 + 8 * h), H("lq", h), S("qm"), True, True)
+        tt(H("oh", h), IND(E, S("lj")), H("p16", h), OP.is_equal)
+
+    def newv(t):
+        cp(S("wi"), S("pr", 288, 304))
+        ts(H("a1", 0, 16), S("wi"), 4095 | (1 << 22), OP.bitwise_and)
+        tt(A2(0), H("a1", 0, 16), H("kk", 0, 16), OP.min)
+        cp(S("ox"), A2(0))
+        X = IND(S("boxw"), S("ox"))
+        act(S("yy"), X, AF.Identity, bias=col("drc", 4 + t))
+        ts(S("ym"), X, col("drc", 8 + t), OP.is_lt, 256.0, OP.mult)
+        if t < 2:
+            s = "snd%d" % t
+            ts(H("a1", 1, 16), S("wi"), 12, OP.arith_shift_right, 1023, OP.bitwise_and)
+            cp(S3(s, 0, 8, 32, 34), H("a1", 1, 16))
+            tt(S3(s, 0, 8, 34, 36), H("a1", 1, 16), S3(s, 0, 8, 32, 34), OP.subtract)
+            tt(S3(s, 0, 8, 0, 32), S("yy"), S("ym"), OP.add)
+        else:
+            tt(S("vout"), S("yy"), S("ym"), OP.add)
+            dma("S", T.yv[:], S("vout"), "o_yv", 65536)
+
+    def send(t):
+        s, r = "snd%d" % t, "rcv%d" % t
+        mk = masks_of(core, cores, topo)
+        trs = []
+        for q, d in enumerate(cores):
+            if d != core:
+                rid, pid = topo.addr(d, core)
+                trs.append(RemoteDMATransfer(dst_ids=[DstId(rid=rid, pnc=pid)], dma_engine_mask=sum(1 << e for e in mk[d]),
+                                             remote_sem=T.sem["arr%d" % t], src=T[s][:, q, 0:SENT], dst=T[r][:, rank, 0:SENT]))
+        add("G", lambda: g.remote_dma_fused(trs, local_sem=T.sem.sent), keys(S3(s, 0, 8, 0, SENT)), [], 1000, "sent",
+            -sum(len(m) for m in mk.values()))
+        n = sum(len(masks_of(c, cores, topo)[core]) for c in cores if c != core)
+        add("X", None, [], [(r, q * SLOT, q * SLOT + SLOT) for q in range(N) if q != rank], 0, "arr%d" % t, -n, DEAL, len(ops) - 1)
+        act(S3(r, rank, rank + 1, 0, SENT), S3(s, rank, rank + 1, 0, SENT))
+
+    def record(t, parts, bank):
+        for a, b in parts:
+            for c in range(a // 128, b // 128):
+                mm(H("pu0", c), H("oh", c), S("idb"), True, True)
+            tt(S("mc", a, b), S("pu0", a, b), S("ci", a, b), OP.mult)
+            act(S("ohs", a, b), S("pu0", a, b))
+            for k in (bank, "py") if t else ("py",):
+                mm(S(k, a, b), S("idf"), S("xf", a, b), True, False)
+                for c in range(a // 128, b // 128):
+                    mm(H(k, c), H("oh", c), H("dk", c), False, False)
+                    mm(H(k, 2 + c), H("es", c), S("idf"), False, False)
+                mm(S(k, a, b), H("ib", t), S("ohs", a, b), False, False)
+                mm(S(k, a, b), S("nidf"), S("mc", a, b), False, k == bank or not t)
+            if t:
+                tt(S("yr2", a, b), S(bank, a, b), S("rot", a, b), OP.mult)
+                tt(S("yr2", 256 + a, 256 + b), S(bank, 256 + a, 256 + b), S("rot", a, b), OP.mult)
+                mm(S("py", a, b), S("rmi"), S("yr2", a, b), False, False)
+                mm(S("py", 256 + a, 256 + b), S("rmi"), S("yr2", 256 + a, 256 + b), False, True)
+            act(S("ysb", a, b), S("py", a, b))
+        scat(S("rf"), S("oo"), S("ysb"))
+        if t == 2:
+            dma("S", T.yr[:], S("rf", 0, V), "o_yr", 512 * V)
+        else:
+            act(S("esb"), S("py", 256, 512), AF.Identity, bias=4097.0)
+
+    def newbox(t):
+        mm(S("pu1", 0, 256), S("idb"), S("k256"), True, False)
+        mm(S("pu1", 0, 256), S("idb"), S("boxw", 2560, 2816), False, False)
+        mm(S("pu1", 0, 256), S("idb"), S("yy"), False, True)
+        act(S("nbf"), S("pu1", 0, 256), AF.Identity, bias=MAGIC, scale=0.4999)
+        act(H("boxw", 7 + t, TH), S("nbf"), AF.Identity, bias=-MAGIC)
+
+    def digits(t):
+        act(S("ha"), IND(S("dh", 0, 513), S("sl")))
+        act(S("hb"), IND(S("dl", 0, 513), S("sl")))
+        for j, k in enumerate(("ha", "hb")):
+            for h in range(2):
+                mm(H("py", 2 * j + h), H(k, h), S("idb"), True, True)
+        act(S("ht"), S("py"))
+        if t == 2:
+            for h in range(2):
+                mm(H("pr", 40 + h, 8), H("na", h), H("g24", 2, 8), True, True)
+                ts(H("a2", 4 + h, 8), H("pr", 40 + h, 8), 0.0, OP.is_equal, col("ww", 16 + h), OP.mult)
+
+    def askers(t, h):
+        flag = S("pz", HS * h + SEG - 1, HS * h + HS, SEG)
+        if t < 2:
+            ts(H("wa", h, 8), flag, col("ww", 16 + h), OP.mult)
+        else:
+            tt(H("wa", h, 8), flag, H("a2", 4 + h, 8), OP.mult)
+        tt(H("hw", h), IND(H("wa", h, 8), S("lj")), H("ht", 2 + h), OP.mult)
+
+    def makers(t):
+        for h in range(2):
+            mm(H("pn", 2), H("ht", h), H("hw", h), h == 0, h == 1)
+        tt(S("hm"), H("pn", 2), S("bo"), OP.mult)
+        mm(S("pn", 256, 512), S("hm"), S("ha"), True, True)
+        tt(S("hu"), S("pn", 256, 512), S("hb"), OP.mult)
+        mm(S("pn", 256, 512), S("bo"), S("hu"), True, False)
+        if t == 2:
+            mm(S("pn", 256, 512), S("idbig"), S("na"), False, False)
+        mm(S("pn", 256, 512), S("bob"), S("ohs"), False, True)
+        tt(S("fl"), S("pn", 256, 512), S("thr"), OP.is_lt)
+        tt(H("yhs", t, TH), S("py", 256, 512), S("fl"), OP.mult)
+        dma("S", T.yh[:, TH * t:TH * t + TH], H("yhs", t, TH), "o_h%d" % t, 512 * TH)
+        if t == 2:
+            return
+        wrap("pn", 256, "fl", 0)
+        ts(A2(3), S("pn", 256, 272), 0.5, OP.is_lt, 4096.0, OP.mult)
+        tt(A2(3), A2(3), SK(t), OP.add)
+        tt(A2(5), A2(3), H("kk", 2, 16), OP.min)
+        cp(S("osa"), A2(5))
+        if t == 0:
+            scat(S("tb", 0, TBD + TH), S("osa"), S("esb"))
+            act(S("sm"), S("tb", 1, 257), AF.Sign, bias=-4090.0)
+            mm(S("pz", 0, 256), S("idf"), S("tb", 1, 257), True, False)
+            mm(S("pz", 0, 256), S("m2"), S("sm"), False, True)
+            act(S("tb", 257, 513), S("pz", 0, 256), AF.Identity, bias=-2048.5)
+        else:
+            ts(H("a1", 3, 16), S("wi"), 23, OP.arith_shift_right)
+            ts(A2(4), H("a1", 3, 16), 512.0, OP.mult)
+            tt(A2(3), A2(3), A2(4), OP.add)
+            tt(A2(3), A2(3), H("kk", 2, 16), OP.min)
+            cp(S("osb"), A2(3))
+            scat(S("tb", 256, TBD + 2 * TH), S("osa"), S("esb"))
+            scat(S("tb", 0, TBD + TH), S("osb"), S("esb"))
+
+    for t in range(RO):
+        pre(t)
+        boxlist(t, 0)
+        boxlist(t, 1)
+        if t == 0:
+            cp(S("xf"), IND(S("reci"), OW(0)))
+            cp(S("rf", 0, V), S("reci"))
+        else:
+            act(S("xf"), IND(S("rf", 0, V), OW(t)))
+        shapes(t)
+        keys_init(t)
+        digits(t)
+        objects(t)
+        for u in range(4):
+            chunk(t, u)
+        red(0, False)
+        bounds(t, 0, True)
+        bounds(t, 1, False)
+        for u in range(4, 8):
+            chunk(t, u)
+        choose(0)
+        askers(t, 0)
+        red(1, True)
+        choose(1)
+        askers(t, 1)
+        if t < 2:
+            newv(t)
+            send(t)
+            newbox(t)
+            record(t, [(0, 256)], "pq0")
+            if t == 1:
+                act(S("vis"), H("sr", 1, TH), scale=-1.0)
+                scat(S("shb"), S("oo"), S("vis"))
+        else:
+            record(t, [(0, 128), (128, 256)], "pq0")
+            newv(t)
+        makers(t)
+
+    emit(g, T, order(ops, psum))
+
+
+def schedule(ops):
+    n = len(ops)
+    lag = [{j: (HOP + ops[j]["late"] if j in o["deps"] else 0) for j in o["pred"]} for o in ops]
+    back = [{} for _ in ops]
+    for i in range(n):
+        for j, x in lag[i].items():
+            back[j][i] = x
+
+    def place(before, after, rank, tail):
+        left = [len(b) for b in before]
+        ready = list(tail)
+        pool = [i for i in range(n) if not left[i]]
+        busy, end = {}, [0.0] * n
+        while pool:
+            i = min(pool, key=lambda k: (rank[k], k))
+            pool.remove(i)
+            row = busy.setdefault(ops[i]["e"], [])
+            s, c, at = ready[i], ops[i]["cost"], 0
+            for a, b in row:
+                if a >= s + c:
+                    break
+                s = max(s, b)
+                at += 1
+            row.insert(at, (s, s + c))
+            end[i] = s + c
+            for k, x in after[i].items():
+                ready[k] = max(ready[k], end[i] + x)
+                left[k] -= 1
+                if not left[k]:
+                    pool.append(k)
+        return end
+
+    late = [o["late"] for o in ops]
+    end = [float(i) for i in range(n)]
+    seed = SEED
+    best = None
+    for _ in range(ROUNDS):
+        shake = []
+        for x in end:
+            seed = (seed * 1103515245 + 12345) % 2147483648
+            shake.append(-x - SHAKE * seed / 2147483648)
+        rev = place(back, lag, shake, late)
+        end = place(lag, back, [-x for x in rev], [0.0] * n)
+        span = max(e + x for e, x in zip(end, late))
+        if best is None or span < best[0]:
+            best = (span, sorted(range(n), key=lambda i: (end[i] - ops[i]["cost"], end[i], i)), end)
+        end = best[2]
+    return best[1]
+
+
+def order(ops, psum):
+    seen = {}
+    for i, o in enumerate(ops):
+        deps, soft = set(), set()
+        for mode, ks in (("r", o["rd"]), ("w", o["wr"])):
+            for name, lo, hi in ks:
+                hist = seen.setdefault(name, [])
+                for j, m, l2, h2 in hist:
+                    if j == i:
+                        continue
+                    clash = (mode == "w" or m == "w") and l2 < hi and lo < h2
+                    if name in psum and ops[j]["e"] == o["e"] == "P":
+                        soft.add(j)
+                    elif clash or (name in psum and ops[j]["e"] != o["e"]):
+                        deps.add(j)
+                if mode == "w":
+                    hist[:] = [x for x in hist if not (lo <= x[2] and x[3] <= hi) or name in psum and x[0] > i - 400]
+                hist.append((i, mode, lo, hi))
+        if o["after"] is not None:
+            soft.add(o["after"])
+        if o["e"] in "SG" or o["sem"]:
+            soft |= {j for j in range(i) if ops[j]["e"] == o["e"] and (ops[j]["sem"] or o["e"] == "G")}
+        o["deps"], o["pred"] = deps, deps | soft
+    out = schedule(ops)
+    place = {i: k for k, i in enumerate(out)}
+    for o in ops:
+        o["deps"] = {place[j] for j in o["deps"]}
+    return [ops[i] for i in out]
+
+
+def emit(g, T, ops):
+    queue = {"D": g.vector, "A": g.scalar, "P": g.tensor, "G": g, "S": g.sync}
+    total = {}
+    for o in ops:
+        if o["sem"]:
+            total[o["sem"]] = total.get(o["sem"], 0) + abs(o["inc"])
+    known = {e: {} for e in queue}
+    for o in ops:
+        o["waits"] = []
+        if o["e"] == "X":
+            continue
+        need = {}
+        for j in o["deps"]:
+            k = ops[j]["sem"] or ops[j]["e"]
+            need[k] = max(need.get(k, -1), j)
+        kn = known[o["e"]]
+        for k, j in sorted(need.items(), key=lambda x: -x[1]):
+            if kn.get(k, -1) < j:
+                o["waits"].append(j)
+                ops[j]["mark"] = True
+                for k2, j2 in ops[j].get("clock", {}).items():
+                    kn[k2] = max(kn.get(k2, -1), j2)
+                kn[k] = len(ops) if ops[j]["sem"] else j
+        o["clock"] = dict(kn)
+    count = {e: 0 for e in queue}
+    waited = set()
+    for o in ops:
+        if o["e"] == "X":
+            continue
+        q = queue[o["e"]]
+        for j in o["waits"]:
+            d = ops[j]
+            if d["sem"]:
+                q.wait_ge(T.sem[d["sem"]], total[d["sem"]])
+                waited.add(d["sem"])
+            else:
+                q.wait_ge(T.sem["s" + d["e"]], d["n"])
+        ins = o["fn"]()
+        if o["sem"]:
+            if o["inc"] > 0:
+                ins.then_inc(T.sem[o["sem"]], o["inc"])
+        elif o.get("mark"):
+            count[o["e"]] += 1
+            o["n"] = count[o["e"]]
+            ins.then_inc(T.sem["s" + o["e"]], 1)
+    for s, n in total.items():
+        if s not in waited:
+            g.wait_ge(T.sem[s], n)

@@ -7,53 +7,44 @@ F32, BF, I32, U16 = "float32", "bfloat16", "int32", "uint16"
 SLOT, SENT = 40, 36
 SEG = 18
 HS = 8 * SEG
+OFF = 34 * 4096
 RHO = 1.8
 MAGIC = 12582912.0
-TBD = 1032
+TBD = 776
 WIDTHS = {
-    I32: dict(obi=16, reci=V, shi=56, bdi=S0, pi=8, lei=16, lli=8, xi=TH, ci=TH, wi=16, a1=64),
-    U16: dict(le=16, ll=8, lj=8, ow=48, cu=TH, oru=TH, sl=16, ox=16, oo=16, osa=16, osb=16),
-    BF: dict(sh1=56, sh2=V, shb=V + TH, boxw=2816, v0=TH, drb=8, dg=2048, k256=256, one=128, em=512, idb=128, bo=128, bob=128,
-             idbig=128, ib=384, dk=256, g24=24, hi=432, lo=HS, kp=2 * HS, kz=HS, vt=256, bg=4096, da=4096, eq=4096,
-             dh=520, dl=520, ha=TH, hb=TH, ht=512, hw=TH, hm=128, hu=TH,
-             sg=TH, cb=TH, sr=3 * TH, rot=TH, na=TH, oh=256, ff=2 * HS, yy=TH, ym=TH, vout=TH, ohs=TH, fl=TH, vis=TH),
-    F32: dict(rf=V + TH, tb=1544, drc=16, io=V, pc=16, jm=128, dm=128, idf=128, nidf=128, m2=128, rmi=128, qm=8, thrs=8, vq=HS,
-              xu=HS, hq=HS, dmz=HS, tmpc=2 * HS, iw=16, kk=48, ww=18, thr=256, thw=16, lef=16, owf=48, xf=TH, sm=TH,
-              sk=48, hv=TH, hr=TH, es=256, p16=256, me=16, tt=2 * HS, mm=2 * HS, s2=2 * HS, lq=256, a2=128, mc=TH, yr2=512,
-              ysb=TH, esb=TH, nbf=TH, wa=16, yhs=3 * TH),
+    I32: dict(obi=16, reci=V, shi=V, bdi=S0, pi=8, lei=16, lli=8, xi=TH, ci=TH, owi=48),
+    U16: dict(le=16, ll=8, ow=48, cu=TH, oru=TH, sl=16, ox=16, oo=16, osa=16),
+    BF: dict(sh1=V, shb=V + TH, boxw=NB + 2 * TH, v0=TH, drb=8, dg=144, one=128, em=512, idb=128, nidb=128, bo=128, e8=128,
+             bo8k=128, idbig=128, ib=384, dk=256, dw=256, in23=128, ip24=128, i64=128, i05=128, mh=128, g24=32, hi=432,
+             lo=HS, thb=128, dm=128, fc=160, fd=160, kpa=2 * HS, kpb=2 * HS, vt=256, bd=8192, eq=4096, dh=520, dl=520,
+             ha=TH, hn=TH, hta=TH, hw=TH, hm=128, flu=TH, thrn=TH, cb=TH, sr=3 * TH, rot=TH, rn=TH, na=TH, oh=256,
+             ff=2 * HS, yy=TH, ys=TH, vout=TH),
+    F32: dict(rf=V + TH, tb=TBD + TH, drc=16, io=V, pc=16, idf=128, rm=128, qm=8, vqx=160, hq=HS, e1=160, dmz=HS, fk=HS,
+              p16=256, dmx=128, iw=16, kk=32, ww=24, thr=256, lef=16, me=16, owf=48, xf=TH, sk=48, hv=TH, hr=TH, es=256,
+              t2=256, tt=2 * HS, mm=2 * HS, s2=2 * HS, lq=512, a2=128, mc=TH, ya=TH, ysb=TH, ea=TH, esel=TH, yhs=3 * TH),
 }
 SCRATCH = {k: ("sbuf", [128, n], d) for d, w in WIDTHS.items() for k, n in w.items()}
-SCRATCH.update({k: ("sbuf", [128, 16, SEG], F32) for k in ("ps", "e3")})
 SCRATCH.update({k: ("sbuf", [128, 8, SLOT], BF) for k in ("snd0", "snd1", "rcv0", "rcv1")})
+SCRATCH["e3"] = ("sbuf", [128, 16, SEG], F32)
 SCRATCH.update({k: ("psum", [128, 512], F32) for k in ("pq0", "pq1", "pz", "pr", "pu0", "pu1", "pn", "py")})
-SEMAPHORES = ["sD", "sA", "sP", "sG", "arr0", "arr1", "sent", "l_ob", "l_rec", "l_box", "l_tv", "l_dr", "l_bd", "l_sh",
-              "o_yr", "o_yv", "o_h0", "o_h1", "o_h2"]
+SEMAPHORES = ["sD", "sA", "sP", "sG", "arr00", "arr01", "arr10", "arr11", "sent", "l_ob", "l_rec", "l_box", "l_tv", "l_dr",
+              "l_bd", "l_sh", "o_yr", "o_yv", "o_h0", "o_h1", "o_h2"]
 
-MODES = ["ADDDADDD", "DADDADDD", "DADDADDD"]
-HOP, DEAL, ROUNDS, SEED, SHAKE = 100, 3500, 40, 1, 1000
+MODES = ["DADADADD", "DADADADD", "DADADADD"]
+HOP, DEAL, ROUNDS, SEED, SHAKE = 190, 2600, 30, 1, 1000
+CY, GAT, SCA, PE = 0.83, 1.5, 3.5, 0.37
+FIRST = 2500
+ORDERS = {}
 
 
-def masks_of(src, cores, topo):
-    dsts = [c for c in cores if c != src]
+def masks_of(src, dsts, topo):
     far = [c for c in dsts if c not in topo.cores_of(src)]
-    near = [c for c in dsts if c not in far]
     pool = [e for e in topo.engines(src, far[0]) if all(e in topo.engines(src, c) for c in far)]
-    share = {c: 1 for c in far}
-    spare = len(pool) - len(far)
-    for c in [c for c in far if not topo.same_plane(src, c) and not topo.mates(src, c)] + far:
-        if spare >= 1 and share[c] == 1:
-            share[c] = 2
-            spare -= 1
-    out, used = {}, set(pool)
-    for c in sorted(far, key=lambda c: -share[c]):
-        out[c] = [pool.pop(0) for _ in range(share[c])]
-    for c in near:
-        free = [e for e in topo.engines(src, c) if e not in used]
-        k = 1
-        while 2 * k * len(near) <= len(free):
-            k *= 2
-        out[c] = free[:k]
-        used |= set(out[c])
+    k = len(pool) // len(far)
+    out = {c: pool[k * j:k * j + k] for j, c in enumerate(far)}
+    for c in dsts:
+        if c not in far:
+            out[c] = [e for e in topo.engines(src, c) if e not in pool][:k]
     return out
 
 
@@ -64,6 +55,8 @@ def rank_program(g, core, T, topo):
     cores = list(T.cores)
     ops = []
     psum = {k for k, s in SCRATCH.items() if s[0] == "psum"}
+    own = rank // 4
+    halves = (1 - own, own)
 
     def S(name, lo=None, hi=None, step=1, p=None):
         n = SCRATCH[name][1][1]
@@ -73,7 +66,7 @@ def rank_program(g, core, T, topo):
         ap = T[name][rows, lo:hi:step] if step != 1 else T[name][rows, lo:hi]
         return (ap, [(name, lo, hi)], len(range(lo, hi, step)), SCRATCH[name][2] in (BF, U16))
 
-    def S3(name, q0, q1, c0, c1):
+    def S3(name, q0, q1, c0=0, c1=SEG):
         w = SCRATCH[name][1][2]
         ap = T[name][:, q0, c0:c1] if q1 == q0 + 1 else T[name][:, q0:q1, c0:c1]
         return (ap, [(name, q * w + c0, q * w + c1) for q in range(q0, q1)], (q1 - q0) * (c1 - c0), SCRATCH[name][2] == BF)
@@ -85,7 +78,7 @@ def rank_program(g, core, T, topo):
         return S(name, j, j + 1)
 
     def IND(win, off):
-        return (win[0].indirect(off[0]), win[1] + off[1], -16 * off[2], False)
+        return (win[0].indirect(off[0]), win[1] + off[1], -16 * off[2], False, win, off)
 
     def val(x):
         return x[0] if isinstance(x, tuple) else x
@@ -96,457 +89,443 @@ def rank_program(g, core, T, topo):
     def add(eng, fn, rd, wr, cost, sem=None, inc=None, late=0, after=None):
         ops.append({"e": eng, "fn": fn, "rd": rd, "wr": wr, "sem": sem, "inc": inc, "cost": cost, "late": late, "after": after})
 
-    def ns(out, a, k=1.0):
+    def vec(fn, out, ins, k=1.0):
+        if out[2] < 0:
+            return add("D", fn, keys(*ins) + out[5][1], out[4][1], 50 - CY * SCA * out[2])
+        a = ins[0] if ins else out
         if a[2] < 0:
-            return 55 + 1.3 * out[2]
-        return 30 + max(64, k * out[2] * (0.5 if out[3] and a[3] else 1.0))
+            return add("D", fn, keys(*ins), keys(out), 50 + CY * GAT * out[2])
+        half = out[3] and all(x[3] for x in ins if isinstance(x, tuple) and x[2] > 1)
+        add("D", fn, keys(*ins), keys(out), 35 + CY * max(64, k * out[2] * (0.5 if half else 1.0)))
 
     def cp(out, in_):
-        add("D", lambda: g.vector.tensor_copy(out[0], in_[0]), keys(in_), keys(out), ns(out, in_))
-
-    def scat(win, off, in_):
-        add("D", lambda: g.vector.tensor_copy(win[0].indirect(off[0]), in_[0]), keys(in_, off), keys(win), 50 + 3.2 * in_[2])
+        vec(lambda: g.vector.tensor_copy(out[0], in_[0]), out, [in_])
 
     def tt(out, a, b, op):
         k = 1.0 if a[1][0][0] in psum or b[1][0][0] in psum else 2.0
-        add("D", lambda: g.vector.tensor_tensor(out[0], a[0], b[0], op), keys(a, b), keys(out), ns(out, a, k))
+        vec(lambda: g.vector.tensor_tensor(out[0], a[0], b[0], op), out, [a, b], k)
 
     def ts(out, a, s1, op0, s2=None, op1=None):
         if op1 is None:
-            add("D", lambda: g.vector.tensor_scalar(out[0], a[0], val(s1), None, op0), keys(a, s1), keys(out), ns(out, a))
+            vec(lambda: g.vector.tensor_scalar(out[0], a[0], val(s1), None, op0), out, [a, s1])
         else:
-            add("D", lambda: g.vector.tensor_scalar(out[0], a[0], val(s1), val(s2), op0, op1), keys(a, s1, s2), keys(out), ns(out, a))
+            vec(lambda: g.vector.tensor_scalar(out[0], a[0], val(s1), val(s2), op0, op1), out, [a, s1, s2])
 
     def scan(out, d0, d1, init, op0, op1):
-        add("D", lambda: g.vector.tensor_tensor_scan(out[0], d0[0], d1[0], init, op0, op1), keys(d0, d1), keys(out), 30 + out[2])
+        vec(lambda: g.vector.tensor_tensor_scan(out[0], d0[0], d1[0], init, op0, op1), out, [d0, d1])
 
     def ms(out, c):
-        add("D", lambda: g.vector.memset(out[0], c), [], keys(out), ns(out, out))
+        vec(lambda: g.vector.memset(out[0], c), out, [])
 
     def act(out, a, func=AF.Copy, bias=0.0, scale=1.0):
-        cost = 95 + 1.3 * out[2] if a[2] < 0 else 60 + max(64, out[2])
+        cost = 65 + CY * GAT * out[2] if a[2] < 0 else 60 + CY * max(64, out[2])
+        if func == AF.Exp and not any(o.get("exp") for o in ops):
+            cost += 1300
         add("A", lambda: g.scalar.activation(out[0], a[0], func, bias=val(bias), scale=val(scale)), keys(a, bias, scale), keys(out), cost)
+        ops[-1]["exp"] = func == AF.Exp
 
-    def mm(out, lhsT, rhs, start, stop):
+    def mm(out, lhsT, rhs, start=True, stop=True):
         add("P", lambda: g.tensor.matmul(out[0], lhsT[0], rhs[0], start, stop), keys(lhsT, rhs), keys(out),
-            0.5 * max(min(64, lhsT[2]), rhs[2]) * (1 if lhsT[3] else 4))
+            10 + PE * max(min(64, lhsT[2]), rhs[2]) * (1 if lhsT[3] else 4))
+
+    def group(out, terms):
+        for j, (lhsT, rhs) in enumerate(terms):
+            mm(out, lhsT, rhs, j == 0, j == len(terms) - 1)
 
     def iota(out, pattern, base, mult=0):
         if SCRATCH[out[1][0][0]][2] == I32:
-            add("G", lambda: g.iota(out[0], pattern, base, mult), [], keys(out), 130 + 2 * out[2])
+            add("G", lambda: g.iota(out[0], pattern, base, mult), [], keys(out), 130 + 2 * CY * out[2])
         else:
-            add("G", lambda: g.iota(out[0], pattern, base, mult, allow_small_or_imprecise_dtypes=True), [], keys(out), 130 + 2 * out[2])
+            add("G", lambda: g.iota(out[0], pattern, base, mult, allow_small_or_imprecise_dtypes=True), [], keys(out),
+                130 + 2 * CY * out[2])
 
-    def pick(out, in_, pattern, base):
-        add("G", lambda: g.affine_select(out[0], in_[0], pattern, OP.is_equal, 0.0, base, 1), keys(in_), keys(out), 170 + 2 * out[2])
+    def pick(out, in_, pattern, base, mult=1):
+        add("G", lambda: g.affine_select(out[0], in_[0], pattern, OP.is_equal, 0.0, base, mult), keys(in_), keys(out),
+            170 + 2 * CY * out[2])
 
     moved = [0]
 
     def dma(q, out, in_, sem, nbytes):
         eng = {"S": g.sync, "A": g.scalar, "G": g}[q]
         moved[0] = moved[0] + nbytes if sem[0] == "l" else nbytes
-        add(q, lambda: eng.dma_start(val(out), val(in_)), keys(in_), keys(out), 60, sem, 16, 1800 + moved[0] / 180)
+        add(q, lambda: eng.dma_start(val(out), val(in_)), keys(in_), keys(out), 60, sem, 16, 1800 + moved[0] / 190)
 
     dma("S", S("obi"), T.ob[:], "l_ob", 8192)
+    dma("A", S("shi", p=(0, 8)), T.shp[:], "l_sh", 32 * V)
     dma("S", S("reci"), T.rec[:], "l_rec", 512 * V)
     dma("A", S("v0"), T.tv[:], "l_tv", 65536)
-    dma("A", S("shi"), T.shp[:], "l_sh", 32 * V)
     dma("S", S("boxw", 0, NB), T.box[:], "l_box", 256 * NB)
     dma("A", S("drb", 0, 3), T.dr[:], "l_dr", 4096)
     dma("S", S("bdi"), T.bound[:], "l_bd", 512 * S0)
 
+    pc = [col("pc", j) for j in range(11)]
     iota(S("pi", 0, 1), [[0, 1]], 0, 1)
-    iota(S("one"), [[0, 128]], 1)
+    ms(S("one"), 1.0)
     pick(S("idb"), S("one"), [[-1, 128]], 0)
-    iota(S("io", 0, 256), [[1, 256]], 0)
-    iota(S("jm"), [[0, 8], [1, 16]], 0)
-    iota(S("em"), [[1, 32], [0, 16]], 0)
-    iota(S("iw"), [[16, 16]], 0)
-    iota(S("lo"), [[0, 8], [1, SEG]], 15)
-    iota(S("hi", 0, HS), [[-1, 8], [0, SEG]], 7)
-    iota(S("lli"), [[SEG, 8]], SEG - 1)
     iota(S("bo"), [[1, 8], [0, 16]], 0)
+    iota(S("io", 0, 256), [[1, 256]], 0)
+    iota(S("iw"), [[16, 16]], 0)
+    iota(S("em"), [[1, 32], [0, 16]], 0)
     iota(S("io", 256, V), [[1, V - 256]], 256)
+    iota(S("hi", 0, HS), [[-34, 8], [0, SEG]], 239)
     iota(S("hi", HS, 432), [[0, 432 - HS]], 0)
-    iota(S("tb", 0, 1), [[0, 1]], 0)
-    iota(S("dh", 0, 1), [[0, 1]], 0)
-    iota(S("dl", 0, 1), [[0, 1]], 0)
+    iota(S("lo"), [[0, 8], [1, SEG]], -17)
+    iota(S("fk"), [[0, 8], [1, SEG]], -4097, 16)
+    iota(S("fc", 1, HS + 1), [[16, 8], [1, SEG]], -1)
+    iota(S("fd", 1, HS + 1), [[16, 8], [1, SEG]], -1)
+    iota(S("fc", 0, HS + 1, SEG), [[0, 9]], -5)
+    iota(S("fd", SEG, HS + 1, SEG), [[16, 8]], 0)
+    for k in ("fc", "fd"):
+        iota(S(k, 1, HS + 2, SEG), [[0, 9]], -5)
+    iota(S("thb"), [[-34, 8], [0, 16]], 239)
+    iota(S("p16", 0, 128), [[0, 8], [1, 16]], -4096, 16)
+    iota(S("dm"), [[0, 8], [1, 16]], 0)
+    iota(S("lli"), [[SEG, 8]], SEG - 1)
+    for k in ("tb", "dh", "dl"):
+        iota(S(k, 0, 1), [[0, 1]], 0)
     iota(S("dh", 1, 513), [[0, 2], [1, 16], [0, 16]], 0)
     iota(S("dl", 1, 513), [[0, 32], [1, 16]], 0)
-    iota(S("boxw", NB, 2560), [[0, 2560 - NB]], 0)
-    iota(S("k256"), [[0, 256]], 256)
-    iota(S("tb", 513, TBD), [[0, TBD - 513]], 0)
-    pc = [col("pc", j) for j in range(11)]
-    J = S("io", 0, HS)
+    iota(S("tb", 513, 769), [[0, 256]], 0)
     ts(col("pi", 1), col("pi", 0), 15, OP.bitwise_and)
     ts(col("pi", 2), col("pi", 0), 4, OP.arith_shift_right)
     ts(col("pi", 3), col("pi", 0), 31, OP.bitwise_and)
     cp(S("pc", 0, 4), S("pi", 0, 4))
+    ts(S("e8"), S("bo"), pc[0], OP.is_equal)
+    ts(S("bo"), S("bo"), pc[2], OP.is_equal)
     ts(S("em"), S("em"), pc[3], OP.is_equal, -1.0, OP.mult)
-    for j, sc in enumerate((16.0, 2.0 ** 20, 1.0)):
+    for j, sc in enumerate((32.0, 2.0 ** 21, 1.0, 128.0)):
         ts(H("g24", j, 8), S("io", 0, 8), pc[2], OP.is_equal, sc, OP.mult)
-    ts(S("dm"), S("jm"), pc[1], OP.is_equal)
+    ts(S("qm"), S("io", 0, 8), pc[2], OP.is_equal)
+    ms(S("dg"), 0.0)
+    cp(S("dg", 15, 143, 16), S("qm"))
     ts(S("iw"), S("iw"), pc[1], OP.add)
-    ts(pc[4], pc[2], float(SEG), OP.mult, 1.0, OP.add)
-    tt(pc[4], pc[4], pc[1], OP.add)
-    ts(pc[6], pc[4], -1.0, OP.add)
-    ts(S("hi", 0, HS), S("hi", 0, HS), 65536.0, OP.mult)
-    ts(S("thrs"), S("hi", 1, HS, SEG), 15.5, OP.add)
-    ms(S("hi", 0, HS, SEG), 2.0 ** 22)
-    ms(S("hi", SEG - 1, HS, SEG), 2.0 ** 22)
     top = 108 * math.log(2.0)
     for h in range(2):
         act(col("ww", 16 + h), pc[0], AF.Exp, bias=top - 128 * h * math.log(RHO), scale=-math.log(RHO))
     act(S("ww", 0, 16), S("iw"), AF.Exp, bias=top, scale=-math.log(RHO))
-    act(S("thw"), S("iw"), AF.Exp, bias=top + math.log(2.5), scale=-math.log(RHO))
     act(S("thr"), S("io", 0, 256), AF.Exp, bias=top + math.log(2.5), scale=-math.log(RHO))
-    for r in range(16):
-        act(H("dg", r), S("idb"), scale=col("dm", r))
-    ts(S("vq"), J, pc[4], OP.is_equal, -2.0 ** 20, OP.mult)
-    ts(H("tmpc", 0, HS), J, pc[6], OP.is_equal, 2.0 ** -22, OP.mult)
-    ts(S("dmz"), S("vq"), -2.0 ** -42, OP.mult)
-    tt(S("dmz"), S("dmz"), H("tmpc", 0, HS), OP.subtract)
-    ts(S("qm"), S("io", 0, 8), pc[2], OP.is_equal, 2.0 ** 22, OP.mult)
+    act(S("thrn"), S("thr"), scale=-1.0)
+    act(S("ww", 18, 20), S("ww", 16, 18), scale=-5.0)
+    ts(S("sh1", p=(0, 8)), S("shi", p=(0, 8)), 1.0, OP.add)
+    for h, bank in enumerate(("py", "pz")):
+        mm(S(bank, 0, 448), S("e8", p=(0, 8)), S("sh1", 448 * h, 448 * h + 448, p=(0, 8)))
+        act(H("shb", h, 448), S(bank, 0, 448))
+    act(pc[4], pc[2], AF.Identity, bias=7.0 * OFF, scale=-float(OFF))
+    act(pc[5], pc[0], AF.Identity, bias=-2047.0, scale=16.0)
+    ts(S("hi", 0, HS), S("hi", 0, HS), 4096.0, OP.mult)
+    tt(S("fk"), S("fk"), S("hi", 0, HS), OP.add)
+    ts(S("fk", SEG - 1, HS, SEG), S("fk", SEG - 1, HS, SEG), 2032.0, OP.add)
+    ms(S("fk", 0, HS, SEG), 2.0 ** 22)
+    ms(S("hi", 0, HS, SEG), 2.0 ** 22)
+    ms(S("hi", HS + SEG - 1, 2 * HS, SEG), 2.0 ** 21)
+    ms(S("lo", SEG - 1, HS, SEG), 2.0 ** 22)
+    act(S("thb"), S("thb"), scale=4096.0)
+    tt(H("p16", 0), H("p16", 0), S("thb"), OP.add)
+    act(H("p16", 1), H("p16", 0))
+    ts(S("dm"), S("dm"), pc[1], OP.is_equal)
+    act(S("dmx"), S("thb"), AF.Identity, bias=pc[5])
+    tt(S("dmx"), S("dmx"), S("dm"), OP.mult)
+    ts(S("vqx", 0, HS + 1), S("fc", 0, HS + 1), pc[0], OP.is_equal, -2.0 ** 21, OP.mult)
+    ts(S("e1", 1, HS + 2), S("fd", 1, HS + 2), pc[0], OP.is_equal, 2.0 ** -12, OP.mult)
+    tt(S("dmz"), S("e1", 1, HS + 1), S("e1", 2, HS + 2), OP.subtract)
     ts(S("lef"), S("iw"), -8.5, OP.add, 1.0 / SEG, OP.mult)
     cp(S("lei"), S("lef"))
     cp(S("le"), S("lei"))
-    cp(S("lj"), S("io", 0, 8))
     cp(S("ll"), S("lli"))
-    for j, b in enumerate((2560.0, float(V), float(TBD))):
-        ts(H("kk", j, 16), S("iw"), b, OP.add)
-    ts(S("drc", 0, 3), S("drb", 0, 3), -1.0, OP.mult)
-    ts(S("drc", 4, 7), S("drb", 0, 3), -256.0, OP.add)
-    ts(S("drc", 8, 11), S("drb", 0, 3), -1.0, OP.mult, 256.0, OP.add)
+    act(H("kk", 0, 16), S("iw"), AF.Identity, bias=V / 16.0, scale=1 / 16.0)
+    act(H("kk", 1, 16), S("iw"), AF.Identity, bias=1 - TBD / 4096.0, scale=-1 / 4096.0)
+    act(S("drc", 0, 1), S("drb", 0, 1), scale=-1.0)
+    act(S("drc", 1, 3), S("drb", 1, 3), AF.Identity, bias=128.0, scale=-1.0)
+    act(S("drc", 4, 6), S("drb", 0, 2), AF.Identity, bias=-2.0, scale=1 / 128.0)
+    act(S("drc", 6, 7), S("drb", 2, 3), AF.Identity, bias=-256.0)
+    act(S("drc", 8, 10), S("drb", 0, 2), AF.Identity, bias=-255.5)
+    act(S("drc", 10, 11), S("drb", 2, 3), AF.Identity, bias=256.0, scale=-1.0)
     cp(S("tb", 1, S0 + 1), S("bdi"))
-    ts(S("bo"), S("bo"), pc[2], OP.is_equal)
-    ts(S("sh1"), S("shi"), 1.0, OP.add)
     ts(S("dh", 1, 513), S("dh", 1, 513), pc[1], OP.is_equal)
-    ts(S("dl", 1, 513), S("dl", 1, 513), pc[1], OP.is_equal)
-    for h, bank in enumerate(("py", "pz")):
-        for c in range(8):
-            mm(H(bank, c, 56), H("dg", 8 * h + c), S("sh1"), True, True)
-        act(H("sh2", h, 448), S(bank, 0, 448))
-        mm(S(bank, 0, 448), S("bo"), H("sh2", h, 448), True, True)
-        act(H("shb", h, 448), S(bank, 0, 448))
+    ts(S("dl", 1, 513), S("dl", 1, 513), pc[1], OP.not_equal)
     act(S("idf"), S("idb"))
-    act(S("nidf"), S("idb"), scale=-1.0)
-    act(S("m2"), S("idb"), scale=-2048.5)
-    act(S("bob"), S("bo"), scale=2.0 ** 99)
-    act(S("bob"), S("bob"), scale=2.0 ** 13)
-    act(S("idbig"), S("idb"), scale=2.0 ** 99)
-    act(S("idbig"), S("idbig"), scale=2.0 ** 13)
+    for k, sc in (("nidb", -1.0), ("ip24", 2.0 ** 24), ("i64", 64.0), ("i05", 0.5), ("in23", -2.0 ** 23)):
+        ts(S(k), S("idb"), sc, OP.mult)
+    ts(S("idbig"), S("idb"), 2.0 ** 99, OP.mult, 2.0 ** 13, OP.mult)
+    ts(S("bo8k"), S("bo"), 8192.0, OP.mult)
+    ms(S("mh"), -0.5)
     for t in range(RO):
-        act(H("ib", t), S("idb"), scale=float(NB + TH * t))
-    act(H("dk", 0), S("idb"), scale=pc[0])
-    tt(H("dk", 1), S("io", 128, 256), S("idb"), OP.mult)
-    ts(pc[9], pc[1], 0.0, OP.is_equal, 2.0, OP.mult)
-    ts(pc[8], pc[9], 8.0, OP.mult, -1.0, OP.add)
-    tt(pc[10], pc[0], pc[8], OP.add)
-    ts(pc[5], pc[1], 15.0, OP.is_equal, -16.0, OP.mult)
-    ts(pc[5], pc[5], pc[4], OP.add, 1.0, OP.add)
-    ts(pc[7], pc[4], 15.0, OP.add)
-    ts(S("xu"), J, pc[5], OP.is_equal, -2.0 ** 20, OP.mult)
-    tt(S("hq"), S("xu"), S("vq"), OP.subtract)
-    ts(H("kp", 0, HS), J, pc[4], OP.is_equal, pc[8], OP.mult)
-    ts(H("tmpc", 1, HS), S("vq"), -4096.0, OP.mult)
-    tt(H("kp", 1, HS), H("tmpc", 1, HS), S("xu"), OP.subtract)
-    ts(S("kz"), J, pc[7], OP.is_equal, pc[9], OP.mult)
-    ts(S("rmi"), S("io", 0, 128), pc[10], OP.is_equal)
-    tt(S("rmi"), S("rmi"), S("idf"), OP.subtract)
+        ts(H("ib", t), S("idb"), float(NB + TH * t), OP.mult)
+    ts(H("dk", 0), S("idb"), pc[0], OP.mult)
+    ts(H("dk", 1), S("io", 0, 128), 128.0, OP.add)
+    tt(H("dk", 1), H("dk", 1), S("idb"), OP.mult)
+    for h in range(2):
+        ts(H("dw", h), S("idb"), col("ww", 18 + h), OP.mult)
+    ts(pc[6], pc[1], 0.0, OP.is_equal, 2.0 ** 22, OP.mult)
+    ts(pc[7], pc[6], 2.0 ** 11, OP.mult, 2.0 ** 33, OP.add)
+    ts(pc[8], pc[1], 15.0, OP.is_equal, -2.0 ** 22, OP.mult)
+    ts(pc[9], pc[8], 0.5, OP.mult, 2.0 ** 21, OP.add)
+    ts(pc[10], pc[6], 2.0 ** -18, OP.mult, -1.0, OP.add)
+    tt(pc[10], pc[10], pc[0], OP.add)
+    for j in range(2):
+        ts(H("kpa", j, HS), S("fc", 1, HS + 1), pc[0], OP.is_equal, pc[6 + j], OP.mult)
+        ts(H("kpb", j, HS), S("fc", 0, HS), pc[0], OP.is_equal, pc[8 + j], OP.mult)
+    tt(S("hq"), S("vqx", 0, HS), S("vqx", 1, HS + 1), OP.subtract)
+    ts(S("rm"), S("io", 0, 128), pc[10], OP.is_equal)
 
-    def vall(t):
-        return S("v0") if t == 0 else S3("rcv%d" % (t - 1), 0, 8, 0, 32)
+    def vhalf(t, h):
+        return H("v0", h) if t == 0 else S3("rcv%d" % (t - 1), 4 * h, 4 * h + 4, 0, 32)
 
     def vblock(t, u):
         return H("v0", u, 32) if t == 0 else S3("rcv%d" % (t - 1), u, u + 1, 0, 32)
 
-    def OW(t, a=0, b=16):
-        return S("ow", 16 * t + a, 16 * t + b)
+    def W(name, t, a=0, b=16):
+        return S(name, 16 * t + a, 16 * t + b)
 
-    def OWF(t, a=0, b=16):
-        return S("owf", 16 * t + a, 16 * t + b)
+    def WH(name, t, h):
+        return W(name, t, 8 * h, 8 * h + 8)
 
-    def SK(t, a=0, b=16):
-        return S("sk", 16 * t + a, 16 * t + b)
+    def wrap(out, row, c0, more=()):
+        group(out, [(S("dg", 15 - r, 143 - r), S(row, c0 + r, c0 + TH, 16)) for r in range(16)] + list(more))
 
-    def A2(j):
-        return H("a2", j, 16)
-
-    def wrap(bank, o, row, c0):
-        for r in range(16):
-            mm(S(bank, o, o + 16), H("dg", r), S(row, c0 + r, c0 + TH, 16), r == 0, r == 15)
-
-    def pre(t):
+    def pre(t, h, direct):
         if t == 0:
-            cp(OW(0), S("obi"))
-            cp(OWF(0), S("obi"))
+            cp(WH("ow", 0, h), H("obi", h, 8))
+            ts(H("ci", h), IND(S("reci"), WH("ow", 0, h)), 4095, OP.bitwise_and)
         else:
             r = "rcv%d" % (t - 1)
-            tt(OWF(t), S3(r, 0, 8, 32, 34), S3(r, 0, 8, 34, 36), OP.add)
-            cp(OW(t), OWF(t))
-        for u in range(8):
-            k = 32 * (u % 4)
-            mm(S("pu1", 128 * (u // 4), 128 * (u // 4) + 128, p=(k, k + 32)), vblock(t, u), S("idb"), True, True)
-        act(S("vt"), S("pu1", 0, 256))
-        act(S("boxw", 2560, 2816), vall(t), AF.Identity, bias=col("drc", t))
-
-    def boxlist(t, h):
-        if t == 0:
-            ts(H("ci", h), IND(S("reci"), OW(t, 8 * h, 8 * h + 8)), 4095, OP.bitwise_and)
-        else:
-            cp(H("xi", h), IND(S("rf", 0, V), OW(t, 8 * h, 8 * h + 8)))
+            tt(WH("owi", t, h), S3(r, 4 * h, 4 * h + 4, 32, 34), S3(r, 4 * h, 4 * h + 4, 34, 36), OP.add)
+            cp(WH("ow", t, h), WH("owi", t, h))
+        act(H("xf", h), IND(S("rf", 0, V), WH("ow", t, h)), AF.Identity, bias=-1280.0)
+        if t:
+            if direct:
+                cp(H("xi", h), IND(S("rf", 0, V), WH("ow", t, h)))
+            else:
+                ts(H("xi", h), H("xf", h), 1280.0, OP.add)
             ts(H("ci", h), H("xi", h), 4095, OP.bitwise_and)
         cp(H("cu", h), H("ci", h))
+        for k in range(4):
+            mm(S("pz", 128 * h, 128 * h + 128, p=(32 * k, 32 * k + 32)), vblock(t, 4 * h + k), S("idb"))
+        if t:
+            act(H("vt", h), H("pz", h), AF.Identity, bias=128.0, scale=128.0)
+        else:
+            act(H("vt", h), H("pz", h))
 
-    def chunk(t, u):
-        src = IND(S("boxw", 0, NB + TH * t), H("cu", u, 32))
-        dst = H("bg", u, 512)
-        if MODES[t][u] == "D":
+    def chunk(t, h, k, mode):
+        src = IND(S("boxw", 0, NB + TH * t), H("cu", 4 * h + k, 32))
+        dst = H("bd", 8 * h + k, 512)
+        if mode == "D":
             cp(dst, src)
         else:
             act(dst, src)
-        b, h, k = "pu%d" % (u % 2), u // 4, 32 * (u % 4)
-        mm(S(b), S("idb"), dst, True, False)
-        mm(S(b), S("vt", 128 * h, 128 * h + 128, p=(k, k + 32)), S("em", p=(k, k + 32)), False, True)
-        act(H("da", u, 512), S(b), AF.Abs)
+        rows = (32 * k, 32 * k + 32)
+        group(S("pu%d" % (k % 2)), [(S("idb"), dst), (S("vt", 128 * h, 128 * h + 128, p=rows), S("em", p=rows))])
+        act(H("bd", 8 * h + 4 + k, 512), S("pu%d" % (k % 2)), AF.Abs)
 
-    def red(h, last):
-        for a in range(16):
-            mm(S("pq%d" % h, 1 + a, 432, SEG), S("da", 2048 * h + a, 2048 * h + 2048, 16), S("g24"), False, last and a == 15)
+    def red(t, h):
+        q, o, n = "pq%d" % h, 4096 * h + 2048, 17 if t else 16
+        for u in range(n):
+            mm(S(q, 1 + u, 432, SEG), S("bd", o + u % 16, o + 2048, 16), S("g24", 0, 24), False, u == n - 1)
+        if t:
+            cp(S("bd", o, o + 2048, 16), S("bd", o - 2048, o, 16))
+        act(S("bd", o + 1, o + 2048, 16), vhalf(t, h), AF.Identity, bias=col("drc", t), scale=128.0 if t else 1.0)
 
     def shapes(t):
-        W = S("pr", 304, 320)
-        act(H("sr", t, TH), IND(S("shb", 0, V), OW(t)), AF.Abs if t < 2 else AF.Copy)
-        wrap("pr", 304, "sr", TH * t)
+        P = S("pz", 256, 272)
+        act(H("sr", t, TH), IND(S("shb", 0, V), W("ow", t)))
+        wrap(P, "sr", TH * t)
         if t < 2:
-            cp(S("sl"), W)
-            act(SK(t), W)
+            ts(S("sl"), P, 1 / 16.0, OP.mult)
+            act(W("sk", t), P, scale=-2.0 ** -16)
         else:
-            act(SK(t), W, AF.Abs)
-            ts(A2(6), W, 0.0, OP.is_lt, 256.0, OP.mult)
-            tt(A2(6), A2(6), SK(t), OP.add)
-            cp(S("sl"), A2(6))
+            act(W("sk", t), P, AF.Abs, scale=1 / 16.0)
+            ts(W("a2", 6), P, 0.0, OP.is_lt, 256.0, OP.mult)
+            tt(W("a2", 6), W("a2", 6), W("sk", t), OP.add)
+            cp(S("sl"), W("a2", 6))
         act(S("hv"), IND(S("tb", 0, 257 if t < 2 else 513), S("sl")))
         if t:
             act(S("hr"), S("hv"), AF.Relu, bias=-4096.0)
             act(S("rot"), S("hr"), AF.Sign)
+        if t == 1:
+            act(S("rn"), S("rot"), AF.Identity, bias=1.0, scale=-2.0)
+            wrap(S("pz", 272, 288), "rot", 0)
+            act(W("sk", 2), S("pz", 272, 288), scale=-1 / 256.0)
         if t == 2:
-            act(S("na"), IND(S("tb", 512, 1025), S("sl")), AF.Sign)
+            act(S("na"), IND(S("tb", 256, 769), S("sl")), AF.Sign, bias=-4090.0)
 
-    def keys_init(t):
-        for h in range(2):
-            q = "pq%d" % h
-            mm(S(q, 0, 432), S("idb"), S("hi"), True, False)
-            mm(S(q, 0, HS), S("idb"), S("lo"), False, False)
-        for h in range(2):
-            o = H("pr", h, HS)
-            mm(o, S("idb"), S("hi", 0, HS), h == 0, False)
-            mm(o, S("idb"), S("lo"), False, t == 0 and h == 1)
-            if t:
-                mm(o, H("rot", h), H("kp", 0, HS), False, h == 1)
-        act(S3("ps", 0, 16, 0, SEG), S("pr", 0, 2 * HS), AF.Identity, bias=-16.0)
-        act(S("p16"), S3("ps", 0, 16, 1, 17))
-        for h in range(2):
-            mm(H("pz", h, HS), H("xf", h), S("dmz"), h == 0, t == 0 and h == 1)
-            if t == 1:
-                mm(H("pz", h, HS), H("rot", h), S("kz"), False, h == 1)
-            if t == 2:
-                mm(H("pz", h, HS), H("na", h), S("kz"), False, h == 1)
+    def keys_init(t, h):
+        q = "pq%d" % h
+        mm(S(q, 0, 432), S("idb"), S("hi"), True, False)
+        mm(H(q, 0, HS), S("idb"), S("lo"), False, False)
+        if t < 2:
+            mm(H("pr", h, HS), H("xf", h), S("dmz"))
 
-    def bounds(t, h, last):
+    def bounds(t, h):
         q = "pq%d" % h
         if t:
             mm(H(q, 1, HS), H("hr", h), S("hq"), False, False)
-            mm(S(q, 0, 2 * HS), H("rot", h), S("kp"), False, False)
-        mm(H(q, 1, HS), H("hv", h), S("vq"), False, last)
+            mm(S(q, 0, 2 * HS), H("rot", h), S("kpa"), False, False)
+            mm(S(q, 0, 2 * HS), H("rot", h), S("kpb"), False, False)
+            P = H("pr", 40 + h, 8)
+            mm(P, H("rot", h), H("g24", 3, 8))
+            tt(S("p16", 128 * h, 128 * h + 128, 16), P, S("fk", 1, HS, SEG), OP.add)
+        mm(H(q, 1, HS), H("hv", h), S("vqx", 1, HS + 1), False, False)
 
     def objects(t):
-        cp(S("oru"), IND(S("io"), OW(t)))
+        cp(W("owf", t), S("obi") if t == 0 else W("owi", t))
+        cp(S("oru"), IND(S("io"), W("ow", t)))
+        mm(S("pn", 0, 256), S("idb"), S("thrn"), True, False)
         for q in range(16):
             e = S("eq", 272 * q, 256 * q + 256)
-            ts(e, S("oru", 16 * q, TH), OWF(t, q, q + 1), OP.is_equal, col("ww", q), OP.mult)
-            mm(S("pn", 16 * q, 256), S("bo"), e, q == 0, q == 15)
-        act(S("cb"), S("pn", 0, 256))
-        wrap("pn", 0, "cb", 0)
-        tt(A2(1), S("pn", 0, 16), S("thw"), OP.is_ge)
-        tt(A2(1), A2(1), H("kk", 1, 16), OP.mult)
-        tt(A2(1), A2(1), OWF(t), OP.max)
-        cp(S("oo"), A2(1))
-
-    def choose(h):
-        q, o = "pq%d" % h, HS * h
-        M, E = H("mm", h, HS), H("me", h, 8)
-        tt(H("tt", h, HS), H(q, 1, HS), S3("ps", 8 * h, 8 * h + 8, 0, SEG), OP.max)
-        scan(M, H("tt", h, HS), H(q, 0, HS), 2.0 ** 23, OP.min, OP.min)
-        cp(E, S("mm", o + SEG - 1, o + HS, SEG))
-        tt(S("pz", o + SEG - 1, o + HS, SEG), E, S("thrs"), OP.is_ge)
-        act(S3("e3", 8 * h, 8 * h + 8, 0, SEG), H(q, 2, HS))
-        act(H("es", h), S3("e3", 8 * h, 8 * h + 8, 1, 17))
-        tt(H("ff", h, HS), IND(E, S("le", 0, 9)), M, OP.is_equal)
-        scan(H("s2", h, HS), H("pz", h, HS), H("ff", h, HS), 0.0, OP.add, OP.mult)
-        tt(H("lq", h), IND(H("s2", h, HS), S("ll")), S("dm"), OP.mult)
-        mm(S("pr", 288 + 8 * h, 296 + 8 * h), H("lq", h), S("qm"), True, True)
-        tt(H("oh", h), IND(E, S("lj")), H("p16", h), OP.is_equal)
-
-    def newv(t):
-        cp(S("wi"), S("pr", 288, 304))
-        ts(H("a1", 0, 16), S("wi"), 4095 | (1 << 22), OP.bitwise_and)
-        tt(A2(0), H("a1", 0, 16), H("kk", 0, 16), OP.min)
-        cp(S("ox"), A2(0))
-        X = IND(S("boxw"), S("ox"))
-        act(S("yy"), X, AF.Identity, bias=col("drc", 4 + t))
-        ts(S("ym"), X, col("drc", 8 + t), OP.is_lt, 256.0, OP.mult)
-        if t < 2:
-            s = "snd%d" % t
-            ts(H("a1", 1, 16), S("wi"), 12, OP.arith_shift_right, 1023, OP.bitwise_and)
-            cp(S3(s, 0, 8, 32, 34), H("a1", 1, 16))
-            tt(S3(s, 0, 8, 34, 36), H("a1", 1, 16), S3(s, 0, 8, 32, 34), OP.subtract)
-            tt(S3(s, 0, 8, 0, 32), S("yy"), S("ym"), OP.add)
-        else:
-            tt(S("vout"), S("yy"), S("ym"), OP.add)
-            dma("S", T.yv[:], S("vout"), "o_yv", 65536)
-
-    def send(t):
-        s, r = "snd%d" % t, "rcv%d" % t
-        mk = masks_of(core, cores, topo)
-        trs = []
-        for q, d in enumerate(cores):
-            if d != core:
-                rid, pid = topo.addr(d, core)
-                trs.append(RemoteDMATransfer(dst_ids=[DstId(rid=rid, pnc=pid)], dma_engine_mask=sum(1 << e for e in mk[d]),
-                                             remote_sem=T.sem["arr%d" % t], src=T[s][:, q, 0:SENT], dst=T[r][:, rank, 0:SENT]))
-        add("G", lambda: g.remote_dma_fused(trs, local_sem=T.sem.sent), keys(S3(s, 0, 8, 0, SENT)), [], 1000, "sent",
-            -sum(len(m) for m in mk.values()))
-        n = sum(len(masks_of(c, cores, topo)[core]) for c in cores if c != core)
-        add("X", None, [], [(r, q * SLOT, q * SLOT + SLOT) for q in range(N) if q != rank], 0, "arr%d" % t, -n, DEAL, len(ops) - 1)
-        act(S3(r, rank, rank + 1, 0, SENT), S3(s, rank, rank + 1, 0, SENT))
-
-    def record(t, parts, bank):
-        for a, b in parts:
-            for c in range(a // 128, b // 128):
-                mm(H("pu0", c), H("oh", c), S("idb"), True, True)
-            tt(S("mc", a, b), S("pu0", a, b), S("ci", a, b), OP.mult)
-            act(S("ohs", a, b), S("pu0", a, b))
-            for k in (bank, "py") if t else ("py",):
-                mm(S(k, a, b), S("idf"), S("xf", a, b), True, False)
-                for c in range(a // 128, b // 128):
-                    mm(H(k, c), H("oh", c), H("dk", c), False, False)
-                    mm(H(k, 2 + c), H("es", c), S("idf"), False, False)
-                mm(S(k, a, b), H("ib", t), S("ohs", a, b), False, False)
-                mm(S(k, a, b), S("nidf"), S("mc", a, b), False, k == bank or not t)
-            if t:
-                tt(S("yr2", a, b), S(bank, a, b), S("rot", a, b), OP.mult)
-                tt(S("yr2", 256 + a, 256 + b), S(bank, 256 + a, 256 + b), S("rot", a, b), OP.mult)
-                mm(S("py", a, b), S("rmi"), S("yr2", a, b), False, False)
-                mm(S("py", 256 + a, 256 + b), S("rmi"), S("yr2", 256 + a, 256 + b), False, True)
-            act(S("ysb", a, b), S("py", a, b))
-        scat(S("rf"), S("oo"), S("ysb"))
-        if t == 2:
-            dma("S", T.yr[:], S("rf", 0, V), "o_yr", 512 * V)
-        else:
-            act(S("esb"), S("py", 256, 512), AF.Identity, bias=4097.0)
-
-    def newbox(t):
-        mm(S("pu1", 0, 256), S("idb"), S("k256"), True, False)
-        mm(S("pu1", 0, 256), S("idb"), S("boxw", 2560, 2816), False, False)
-        mm(S("pu1", 0, 256), S("idb"), S("yy"), False, True)
-        act(S("nbf"), S("pu1", 0, 256), AF.Identity, bias=MAGIC, scale=0.4999)
-        act(H("boxw", 7 + t, TH), S("nbf"), AF.Identity, bias=-MAGIC)
+            ts(e, S("oru", 16 * q, TH), W("owf", t, q, q + 1), OP.is_equal, col("ww", q), OP.mult)
+            mm(S("pn", 16 * q, 256), S("bo"), e, False, q == 15)
+        act(S("cb"), S("pn", 0, 256), AF.Sign)
+        wrap(S("pn", 256, 272), "cb", 0)
+        tt(W("a2", 1), S("pn", 256, 272), H("kk", 0, 16), OP.mult)
+        tt(W("a2", 1), W("a2", 1), W("owf", t), OP.max)
+        cp(S("oo"), W("a2", 1))
 
     def digits(t):
         act(S("ha"), IND(S("dh", 0, 513), S("sl")))
-        act(S("hb"), IND(S("dl", 0, 513), S("sl")))
-        for j, k in enumerate(("ha", "hb")):
-            for h in range(2):
-                mm(H("py", 2 * j + h), H(k, h), S("idb"), True, True)
-        act(S("ht"), S("py"))
+        act(S("hn"), IND(S("dl", 0, 513), S("sl")))
+        for h in range(2):
+            mm(H("py", h), H("ha", h), S("idb"))
+            group(H("py", 2 + h), [(S("idb"), S("thb")), (H("hn", h), S("ip24"))] + [(H("na", h), S("bo8k"))] * (t == 2))
+        for h in range(2):
+            act(H("hta", h), H("py", h), scale=col("ww", 16 + h))
+        act(S("t2"), S("py", 256, 512), AF.Identity, bias=-8.0 + (2.0 ** 17 if t == 2 else 0.0))
+
+    def choose(t, h):
+        q, M = "pq%d" % h, H("mm", h, HS)
+        tt(H("tt", h, HS), H(q, 1, HS), S("fk"), OP.max)
+        scan(M, H("tt", h, HS), H(q, 0, HS), 2.0 ** 23, OP.min, OP.min)
+        tt(H("lq", h), IND(M, S("ll")), S("dmx"), OP.min)
+        P = H("pr", 36 + h, 8)
+        mm(P, H("lq", h), S("qm"))
+        ts(H("ox", h, 8), P, pc[4], OP.subtract)
+        act(S3("e3", 8 * h, 8 * h + 8), H(q, 2, HS))
+        X = IND(H("bd", h, 4096), H("ox", h, 8))
+        act(H("yy", h), X, AF.Identity, bias=col("drc", 4 + t), scale=1 / 128.0 if t < 2 else 1.0)
         if t == 2:
-            for h in range(2):
-                mm(H("pr", 40 + h, 8), H("na", h), H("g24", 2, 8), True, True)
-                ts(H("a2", 4 + h, 8), H("pr", 40 + h, 8), 0.0, OP.is_equal, col("ww", 16 + h), OP.mult)
+            ts(H("ys", h), X, col("drc", 10), OP.is_lt, 256.0, OP.mult)
+            tt(H("vout", h), H("yy", h), H("ys", h), OP.add)
+            return
+        act(H("ys", h), X, AF.Sign, bias=col("drc", 8 + t))
+        cp(H("me", h, 8), S("mm", HS * h + SEG - 1, HS * h + HS, SEG))
+        tt(H("ff", h, HS), IND(H("me", h, 8), S("le", 0, 9)), M, OP.is_equal)
+        scan(H("s2", h, HS), H("pr", h, HS), H("ff", h, HS), 0.0, OP.add, OP.mult)
+        tt(H("lq", 2 + h), IND(H("s2", h, HS), S("ll")), S("dm"), OP.mult)
+        P = H("pr", 38 + h, 8)
+        mm(P, H("lq", 2 + h), S("qm"))
+        s = "snd%d" % t
+        cp(S3(s, 4 * h, 4 * h + 4, 32, 34), P)
+        tt(S3(s, 4 * h, 4 * h + 4, 34, 36), P, S3(s, 4 * h, 4 * h + 4, 32, 34), OP.subtract)
+        tt(S3(s, 4 * h, 4 * h + 4, 0, 32), H("yy", h), H("ys", h), OP.subtract)
+
+    def send(t, h):
+        s, r, late = "snd%d" % t, "rcv%d" % t, int(h == own)
+        sem = "arr%d%d" % (t, late)
+
+        def plan(c, half):
+            return masks_of(c, [d for d in cores[4 * half:4 * half + 4] if d != c], topo)
+        mk = plan(core, h)
+        trs = []
+        for d, es in mk.items():
+            rid, pid = topo.addr(d, core)
+            trs.append(RemoteDMATransfer(dst_ids=[DstId(rid=rid, pnc=pid)], dma_engine_mask=sum(1 << e for e in es),
+                                         remote_sem=T.sem[sem], src=T[s][:, cores.index(d), 0:SENT], dst=T[r][:, rank, 0:SENT]))
+        add("G", lambda: g.remote_dma_fused(trs, local_sem=T.sem.sent), keys(S3(s, 4 * h, 4 * h + 4, 0, SENT)), [], 900 + FIRST * (t + late == 0), "sent",
+            -sum(len(m) for m in mk.values()))
+        srcs = [q for q in range(4 * h, 4 * h + 4) if q != rank]
+        n = sum(len(plan(cores[q], own)[core]) for q in srcs)
+        add("X", None, [], [(r, q * SLOT, q * SLOT + SLOT) for q in srcs], 0, sem, -n, DEAL, len(ops) - 1)
+        if late:
+            act(S3(r, rank, rank + 1, 0, SENT), S3(s, rank, rank + 1, 0, SENT))
+
+    def turn(t, out, part, P):
+        n = part[2]
+        a = part[1][0][1]
+        group(P, [(S("rm"), part), (S("ip24"), S("rot", a, a + n))] + [(S("in23"), S("one"))] * (n == 128))
+        tt(out, P, part, OP.max)
+
+    def record(t, h):
+        tt(H("oh", h), IND(H("mm", h, HS), S("ll")), H("p16", h), OP.is_equal)
+        mm(H("py", 2 + h), H("oh", h), S("nidb"))
+        tt(H("mc", h), H("py", 2 + h), H("ci", h), OP.mult)
+        group(H("py", h), [(S("idf"), H("xf", h)), (H("oh", h), H("dk", h)), (H("oh", h), H("ib", t))]
+              + [(S("in23"), H("rot", h))] * (t > 0) + [(S("idf"), H("mc", h))])
+        act(H("ya" if t else "ysb", h), H("py", h), AF.Identity, bias=1280.0)
+        if t:
+            turn(t, H("ysb", h), H("ya", h), H("py", 2 + h))
+        cp(IND(S("rf"), H("oo", h, 8)), H("ysb", h))
+
+    def newbox(t, h):
+        P, o = S("pr", 336, 464), 4096 * h + 2049
+        group(P, [(S("i05"), S("mh")), (S("i05"), S("bd", o, o + 2047, 16)), (S("i64"), H("yy", h))])
+        ts(H("boxw", 14 + 2 * t + h), P, MAGIC + 128, OP.add, MAGIC, OP.subtract)
 
     def askers(t, h):
-        flag = S("pz", HS * h + SEG - 1, HS * h + HS, SEG)
-        if t < 2:
-            ts(H("wa", h, 8), flag, col("ww", 16 + h), OP.mult)
-        else:
-            tt(H("wa", h, 8), flag, H("a2", 4 + h, 8), OP.mult)
-        tt(H("hw", h), IND(H("wa", h, 8), S("lj")), H("ht", 2 + h), OP.mult)
+        pick(H("es", h), S3("e3", 8 * h, 8 * h + 8, 1, 17), [[0, 128]], 0, 0)
+        tt(H("hw", h), IND(H("mm", h, HS), S("ll")), H("t2", h), OP.is_ge)
+        if t:
+            group(H("pz", h), [(H("es", h), S("idf")), (S("in23"), H("rot", h))])
+            act(H("ea", h), H("pz", h))
+            turn(t, H("esel", h), H("ea", h), H("pz", 2 + h))
 
     def makers(t):
+        group(H("pn", 0), [(H("hta", h), H("hw", h)) for h in halves])
+        tt(S("hm"), H("pn", 0), S("bo"), OP.mult)
+        P = S("pn", 256, 512)
+        mm(P, S("idbig"), S("hn"), True, False)
         for h in range(2):
-            mm(H("pn", 2), H("ht", h), H("hw", h), h == 0, h == 1)
-        tt(S("hm"), H("pn", 2), S("bo"), OP.mult)
-        mm(S("pn", 256, 512), S("hm"), S("ha"), True, True)
-        tt(S("hu"), S("pn", 256, 512), S("hb"), OP.mult)
-        mm(S("pn", 256, 512), S("bo"), S("hu"), True, False)
-        if t == 2:
-            mm(S("pn", 256, 512), S("idbig"), S("na"), False, False)
-        mm(S("pn", 256, 512), S("bob"), S("ohs"), False, True)
-        tt(S("fl"), S("pn", 256, 512), S("thr"), OP.is_lt)
-        tt(H("yhs", t, TH), S("py", 256, 512), S("fl"), OP.mult)
+            mm(H("pn", 2 + h), H("hw", h), H("dw", h), False, False)
+        mm(P, S("hm"), S("ha"), False, True)
+        tt(S("flu"), P, S("thrn"), OP.is_lt)
+        if t == 0:
+            mm(S("pz", 0, 256), S("bo8k"), S("flu"), True, False)
+            for h in range(2):
+                mm(H("pz", h), H("es", h), S("idf"), False, h == 1)
+            act(H("yhs", t, TH), S("pz", 0, 256), AF.Relu, bias=-8192.0)
+        else:
+            mm(S("pn", 0, 256), S("bo"), S("flu"))
+            tt(H("yhs", t, TH), S("pn", 0, 256), S("esel"), OP.mult)
         dma("S", T.yh[:, TH * t:TH * t + TH], H("yhs", t, TH), "o_h%d" % t, 512 * TH)
         if t == 2:
             return
-        wrap("pn", 256, "fl", 0)
-        ts(A2(3), S("pn", 256, 272), 0.5, OP.is_lt, 4096.0, OP.mult)
-        tt(A2(3), A2(3), SK(t), OP.add)
-        tt(A2(5), A2(3), H("kk", 2, 16), OP.min)
-        cp(S("osa"), A2(5))
+        P = S("pr", 464, 480)
+        wrap(P, "flu", 0, [(S("idf"), W("sk", j)) for j in ((0,), (1, 2))[t]])
+        tt(W("a2", 3), P, H("kk", 1, 16), OP.max)
+        ts(S("osa"), W("a2", 3), -4096.0, OP.mult, 4096.0, OP.add)
+        ts(IND(S("tb"), S("osa")), H("yhs", t, TH), 1.0, OP.mult, 4097.0, OP.add)
         if t == 0:
-            scat(S("tb", 0, TBD + TH), S("osa"), S("esb"))
-            act(S("sm"), S("tb", 1, 257), AF.Sign, bias=-4090.0)
-            mm(S("pz", 0, 256), S("idf"), S("tb", 1, 257), True, False)
-            mm(S("pz", 0, 256), S("m2"), S("sm"), False, True)
-            act(S("tb", 257, 513), S("pz", 0, 256), AF.Identity, bias=-2048.5)
-        else:
-            ts(H("a1", 3, 16), S("wi"), 23, OP.arith_shift_right)
-            ts(A2(4), H("a1", 3, 16), 512.0, OP.mult)
-            tt(A2(3), A2(3), A2(4), OP.add)
-            tt(A2(3), A2(3), H("kk", 2, 16), OP.min)
-            cp(S("osb"), A2(3))
-            scat(S("tb", 256, TBD + 2 * TH), S("osa"), S("esb"))
-            scat(S("tb", 0, TBD + TH), S("osb"), S("esb"))
+            act(S("tb", 257, 513), S("tb", 1, 257), AF.Relu, bias=-4097.0)
 
+    a, b = halves
+    cp(S("rf", 0, V), S("reci"))
     for t in range(RO):
-        pre(t)
-        boxlist(t, 0)
-        boxlist(t, 1)
-        if t == 0:
-            cp(S("xf"), IND(S("reci"), OW(0)))
-            cp(S("rf", 0, V), S("reci"))
-        else:
-            act(S("xf"), IND(S("rf", 0, V), OW(t)))
+        pre(t, a, True)
+        pre(t, b, False)
         shapes(t)
-        keys_init(t)
+        for h in halves:
+            keys_init(t, h)
         digits(t)
         objects(t)
-        for u in range(4):
-            chunk(t, u)
-        red(0, False)
-        bounds(t, 0, True)
-        bounds(t, 1, False)
-        for u in range(4, 8):
-            chunk(t, u)
-        choose(0)
-        askers(t, 0)
-        red(1, True)
-        choose(1)
-        askers(t, 1)
-        if t < 2:
-            newv(t)
-            send(t)
-            newbox(t)
-            record(t, [(0, 256)], "pq0")
-            if t == 1:
-                act(S("vis"), H("sr", 1, TH), scale=-1.0)
-                scat(S("shb"), S("oo"), S("vis"))
-        else:
-            record(t, [(0, 128), (128, 256)], "pq0")
-            newv(t)
+        for h in halves:
+            bounds(t, h)
+        for j, h in enumerate(halves):
+            for k in range(4):
+                chunk(t, h, k, MODES[t][4 * j + k])
+            red(t, h)
+        for h in halves:
+            choose(t, h)
+            if t < 2:
+                send(t, h)
+                newbox(t, h)
+            record(t, h)
+            askers(t, h)
+        if t == 1:
+            tt(IND(S("shb"), S("oo")), H("sr", 1, TH), S("rn"), OP.mult)
+        if t == 2:
+            dma("S", T.yr[:], S("rf", 0, V), "o_yr", 512 * V)
+            dma("S", T.yv[:], S("vout"), "o_yv", 65536)
         makers(t)
 
-    emit(g, T, order(ops, psum))
+    emit(g, T, order(ops, psum, own))
 
 
 def schedule(ops):
@@ -599,7 +578,7 @@ def schedule(ops):
     return best[1]
 
 
-def order(ops, psum):
+def order(ops, psum, kind):
     seen = {}
     for i, o in enumerate(ops):
         deps, soft = set(), set()
@@ -622,7 +601,9 @@ def order(ops, psum):
         if o["e"] in "SG" or o["sem"]:
             soft |= {j for j in range(i) if ops[j]["e"] == o["e"] and (ops[j]["sem"] or o["e"] == "G")}
         o["deps"], o["pred"] = deps, deps | soft
-    out = schedule(ops)
+    if kind not in ORDERS:
+        ORDERS[kind] = schedule(ops)
+    out = ORDERS[kind]
     place = {i: k for k, i in enumerate(out)}
     for o in ops:
         o["deps"] = {place[j] for j in o["deps"]}

@@ -10,18 +10,18 @@ HS = 8 * SEG
 OFF = 34 * 4096
 RHO = 1.8
 MAGIC = 12582912.0
-TBD = 776
+TBD = 520
 WIDTHS = {
-    I32: dict(obi=16, reci=V, shi=V, bdi=S0, pi=8, lei=16, lli=8, xi=TH, ci=TH, owi=48),
-    U16: dict(le=16, ll=8, ow=48, cu=TH, oru=TH, sl=16, ox=16, oo=16, osa=16),
-    BF: dict(sh1=V, shb=V + TH, boxw=NB + 2 * TH, v0=TH, drb=8, dg=144, one=128, em=512, idb=128, nidb=128, bo=128, e8=128,
-             bo8k=128, idbig=128, ib=384, dk=256, dw=256, in23=128, ip24=128, i64=128, i05=128, mh=128, g24=32, hi=432,
-             lo=HS, thb=128, dm=128, fc=160, fd=160, kpa=2 * HS, kpb=2 * HS, vt=256, bd=8192, eq=4096, dh=520, dl=520,
-             ha=TH, hn=TH, hta=TH, hw=TH, hm=128, flu=TH, thrn=TH, cb=TH, sr=3 * TH, rot=TH, rn=TH, na=TH, oh=256,
-             ff=2 * HS, yy=TH, ys=TH, vout=TH),
-    F32: dict(rf=V + TH, tb=TBD + TH, drc=16, io=V, pc=16, idf=128, rm=128, qm=8, vqx=160, hq=HS, e1=160, dmz=HS, fk=HS,
-              p16=256, dmx=128, iw=16, kk=32, ww=24, thr=256, lef=16, me=16, owf=48, xf=TH, sk=48, hv=TH, hr=TH, es=256,
-              t2=256, tt=2 * HS, mm=2 * HS, s2=2 * HS, lq=512, a2=128, mc=TH, ya=TH, ysb=TH, ea=TH, esel=TH, yhs=3 * TH),
+    I32: dict(obi=16, reci=V, shi=V, bdi=S0, pi=8, lei=16, lli=8, ci=TH, owi=48),
+    U16: dict(le=16, ll=8, ow=48, cu=TH, oru=TH, sl=16, sn=16, rev=16, ox=16, oo=16, osa=16),
+    BF: dict(sh1=V, shb=V + TH, boxw=NB + 2 * TH, v0=TH, drb=8, dg=144, one=128, none=128, em=512, idb=128, nidb=128, bo=128,
+             bom=128, bo8k=128, idbig=128, dw=256, dk=256, ib=384, in23=128, ip22=128, in22=128, ip24=128, i64=128, i05=128,
+             cst=128, kr=128, mh=144, g24=24, hi=432, lo=HS, thb=128, jm=128, dm=128, fc=160, fd=160, kpa=2 * HS,
+             kpb=2 * HS, vt=256, bd=8192, eq=4096, dh=520, dl=520, ha=TH, hn=TH, hta=TH, hw=TH, hm=128, flu=TH, thrn=TH,
+             cb=TH, sr=3 * TH, rn=TH, na=TH, vis=TH, oh=256, ff=2 * HS, yy=TH, ys=TH, vout=TH),
+    F32: dict(rf=V + TH, tb=TBD + TH, drc=16, io=V, pc=16, idf=128, nidf=128, rm=128, vqx=160, hq=HS, e1=160, dmz=HS, fk=HS,
+              p16=256, dmx=128, iw=16, kk=40, ww=24, me=2 * HS, owf=48, xd=512, xa=256, xs=512, sk=16, hv=TH, hr=TH,
+              es=512, t2=256, tt=2 * HS, mm=2 * HS, s2=2 * HS, lq=512, a2=64, mc=TH, ea=TH, yhs=3 * TH),
 }
 SCRATCH = {k: ("sbuf", [128, n], d) for d, w in WIDTHS.items() for k, n in w.items()}
 SCRATCH.update({k: ("sbuf", [128, 8, SLOT], BF) for k in ("snd0", "snd1", "rcv0", "rcv1")})
@@ -30,10 +30,10 @@ SCRATCH.update({k: ("psum", [128, 512], F32) for k in ("pq0", "pq1", "pz", "pr",
 SEMAPHORES = ["sD", "sA", "sP", "sG", "arr00", "arr01", "arr10", "arr11", "sent", "l_ob", "l_rec", "l_box", "l_tv", "l_dr",
               "l_bd", "l_sh", "o_yr", "o_yv", "o_h0", "o_h1", "o_h2"]
 
-MODES = ["DADADADD", "DADADADD", "DADADADD"]
-HOP, DEAL, ROUNDS, SEED, SHAKE = 190, 2600, 30, 1, 1000
-CY, GAT, SCA, PE = 0.83, 1.5, 3.5, 0.37
-FIRST = 2500
+MODES = ["DADADADD", "DADDDADD", "DADDDADD"]
+BANKS = ["pu0", "pu1", "pr", "pu0", "pu1", "pu0", "pu1", "pu0"]
+HOP, DEAL, ROUNDS, SEED, SHAKE = 230, 2000, 60, 1, 800
+CY, GAT, SCA, PE, DF, AFX, FIRST, DMA, RATE = 0.83, 1.4, 2.8, 0.37, 25, 45, 1200, 1600, 220
 ORDERS = {}
 
 
@@ -53,7 +53,7 @@ def rank_program(g, core, T, topo):
     if rank is None:
         return
     cores = list(T.cores)
-    ops = []
+    ops, table = [], []
     psum = {k for k, s in SCRATCH.items() if s[0] == "psum"}
     own = rank // 4
     halves = (1 - own, own)
@@ -73,6 +73,12 @@ def rank_program(g, core, T, topo):
 
     def H(name, h, w=128):
         return S(name, w * h, w * h + w)
+
+    def W(name, t, a=0, b=16):
+        return S(name, 16 * t + a, 16 * t + b)
+
+    def WH(name, t, h):
+        return W(name, t, 8 * h, 8 * h + 8)
 
     def col(name, j):
         return S(name, j, j + 1)
@@ -96,7 +102,7 @@ def rank_program(g, core, T, topo):
         if a[2] < 0:
             return add("D", fn, keys(*ins), keys(out), 50 + CY * GAT * out[2])
         half = out[3] and all(x[3] for x in ins if isinstance(x, tuple) and x[2] > 1)
-        add("D", fn, keys(*ins), keys(out), 35 + CY * max(64, k * out[2] * (0.5 if half else 1.0)))
+        add("D", fn, keys(*ins), keys(out), DF + CY * max(64, k * out[2] * (0.5 if half else 1.0)))
 
     def cp(out, in_):
         vec(lambda: g.vector.tensor_copy(out[0], in_[0]), out, [in_])
@@ -118,15 +124,16 @@ def rank_program(g, core, T, topo):
         vec(lambda: g.vector.memset(out[0], c), out, [])
 
     def act(out, a, func=AF.Copy, bias=0.0, scale=1.0):
-        cost = 65 + CY * GAT * out[2] if a[2] < 0 else 60 + CY * max(64, out[2])
-        if func == AF.Exp and not any(o.get("exp") for o in ops):
+        cost = 65 + CY * GAT * out[2] if a[2] < 0 else AFX + CY * max(64, out[2])
+        if not table:
+            table.append(len(ops))
             cost += 1300
-        add("A", lambda: g.scalar.activation(out[0], a[0], func, bias=val(bias), scale=val(scale)), keys(a, bias, scale), keys(out), cost)
-        ops[-1]["exp"] = func == AF.Exp
+        add("A", lambda: g.scalar.activation(out[0], a[0], func, bias=val(bias), scale=val(scale)), keys(a, bias, scale), keys(out),
+            cost, after=table[0] if table[0] < len(ops) else None)
 
     def mm(out, lhsT, rhs, start=True, stop=True):
         add("P", lambda: g.tensor.matmul(out[0], lhsT[0], rhs[0], start, stop), keys(lhsT, rhs), keys(out),
-            10 + PE * max(min(64, lhsT[2]), rhs[2]) * (1 if lhsT[3] else 4))
+            PE * max(min(64, lhsT[2]), rhs[2]) * (1 if lhsT[3] else 4))
 
     def group(out, terms):
         for j, (lhsT, rhs) in enumerate(terms):
@@ -148,7 +155,7 @@ def rank_program(g, core, T, topo):
     def dma(q, out, in_, sem, nbytes):
         eng = {"S": g.sync, "A": g.scalar, "G": g}[q]
         moved[0] = moved[0] + nbytes if sem[0] == "l" else nbytes
-        add(q, lambda: eng.dma_start(val(out), val(in_)), keys(in_), keys(out), 60, sem, 16, 1800 + moved[0] / 190)
+        add(q, lambda: eng.dma_start(val(out), val(in_)), keys(in_), keys(out), 60, sem, 16, DMA + moved[0] / RATE)
 
     dma("S", S("obi"), T.ob[:], "l_ob", 8192)
     dma("A", S("shi", p=(0, 8)), T.shp[:], "l_sh", 32 * V)
@@ -158,7 +165,8 @@ def rank_program(g, core, T, topo):
     dma("A", S("drb", 0, 3), T.dr[:], "l_dr", 4096)
     dma("S", S("bdi"), T.bound[:], "l_bd", 512 * S0)
 
-    pc = [col("pc", j) for j in range(11)]
+    pc = [col("pc", j) for j in range(14)]
+    QM = S("kk", 32, 40)
     iota(S("pi", 0, 1), [[0, 1]], 0, 1)
     ms(S("one"), 1.0)
     pick(S("idb"), S("one"), [[-1, 128]], 0)
@@ -166,9 +174,7 @@ def rank_program(g, core, T, topo):
     iota(S("io", 0, 256), [[1, 256]], 0)
     iota(S("iw"), [[16, 16]], 0)
     iota(S("em"), [[1, 32], [0, 16]], 0)
-    iota(S("io", 256, V), [[1, V - 256]], 256)
     iota(S("hi", 0, HS), [[-34, 8], [0, SEG]], 239)
-    iota(S("hi", HS, 432), [[0, 432 - HS]], 0)
     iota(S("lo"), [[0, 8], [1, SEG]], -17)
     iota(S("fk"), [[0, 8], [1, SEG]], -4097, 16)
     iota(S("fc", 1, HS + 1), [[16, 8], [1, SEG]], -1)
@@ -178,95 +184,105 @@ def rank_program(g, core, T, topo):
     for k in ("fc", "fd"):
         iota(S(k, 1, HS + 2, SEG), [[0, 9]], -5)
     iota(S("thb"), [[-34, 8], [0, 16]], 239)
-    iota(S("p16", 0, 128), [[0, 8], [1, 16]], -4096, 16)
-    iota(S("dm"), [[0, 8], [1, 16]], 0)
+    iota(S("jm"), [[0, 8], [1, 16]], 0)
     iota(S("lli"), [[SEG, 8]], SEG - 1)
+    iota(S("dh", 0, 256), [[-1, 16], [0, 16]], 15)
+    iota(S("dl", 0, 256), [[0, 16], [-1, 16]], 15)
     for k in ("tb", "dh", "dl"):
-        iota(S(k, 0, 1), [[0, 1]], 0)
-    iota(S("dh", 1, 513), [[0, 2], [1, 16], [0, 16]], 0)
-    iota(S("dl", 1, 513), [[0, 32], [1, 16]], 0)
-    iota(S("tb", 513, 769), [[0, 256]], 0)
+        iota(S(k, 256, 257), [[0, 1]], 0)
+    iota(S("dh", 257, 513), [[1, 16], [0, 16]], 0)
+    iota(S("dl", 257, 513), [[0, 16], [1, 16]], 0)
     ts(col("pi", 1), col("pi", 0), 15, OP.bitwise_and)
     ts(col("pi", 2), col("pi", 0), 4, OP.arith_shift_right)
     ts(col("pi", 3), col("pi", 0), 31, OP.bitwise_and)
     cp(S("pc", 0, 4), S("pi", 0, 4))
-    ts(S("e8"), S("bo"), pc[0], OP.is_equal)
+    ts(S("bom"), S("bo"), pc[0], OP.is_equal)
     ts(S("bo"), S("bo"), pc[2], OP.is_equal)
     ts(S("em"), S("em"), pc[3], OP.is_equal, -1.0, OP.mult)
-    for j, sc in enumerate((32.0, 2.0 ** 21, 1.0, 128.0)):
+    for j, sc in enumerate((32.0, 2.0 ** 21, 1.0)):
         ts(H("g24", j, 8), S("io", 0, 8), pc[2], OP.is_equal, sc, OP.mult)
-    ts(S("qm"), S("io", 0, 8), pc[2], OP.is_equal)
+    ts(QM, S("io", 0, 8), pc[2], OP.is_equal)
     ms(S("dg"), 0.0)
-    cp(S("dg", 15, 143, 16), S("qm"))
+    cp(S("dg", 15, 143, 16), QM)
     ts(S("iw"), S("iw"), pc[1], OP.add)
+    ts(S("rev"), S("iw"), -1.0, OP.mult, 255.0, OP.add)
     top = 108 * math.log(2.0)
     for h in range(2):
         act(col("ww", 16 + h), pc[0], AF.Exp, bias=top - 128 * h * math.log(RHO), scale=-math.log(RHO))
     act(S("ww", 0, 16), S("iw"), AF.Exp, bias=top, scale=-math.log(RHO))
-    act(S("thr"), S("io", 0, 256), AF.Exp, bias=top + math.log(2.5), scale=-math.log(RHO))
-    act(S("thrn"), S("thr"), scale=-1.0)
+    act(S("thrn"), S("io", 0, 256), AF.Exp, bias=top + math.log(2.5), scale=-math.log(RHO))
+    ts(S("thrn"), S("thrn"), -1.0, OP.mult)
     act(S("ww", 18, 20), S("ww", 16, 18), scale=-5.0)
     ts(S("sh1", p=(0, 8)), S("shi", p=(0, 8)), 1.0, OP.add)
     for h, bank in enumerate(("py", "pz")):
-        mm(S(bank, 0, 448), S("e8", p=(0, 8)), S("sh1", 448 * h, 448 * h + 448, p=(0, 8)))
+        mm(S(bank, 0, 448), S("bom", p=(0, 8)), S("sh1", 448 * h, 448 * h + 448, p=(0, 8)))
         act(H("shb", h, 448), S(bank, 0, 448))
     act(pc[4], pc[2], AF.Identity, bias=7.0 * OFF, scale=-float(OFF))
-    act(pc[5], pc[0], AF.Identity, bias=-2047.0, scale=16.0)
+    act(pc[5], pc[0], AF.Identity, bias=-2040.0, scale=16.0)
+    act(pc[11], pc[0], AF.Identity, bias=-4096.0, scale=16.0)
+    ms(S("hi", HS, 432), 0.0)
     ts(S("hi", 0, HS), S("hi", 0, HS), 4096.0, OP.mult)
     tt(S("fk"), S("fk"), S("hi", 0, HS), OP.add)
-    ts(S("fk", SEG - 1, HS, SEG), S("fk", SEG - 1, HS, SEG), 2032.0, OP.add)
+    ts(S("fk", SEG - 1, HS, SEG), S("fk", SEG - 1, HS, SEG), 2039.0, OP.add)
     ms(S("fk", 0, HS, SEG), 2.0 ** 22)
     ms(S("hi", 0, HS, SEG), 2.0 ** 22)
     ms(S("hi", HS + SEG - 1, 2 * HS, SEG), 2.0 ** 21)
     ms(S("lo", SEG - 1, HS, SEG), 2.0 ** 22)
     act(S("thb"), S("thb"), scale=4096.0)
-    tt(H("p16", 0), H("p16", 0), S("thb"), OP.add)
-    act(H("p16", 1), H("p16", 0))
-    ts(S("dm"), S("dm"), pc[1], OP.is_equal)
+    ts(S("dm"), S("jm"), pc[1], OP.is_equal)
     act(S("dmx"), S("thb"), AF.Identity, bias=pc[5])
     tt(S("dmx"), S("dmx"), S("dm"), OP.mult)
     ts(S("vqx", 0, HS + 1), S("fc", 0, HS + 1), pc[0], OP.is_equal, -2.0 ** 21, OP.mult)
     ts(S("e1", 1, HS + 2), S("fd", 1, HS + 2), pc[0], OP.is_equal, 2.0 ** -12, OP.mult)
     tt(S("dmz"), S("e1", 1, HS + 1), S("e1", 2, HS + 2), OP.subtract)
-    ts(S("lef"), S("iw"), -8.5, OP.add, 1.0 / SEG, OP.mult)
-    cp(S("lei"), S("lef"))
-    cp(S("le"), S("lei"))
+    ts(W("a2", 0), S("iw"), -8.5, OP.add, 1.0 / SEG, OP.mult)
+    cp(S("lei"), W("a2", 0))
+    ts(S("le"), S("lei"), float(SEG), OP.mult, SEG - 1.0, OP.add)
     cp(S("ll"), S("lli"))
     act(H("kk", 0, 16), S("iw"), AF.Identity, bias=V / 16.0, scale=1 / 16.0)
-    act(H("kk", 1, 16), S("iw"), AF.Identity, bias=1 - TBD / 4096.0, scale=-1 / 4096.0)
+    act(H("kk", 1, 16), S("iw"), AF.Identity, bias=-14 - TBD / 4096.0, scale=-1 / 4096.0)
     act(S("drc", 0, 1), S("drb", 0, 1), scale=-1.0)
     act(S("drc", 1, 3), S("drb", 1, 3), AF.Identity, bias=128.0, scale=-1.0)
     act(S("drc", 4, 6), S("drb", 0, 2), AF.Identity, bias=-2.0, scale=1 / 128.0)
     act(S("drc", 6, 7), S("drb", 2, 3), AF.Identity, bias=-256.0)
     act(S("drc", 8, 10), S("drb", 0, 2), AF.Identity, bias=-255.5)
     act(S("drc", 10, 11), S("drb", 2, 3), AF.Identity, bias=256.0, scale=-1.0)
-    cp(S("tb", 1, S0 + 1), S("bdi"))
-    ts(S("dh", 1, 513), S("dh", 1, 513), pc[1], OP.is_equal)
-    ts(S("dl", 1, 513), S("dl", 1, 513), pc[1], OP.not_equal)
+    cp(S("tb", 0, S0), IND(S("bdi"), S("rev")))
+    for a, b in ((0, 256), (256, 513)):
+        ts(S("dh", a, b), S("dh", a, b), pc[1], OP.is_equal)
+        ts(S("dl", a, b), S("dl", a, b), pc[1], OP.not_equal)
     act(S("idf"), S("idb"))
-    for k, sc in (("nidb", -1.0), ("ip24", 2.0 ** 24), ("i64", 64.0), ("i05", 0.5), ("in23", -2.0 ** 23)):
-        ts(S(k), S("idb"), sc, OP.mult)
-    ts(S("idbig"), S("idb"), 2.0 ** 99, OP.mult, 2.0 ** 13, OP.mult)
-    ts(S("bo8k"), S("bo"), 8192.0, OP.mult)
-    ms(S("mh"), -0.5)
+    for a in range(256, V, 256):
+        act(S("io", a, min(V, a + 256)), S("io", 0, min(V - a, 256)), AF.Identity, bias=float(a))
+    for k, sc in (("nidf", -1.0), ("nidb", -1.0), ("ip24", 2.0 ** 24), ("i64", 64.0), ("i05", 0.5), ("in23", -2.0 ** 23),
+                  ("ip22", 2.0 ** 22), ("in22", -2.0 ** 22)):
+        act(S(k), S("idb"), scale=sc)
     for t in range(RO):
-        ts(H("ib", t), S("idb"), float(NB + TH * t), OP.mult)
-    ts(H("dk", 0), S("idb"), pc[0], OP.mult)
-    ts(H("dk", 1), S("io", 0, 128), 128.0, OP.add)
-    tt(H("dk", 1), H("dk", 1), S("idb"), OP.mult)
+        act(H("ib", t), S("idb"), scale=float(NB + TH * t))
+    act(H("dk", 0), S("idb"), scale=pc[0])
+    act(pc[13], pc[0], AF.Identity, bias=128.0)
+    act(H("dk", 1), S("idb"), scale=pc[13])
+    ts(S("idbig"), S("idb"), 2.0 ** 99, OP.mult, 2.0 ** 13, OP.mult)
+    act(S("bo8k"), S("bo"), scale=8192.0)
+    act(S("bom"), S("bo"), AF.Identity, bias=-1.0)
+    ms(S("mh", 0, 128), -0.5)
+    ms(S("mh", 128, 136), -0.3125)
+    ms(S("none"), -1.0)
+    ms(S("cst"), 2.0 ** 20 - 7 * 4096.0)
     for h in range(2):
-        ts(H("dw", h), S("idb"), col("ww", 18 + h), OP.mult)
-    ts(pc[6], pc[1], 0.0, OP.is_equal, 2.0 ** 22, OP.mult)
-    ts(pc[7], pc[6], 2.0 ** 11, OP.mult, 2.0 ** 33, OP.add)
-    ts(pc[8], pc[1], 15.0, OP.is_equal, -2.0 ** 22, OP.mult)
-    ts(pc[9], pc[8], 0.5, OP.mult, 2.0 ** 21, OP.add)
-    ts(pc[10], pc[6], 2.0 ** -18, OP.mult, -1.0, OP.add)
-    tt(pc[10], pc[10], pc[0], OP.add)
+        act(H("dw", h), S("idb"), scale=col("ww", 18 + h))
+    ts(pc[6], pc[1], 0.0, OP.is_equal, -2.0 ** 21, OP.mult)
+    ts(pc[8], pc[1], 15.0, OP.is_equal, 2.0 ** 21, OP.mult)
+    act(pc[7], pc[6], AF.Identity, bias=-2.0 ** 32, scale=2.0 ** 11)
+    act(pc[9], pc[8], AF.Identity, bias=-2.0 ** 20, scale=0.5)
+    act(pc[12], pc[8], AF.Identity, bias=-0.5, scale=-1019.5 * 2.0 ** -21)
+    ts(pc[10], pc[6], -2.0 ** -17, OP.mult, pc[0], OP.add)
+    act(S("kr"), S("idb"), scale=pc[12])
     for j in range(2):
         ts(H("kpa", j, HS), S("fc", 1, HS + 1), pc[0], OP.is_equal, pc[6 + j], OP.mult)
         ts(H("kpb", j, HS), S("fc", 0, HS), pc[0], OP.is_equal, pc[8 + j], OP.mult)
     tt(S("hq"), S("vqx", 0, HS), S("vqx", 1, HS + 1), OP.subtract)
-    ts(S("rm"), S("io", 0, 128), pc[10], OP.is_equal)
+    ts(S("rm"), S("io", 1, 129), pc[10], OP.is_equal)
 
     def vhalf(t, h):
         return H("v0", h) if t == 0 else S3("rcv%d" % (t - 1), 4 * h, 4 * h + 4, 0, 32)
@@ -274,16 +290,17 @@ def rank_program(g, core, T, topo):
     def vblock(t, u):
         return H("v0", u, 32) if t == 0 else S3("rcv%d" % (t - 1), u, u + 1, 0, 32)
 
-    def W(name, t, a=0, b=16):
-        return S(name, 16 * t + a, 16 * t + b)
-
-    def WH(name, t, h):
-        return W(name, t, 8 * h, 8 * h + 8)
-
     def wrap(out, row, c0, more=()):
-        group(out, [(S("dg", 15 - r, 143 - r), S(row, c0 + r, c0 + TH, 16)) for r in range(16)] + list(more))
+        group(out, [(S("dg", 15 - r, 143 - r), S(row, c0 + r, c0 + 16 * out[2], 16)) for r in range(16)] + list(more))
 
-    def pre(t, h, direct):
+    def place(h, what):
+        first = dict(dif=("pr", 0), box=("pz", 440), ref=("pr", 152), new=("pr", 160), one=("py", 0), turn=("py", 0))
+        last = dict(dif=("pu0", 0), box=("pz", 448), ref=("pu0", 152), new=("pu0", 160), one=("pu1", 0),
+                    turn=("pq%d" % halves[0], 0))
+        bank, o = (first if h == halves[0] else last)[what]
+        return S(bank, o, o + dict(dif=HS, box=8, ref=8, new=128, one=128, turn=256)[what])
+
+    def pre(t, h):
         if t == 0:
             cp(WH("ow", 0, h), H("obi", h, 8))
             ts(H("ci", h), IND(S("reci"), WH("ow", 0, h)), 4095, OP.bitwise_and)
@@ -291,14 +308,10 @@ def rank_program(g, core, T, topo):
             r = "rcv%d" % (t - 1)
             tt(WH("owi", t, h), S3(r, 4 * h, 4 * h + 4, 32, 34), S3(r, 4 * h, 4 * h + 4, 34, 36), OP.add)
             cp(WH("ow", t, h), WH("owi", t, h))
-        act(H("xf", h), IND(S("rf", 0, V), WH("ow", t, h)), AF.Identity, bias=-1280.0)
-        if t:
-            if direct:
-                cp(H("xi", h), IND(S("rf", 0, V), WH("ow", t, h)))
-            else:
-                ts(H("xi", h), H("xf", h), 1280.0, OP.add)
-            ts(H("ci", h), H("xi", h), 4095, OP.bitwise_and)
+            cp(H("ci", h), IND(S("rf", 0, V), WH("ow", t, h)))
+            ts(H("ci", h), H("ci", h), 4095, OP.bitwise_and)
         cp(H("cu", h), H("ci", h))
+        act(H("xd", 2 * h), IND(S("rf", 0, V), WH("ow", t, h)))
         for k in range(4):
             mm(S("pz", 128 * h, 128 * h + 128, p=(32 * k, 32 * k + 32)), vblock(t, 4 * h + k), S("idb"))
         if t:
@@ -306,65 +319,72 @@ def rank_program(g, core, T, topo):
         else:
             act(H("vt", h), H("pz", h))
 
-    def chunk(t, h, k, mode):
+    def chunk(t, h, k, j):
         src = IND(S("boxw", 0, NB + TH * t), H("cu", 4 * h + k, 32))
         dst = H("bd", 8 * h + k, 512)
-        if mode == "D":
+        if MODES[t][j] == "D":
             cp(dst, src)
         else:
             act(dst, src)
         rows = (32 * k, 32 * k + 32)
-        group(S("pu%d" % (k % 2)), [(S("idb"), dst), (S("vt", 128 * h, 128 * h + 128, p=rows), S("em", p=rows))])
-        act(H("bd", 8 * h + 4 + k, 512), S("pu%d" % (k % 2)), AF.Abs)
+        group(S(BANKS[j]), [(S("idb"), dst), (S("vt", 128 * h, 128 * h + 128, p=rows), S("em", p=rows))])
+        act(H("bd", 8 * h + 4 + k, 512), S(BANKS[j]), AF.Abs)
 
     def red(t, h):
         q, o, n = "pq%d" % h, 4096 * h + 2048, 17 if t else 16
         for u in range(n):
-            mm(S(q, 1 + u, 432, SEG), S("bd", o + u % 16, o + 2048, 16), S("g24", 0, 24), False, u == n - 1)
+            mm(S(q, 1 + u, 432, SEG), S("bd", o + u % 16, o + 2048, 16), S("g24"), False, u == n - 1)
         if t:
-            cp(S("bd", o, o + 2048, 16), S("bd", o - 2048, o, 16))
-        act(S("bd", o + 1, o + 2048, 16), vhalf(t, h), AF.Identity, bias=col("drc", t), scale=128.0 if t else 1.0)
+            cp(S("bd", o + 7, o + 2048, 16), S("bd", o - 2048, o, 16))
+        act(S("bd", o + 8, o + 2048, 16), vhalf(t, h), AF.Identity, bias=col("drc", t), scale=128.0 if t else 1.0)
 
-    def shapes(t):
-        P = S("pz", 256, 272)
-        act(H("sr", t, TH), IND(S("shb", 0, V), W("ow", t)))
-        wrap(P, "sr", TH * t)
-        if t < 2:
-            ts(S("sl"), P, 1 / 16.0, OP.mult)
-            act(W("sk", t), P, scale=-2.0 ** -16)
-        else:
-            act(W("sk", t), P, AF.Abs, scale=1 / 16.0)
-            ts(W("a2", 6), P, 0.0, OP.is_lt, 256.0, OP.mult)
-            tt(W("a2", 6), W("a2", 6), W("sk", t), OP.add)
-            cp(S("sl"), W("a2", 6))
-        act(S("hv"), IND(S("tb", 0, 257 if t < 2 else 513), S("sl")))
-        if t:
-            act(S("hr"), S("hv"), AF.Relu, bias=-4096.0)
-            act(S("rot"), S("hr"), AF.Sign)
-        if t == 1:
-            act(S("rn"), S("rot"), AF.Identity, bias=1.0, scale=-2.0)
-            wrap(S("pz", 272, 288), "rot", 0)
-            act(W("sk", 2), S("pz", 272, 288), scale=-1 / 256.0)
+    def shapes(t, h):
+        P = H("pr", 60 + h, 8) if t == 0 or h != own else S("pz", 416, 424)
+        act(H("sr", 2 * t + h), IND(S("shb", 0, V), WH("ow", t, h)))
+        wrap(P, "sr", TH * t + 128 * h)
+        ts(H("sl", h, 8), P, -1 / 16.0, OP.mult, 256.0, OP.add)
         if t == 2:
-            act(S("na"), IND(S("tb", 256, 769), S("sl")), AF.Sign, bias=-4090.0)
+            ts(H("sn", h, 8), P, 1 / 16.0, OP.mult)
+        entry = IND(S("tb", 0, 256 if t < 2 else 513), H("sl", h, 8))
+        act(H("hv", h), entry)
+        if t:
+            act(H("hr", h), entry, AF.Relu, bias=-4096.0)
+            act(H("rn", h), entry, AF.Sign, bias=4090.0, scale=-1.0)
 
     def keys_init(t, h):
         q = "pq%d" % h
         mm(S(q, 0, 432), S("idb"), S("hi"), True, False)
         mm(H(q, 0, HS), S("idb"), S("lo"), False, False)
-        if t < 2:
-            mm(H("pr", h, HS), H("xf", h), S("dmz"))
+        if t:
+            for k in ("kpa", "kpb"):
+                mm(S(q, 0, 2 * HS), S("none"), S(k), False, False)
 
     def bounds(t, h):
         q = "pq%d" % h
+        mm(H(q, 1, HS), H("hv", h), S("vqx", 1, HS + 1), False, False)
         if t:
             mm(H(q, 1, HS), H("hr", h), S("hq"), False, False)
-            mm(S(q, 0, 2 * HS), H("rot", h), S("kpa"), False, False)
-            mm(S(q, 0, 2 * HS), H("rot", h), S("kpb"), False, False)
-            P = H("pr", 40 + h, 8)
-            mm(P, H("rot", h), H("g24", 3, 8))
-            tt(S("p16", 128 * h, 128 * h + 128, 16), P, S("fk", 1, HS, SEG), OP.add)
-        mm(H(q, 1, HS), H("hv", h), S("vqx", 1, HS + 1), False, False)
+            for k in ("kpa", "kpb"):
+                mm(S(q, 0, 2 * HS), H("rn", h), S(k), False, False)
+
+    def seen(t, h):
+        cp(H("xd", 2 * h + 1), H("ci", h))
+        if t:
+            bank = place(h, "turn")[1][0][0]
+            for j in range(2):
+                mm(H(bank, j), S("ip22"), H("rn", h), j == 0, False)
+            mm(H(bank, 0, 256), S("idf"), H("xd", h, 256), False, True)
+            act(S("xa"), H(bank, 0, 256), AF.Identity, bias=-2.0 ** 22)
+            for j in range(2):
+                mm(H(bank, 2 + j), S("in23"), H("rn", h), j == 0, False)
+            mm(H(bank, 1, 256), S("rm"), S("xa"), False, True)
+            tt(H("xs", h, 256), H(bank, 1, 256), S("xa"), OP.max)
+
+    def fields(t, h):
+        if t or h == halves[0]:
+            P = S("pz", 288, 416)
+            group(P, [(S("idb"), S("thb")), (S("idb"), S("jm"))] + [(S("none"), S("kr")), (H("rn", h), S("kr"))] * (t > 0))
+            act(H("p16", h), P, AF.Identity, bias=pc[11])
 
     def objects(t):
         cp(W("owf", t), S("obi") if t == 0 else W("owi", t))
@@ -381,8 +401,13 @@ def rank_program(g, core, T, topo):
         cp(S("oo"), W("a2", 1))
 
     def digits(t):
-        act(S("ha"), IND(S("dh", 0, 513), S("sl")))
-        act(S("hn"), IND(S("dl", 0, 513), S("sl")))
+        n = 256 if t < 2 else 513
+        if t == 0:
+            act(S("sk"), S("pr", 480, 496), AF.Identity, bias=-1 / 16.0, scale=2.0 ** -16)
+        if t == 2:
+            act(S("na"), IND(S("tb", 256, 513), S("sn")), AF.Sign, bias=-4090.0)
+        act(S("ha"), IND(S("dh", 0, n), S("sl")))
+        act(S("hn"), IND(S("dl", 0, n), S("sl")))
         for h in range(2):
             mm(H("py", h), H("ha", h), S("idb"))
             group(H("py", 2 + h), [(S("idb"), S("thb")), (H("hn", h), S("ip24"))] + [(H("na", h), S("bo8k"))] * (t == 2))
@@ -392,11 +417,14 @@ def rank_program(g, core, T, topo):
 
     def choose(t, h):
         q, M = "pq%d" % h, H("mm", h, HS)
+        if t < 2:
+            mm(place(h, "dif"), H("xd", 2 * h), S("dmz"))
         tt(H("tt", h, HS), H(q, 1, HS), S("fk"), OP.max)
-        scan(M, H("tt", h, HS), H(q, 0, HS), 2.0 ** 23, OP.min, OP.min)
+        for out in (M, H("me", h, HS))[:1 + (t < 2)]:
+            scan(out, H("tt", h, HS), H(q, 0, HS), 2.0 ** 23, OP.min, OP.min)
         tt(H("lq", h), IND(M, S("ll")), S("dmx"), OP.min)
-        P = H("pr", 36 + h, 8)
-        mm(P, H("lq", h), S("qm"))
+        P = place(h, "box")
+        mm(P, H("lq", h), QM)
         ts(H("ox", h, 8), P, pc[4], OP.subtract)
         act(S3("e3", 8 * h, 8 * h + 8), H(q, 2, HS))
         X = IND(H("bd", h, 4096), H("ox", h, 8))
@@ -406,12 +434,11 @@ def rank_program(g, core, T, topo):
             tt(H("vout", h), H("yy", h), H("ys", h), OP.add)
             return
         act(H("ys", h), X, AF.Sign, bias=col("drc", 8 + t))
-        cp(H("me", h, 8), S("mm", HS * h + SEG - 1, HS * h + HS, SEG))
-        tt(H("ff", h, HS), IND(H("me", h, 8), S("le", 0, 9)), M, OP.is_equal)
-        scan(H("s2", h, HS), H("pr", h, HS), H("ff", h, HS), 0.0, OP.add, OP.mult)
+        tt(H("ff", h, HS), IND(H("me", h, HS), S("le", 0, 9)), M, OP.is_equal)
+        scan(H("s2", h, HS), place(h, "dif"), H("ff", h, HS), 0.0, OP.add, OP.mult)
         tt(H("lq", 2 + h), IND(H("s2", h, HS), S("ll")), S("dm"), OP.mult)
-        P = H("pr", 38 + h, 8)
-        mm(P, H("lq", 2 + h), S("qm"))
+        P = place(h, "ref")
+        group(P, [(S("idb"), S("mh", 128, 136)), (H("lq", 2 + h), QM)])
         s = "snd%d" % t
         cp(S3(s, 4 * h, 4 * h + 4, 32, 34), P)
         tt(S3(s, 4 * h, 4 * h + 4, 34, 36), P, S3(s, 4 * h, 4 * h + 4, 32, 34), OP.subtract)
@@ -429,97 +456,98 @@ def rank_program(g, core, T, topo):
             rid, pid = topo.addr(d, core)
             trs.append(RemoteDMATransfer(dst_ids=[DstId(rid=rid, pnc=pid)], dma_engine_mask=sum(1 << e for e in es),
                                          remote_sem=T.sem[sem], src=T[s][:, cores.index(d), 0:SENT], dst=T[r][:, rank, 0:SENT]))
-        add("G", lambda: g.remote_dma_fused(trs, local_sem=T.sem.sent), keys(S3(s, 4 * h, 4 * h + 4, 0, SENT)), [], 900 + FIRST * (t + late == 0), "sent",
-            -sum(len(m) for m in mk.values()))
+        add("G", lambda: g.remote_dma_fused(trs, local_sem=T.sem.sent), keys(S3(s, 4 * h, 4 * h + 4, 0, SENT)), [],
+            800 + FIRST * (t + late == 0), "sent", -sum(len(m) for m in mk.values()))
         srcs = [q for q in range(4 * h, 4 * h + 4) if q != rank]
         n = sum(len(plan(cores[q], own)[core]) for q in srcs)
         add("X", None, [], [(r, q * SLOT, q * SLOT + SLOT) for q in srcs], 0, sem, -n, DEAL, len(ops) - 1)
         if late:
             act(S3(r, rank, rank + 1, 0, SENT), S3(s, rank, rank + 1, 0, SENT))
 
-    def turn(t, out, part, P):
-        n = part[2]
-        a = part[1][0][1]
-        group(P, [(S("rm"), part), (S("ip24"), S("rot", a, a + n))] + [(S("in23"), S("one"))] * (n == 128))
-        tt(out, P, part, OP.max)
-
     def record(t, h):
-        tt(H("oh", h), IND(H("mm", h, HS), S("ll")), H("p16", h), OP.is_equal)
-        mm(H("py", 2 + h), H("oh", h), S("nidb"))
-        tt(H("mc", h), H("py", 2 + h), H("ci", h), OP.mult)
-        group(H("py", h), [(S("idf"), H("xf", h)), (H("oh", h), H("dk", h)), (H("oh", h), H("ib", t))]
-              + [(S("in23"), H("rot", h))] * (t > 0) + [(S("idf"), H("mc", h))])
-        act(H("ya" if t else "ysb", h), H("py", h), AF.Identity, bias=1280.0)
-        if t:
-            turn(t, H("ysb", h), H("ya", h), H("py", 2 + h))
-        cp(IND(S("rf"), H("oo", h, 8)), H("ysb", h))
+        x = "xs" if t else "xd"
+        tt(H("oh", h), IND(H("mm", h, HS), S("ll")), H("p16", h if t else halves[0]), OP.is_equal)
+        group(place(h, "one"), [(S("nidf"), H(x, 2 * h + 1)), (H("oh", h), H("dk", h)), (H("oh", h), H("ib", t))])
+        act(H("mc", h), place(h, "one"), AF.Relu)
+        tt(IND(S("rf"), H("oo", h, 8)), H(x, 2 * h), H("mc", h), OP.add)
 
     def newbox(t, h):
-        P, o = S("pr", 336, 464), 4096 * h + 2049
-        group(P, [(S("i05"), S("mh")), (S("i05"), S("bd", o, o + 2047, 16)), (S("i64"), H("yy", h))])
+        P, o = place(h, "new"), 4096 * h + 2056
+        group(P, [(S("i05"), S("mh", 0, 128)), (S("i05"), S("bd", o, o + 2040, 16)), (S("i64"), H("yy", h))])
         ts(H("boxw", 14 + 2 * t + h), P, MAGIC + 128, OP.add, MAGIC, OP.subtract)
 
     def askers(t, h):
-        pick(H("es", h), S3("e3", 8 * h, 8 * h + 8, 1, 17), [[0, 128]], 0, 0)
         tt(H("hw", h), IND(H("mm", h, HS), S("ll")), H("t2", h), OP.is_ge)
-        if t:
-            group(H("pz", h), [(H("es", h), S("idf")), (S("in23"), H("rot", h))])
-            act(H("ea", h), H("pz", h))
-            turn(t, H("esel", h), H("ea", h), H("pz", 2 + h))
+        for j in range(1 + (t > 0)):
+            if h == own and j == 0:
+                act(H("es", 2 * j + h), S3("e3", 8 * h, 8 * h + 8, 1 + j, 17 + j))
+            else:
+                pick(H("es", 2 * j + h), S3("e3", 8 * h, 8 * h + 8, 1 + j, 17 + j), [[0, 128]], 0, 0)
 
     def makers(t):
-        group(H("pn", 0), [(H("hta", h), H("hw", h)) for h in halves])
-        tt(S("hm"), H("pn", 0), S("bo"), OP.mult)
+        group(H("pn", 0), [(S("idbig"), S("bom"))] + [(H("hta", h), H("hw", h)) for h in halves])
+        act(S("hm"), H("pn", 0), AF.Relu)
         P = S("pn", 256, 512)
         mm(P, S("idbig"), S("hn"), True, False)
         for h in range(2):
             mm(H("pn", 2 + h), H("hw", h), H("dw", h), False, False)
+        mm(P, S("nidb"), S("thrn"), False, False)
         mm(P, S("hm"), S("ha"), False, True)
-        tt(S("flu"), P, S("thrn"), OP.is_lt)
-        if t == 0:
-            mm(S("pz", 0, 256), S("bo8k"), S("flu"), True, False)
+        act(S("flu"), P, AF.Sign, scale=-1.0)
+        for j in range(1 + (t > 0)):
+            q = "pq%d" % ((own + j) % 2)
             for h in range(2):
-                mm(H("pz", h), H("es", h), S("idf"), False, h == 1)
-            act(H("yhs", t, TH), S("pz", 0, 256), AF.Relu, bias=-8192.0)
+                mm(H(q, h), H("es", 2 * j + h), S("idf"), h == 0, False)
+            if t:
+                mm(S(q, 0, 256), S(("ip22", "in22")[j]), S("rn"), False, False)
+            if j:
+                mm(S(q, 0, 256), S("cst"), S("em", 0, 256), False, False)
+            mm(S(q, 0, 256), S("bo8k"), S("flu"), False, True)
+        if t:
+            act(S("ea"), S("pq%d" % own, 0, 256), AF.Relu, bias=14 * 8192.0 - 2.0 ** 22)
+            tt(H("yhs", t, TH), S("pq%d" % (1 - own), 0, 256), S("ea"), OP.max)
         else:
-            mm(S("pn", 0, 256), S("bo"), S("flu"))
-            tt(H("yhs", t, TH), S("pn", 0, 256), S("esel"), OP.mult)
+            act(H("yhs", t, TH), S(q, 0, 256), AF.Relu, bias=14 * 8192.0)
         dma("S", T.yh[:, TH * t:TH * t + TH], H("yhs", t, TH), "o_h%d" % t, 512 * TH)
         if t == 2:
             return
-        P = S("pr", 464, 480)
-        wrap(P, "flu", 0, [(S("idf"), W("sk", j)) for j in ((0,), (1, 2))[t]])
+        P = S("pn", 0, 16)
+        wrap(P, "flu", 0, [(S("idf"), S("sk"))])
         tt(W("a2", 3), P, H("kk", 1, 16), OP.max)
-        ts(S("osa"), W("a2", 3), -4096.0, OP.mult, 4096.0, OP.add)
+        ts(S("osa"), W("a2", 3), -4096.0, OP.mult, -14 * 4096.0, OP.add)
         ts(IND(S("tb"), S("osa")), H("yhs", t, TH), 1.0, OP.mult, 4097.0, OP.add)
         if t == 0:
-            act(S("tb", 257, 513), S("tb", 1, 257), AF.Relu, bias=-4097.0)
+            act(S("tb", 257, 513), IND(S("tb", 0, 256), S("rev")), AF.Relu, bias=-4097.0)
 
-    a, b = halves
     cp(S("rf", 0, V), S("reci"))
     for t in range(RO):
-        pre(t, a, True)
-        pre(t, b, False)
-        shapes(t)
         for h in halves:
+            pre(t, h)
+            shapes(t, h)
             keys_init(t, h)
+            bounds(t, h)
+        seen(t, halves[0])
         digits(t)
         objects(t)
-        for h in halves:
-            bounds(t, h)
         for j, h in enumerate(halves):
             for k in range(4):
-                chunk(t, h, k, MODES[t][4 * j + k])
+                chunk(t, h, k, 4 * j + k)
             red(t, h)
+            fields(t, h)
+        if t == 1:
+            tt(S("vis"), H("sr", 1, TH), S("rn"), OP.mult)
+            wrap(S("pz", 424, 440), "vis", 0)
+            act(S("sk"), S("pz", 424, 440), AF.Identity, bias=-1 / 16.0, scale=2.0 ** -16)
+            cp(IND(S("shb"), S("oo")), S("vis"))
         for h in halves:
             choose(t, h)
+            if h != own:
+                seen(t, own)
+            record(t, h)
             if t < 2:
                 send(t, h)
                 newbox(t, h)
-            record(t, h)
             askers(t, h)
-        if t == 1:
-            tt(IND(S("shb"), S("oo")), H("sr", 1, TH), S("rn"), OP.mult)
         if t == 2:
             dma("S", T.yr[:], S("rf", 0, V), "o_yr", 512 * V)
             dma("S", T.yv[:], S("vout"), "o_yv", 65536)
@@ -539,11 +567,10 @@ def schedule(ops):
     def place(before, after, rank, tail):
         left = [len(b) for b in before]
         ready = list(tail)
-        pool = [i for i in range(n) if not left[i]]
+        pool = sorted((-rank[i], i) for i in range(n) if not left[i])
         busy, end = {}, [0.0] * n
         while pool:
-            i = min(pool, key=lambda k: (rank[k], k))
-            pool.remove(i)
+            i = pool.pop()[1]
             row = busy.setdefault(ops[i]["e"], [])
             s, c, at = ready[i], ops[i]["cost"], 0
             for a, b in row:
@@ -557,7 +584,8 @@ def schedule(ops):
                 ready[k] = max(ready[k], end[i] + x)
                 left[k] -= 1
                 if not left[k]:
-                    pool.append(k)
+                    pool.append((-rank[k], k))
+            pool.sort()
         return end
 
     late = [o["late"] for o in ops]

@@ -1,39 +1,44 @@
-import math
 from concourse.bass import DstId, RemoteDMATransfer
 from concourse.mybir import AluOpType as OP, ActivationFunctionType as AF
 
 N, V, NB, S0, TH, RO = 8, 896, 1792, 256, 256, 3
-F32, BF, I32, U16 = "float32", "bfloat16", "int32", "uint16"
-SLOT, SENT = 40, 36
+F32, BF, F16, I32, U16 = "float32", "bfloat16", "float16", "int32", "uint16"
+SLOT, SENT = 40, 34
 SEG = 18
 HS = 8 * SEG
 OFF = 34 * 4096
-RHO = 1.8
+RATIO = 0.5546875
 MAGIC = 12582912.0
-TBD = 520
+TBD = 768
 WIDTHS = {
-    I32: dict(obi=16, reci=V, shi=V, bdi=S0, pi=8, lei=16, lli=8, ci=TH, owi=48),
-    U16: dict(le=16, ll=8, ow=48, cu=TH, oru=TH, sl=16, sn=16, rev=16, ox=16, oo=16, osa=16),
-    BF: dict(sh1=V, shb=V + TH, boxw=NB + 2 * TH, v0=TH, drb=8, dg=144, one=128, none=128, em=512, idb=128, nidb=128, bo=128,
-             bom=128, bo8k=128, idbig=128, dw=256, dk=256, ib=384, in23=128, ip22=128, in22=128, ip24=128, i64=128, i05=128,
+    I32: dict(obi=16, reci=V, shi=448, bdi=S0, pi=8, lei=16, lli=8, ci=TH),
+    U16: dict(le=16, ll=8, ow=48, cu=TH, oru=TH, sl=16, ox=16, oo=16, osa=16),
+    BF: dict(sh1=448, shb=V + TH, boxw=NB + 2 * TH, v0=TH, drb=8, dg=144, one=128, none=128, em=512, idb=128, bo=128,
+             bom=128, bo8k=128, idbig=128, dw=256, dk=256, ib=384, in23=128, ip22=128, in13=128, i64=128, i05=128,
              cst=128, kr=128, mh=144, g24=24, hi=432, lo=HS, thb=128, jm=128, dm=128, fc=160, fd=160, kpa=2 * HS,
-             kpb=2 * HS, vt=256, bd=8192, eq=4096, dh=520, dl=520, ha=TH, hn=TH, hta=TH, hw=TH, hm=128, flu=TH, thrn=TH,
-             cb=TH, sr=3 * TH, rn=TH, na=TH, vis=TH, oh=256, ff=2 * HS, yy=TH, ys=TH, vout=TH),
+             kpb=2 * HS, vt=256, vd=256, bd=8192, eq=4096, dh=512, dl=512, ha=TH, hn=TH, hta=TH, hw=TH, hm=128, flu=TH,
+             thrn=TH, cb=TH, sr=3 * TH, rn=TH, na=TH, vis=TH, oh=256, ff=2 * HS, yy=TH, ys=TH, vout=TH),
+    F16: dict(idh=128, es=512),
     F32: dict(rf=V + TH, tb=TBD + TH, drc=16, io=V, pc=16, idf=128, nidf=128, rm=128, vqx=160, hq=HS, e1=160, dmz=HS, fk=HS,
-              p16=256, dmx=128, iw=16, kk=40, ww=24, me=2 * HS, owf=48, xd=512, xa=256, xs=512, sk=16, hv=TH, hr=TH,
-              es=512, t2=256, tt=2 * HS, mm=2 * HS, s2=2 * HS, lq=512, a2=64, mc=TH, ea=TH, yhs=3 * TH),
+              p16=384, dmx=128, iw=16, kk=40, ww=24, me=16, owf=48, xd=512, xa=256, xs=512, sk=16, hv=TH, hr=TH,
+              t2=256, tt=2 * HS, mm=2 * HS, s2=2 * HS, lq=512, a2=64, mc=TH, ea=TH, yhs=3 * TH),
 }
 SCRATCH = {k: ("sbuf", [128, n], d) for d, w in WIDTHS.items() for k, n in w.items()}
-SCRATCH.update({k: ("sbuf", [128, 8, SLOT], BF) for k in ("snd0", "snd1", "rcv0", "rcv1")})
+SCRATCH.update({k: ("sbuf", [128, 8, SLOT], F16) for k in ("snd0", "snd1", "rcv0", "rcv1")})
 SCRATCH["e3"] = ("sbuf", [128, 16, SEG], F32)
 SCRATCH.update({k: ("psum", [128, 512], F32) for k in ("pq0", "pq1", "pz", "pr", "pu0", "pu1", "pn", "py")})
 SEMAPHORES = ["sD", "sA", "sP", "sG", "arr00", "arr01", "arr10", "arr11", "sent", "l_ob", "l_rec", "l_box", "l_tv", "l_dr",
               "l_bd", "l_sh", "o_yr", "o_yv", "o_h0", "o_h1", "o_h2"]
 
-MODES = ["DADADADD", "DADDDADD", "DADDDADD"]
+MODES = ["DADADADD", "AADDADDD", "AADDADDD"]
 BANKS = ["pu0", "pu1", "pr", "pu0", "pu1", "pu0", "pu1", "pu0"]
-HOP, DEAL, ROUNDS, SEED, SHAKE = 230, 2000, 60, 1, 800
-CY, GAT, SCA, PE, DF, AFX, FIRST, DMA, RATE = 0.83, 1.4, 2.8, 0.37, 25, 45, 1200, 1600, 220
+STARTS, SHORT, ROUNDS, SEED, SHAKE, SLACK, SWAPS, STEP = 20, 25, 100, 5, 200, 250, 26000, 150
+TERMS = ("ns", "cy", "gat", "sca", "pe", "dve", "act", "pool", "dma", "byte", "call", "deal", "first", "hop")
+CASES = [(1, 0.83, 1.3, 3.15, 0.42, 25, 45, 100, 1600, 0.0045, 1000, 1900, 1500, 165),
+         (1, 1.08, 2.0, 5.0, 0.54, 25, 45, 0, 1800, 0.005, 700, 2200, 2000, 190),
+         (1, 0.83, 1.1, 2.1, 0.40, 35, 55, 400, 1500, 0.004, 1600, 2500, 2500, 230),
+         (1, 0.83, 1.1, 2.1, 0.42, 20, 40, 0, 1550, 0.004, 700, 1500, 1000, 180)]
+WEIGHTS = (1.2, 0.4, 0.5, 0.4)
 ORDERS = {}
 
 
@@ -53,7 +58,7 @@ def rank_program(g, core, T, topo):
     if rank is None:
         return
     cores = list(T.cores)
-    ops, table = [], []
+    ops = []
     psum = {k for k, s in SCRATCH.items() if s[0] == "psum"}
     own = rank // 4
     halves = (1 - own, own)
@@ -64,12 +69,12 @@ def rank_program(g, core, T, topo):
         hi = n if hi is None else hi
         rows = slice(None) if p is None else slice(p[0], p[1])
         ap = T[name][rows, lo:hi:step] if step != 1 else T[name][rows, lo:hi]
-        return (ap, [(name, lo, hi)], len(range(lo, hi, step)), SCRATCH[name][2] in (BF, U16))
+        return (ap, [(name, lo, hi)], len(range(lo, hi, step)), SCRATCH[name][2] in (BF, F16, U16))
 
     def S3(name, q0, q1, c0=0, c1=SEG):
         w = SCRATCH[name][1][2]
         ap = T[name][:, q0, c0:c1] if q1 == q0 + 1 else T[name][:, q0:q1, c0:c1]
-        return (ap, [(name, q * w + c0, q * w + c1) for q in range(q0, q1)], (q1 - q0) * (c1 - c0), SCRATCH[name][2] == BF)
+        return (ap, [(name, q * w + c0, q * w + c1) for q in range(q0, q1)], (q1 - q0) * (c1 - c0), SCRATCH[name][2] != F32)
 
     def H(name, h, w=128):
         return S(name, w * h, w * h + w)
@@ -92,17 +97,17 @@ def rank_program(g, core, T, topo):
     def keys(*xs):
         return [k for x in xs if isinstance(x, tuple) for k in x[1]]
 
-    def add(eng, fn, rd, wr, cost, sem=None, inc=None, late=0, after=None):
+    def add(eng, fn, rd, wr, cost, sem=None, inc=None, late={}, after=None):
         ops.append({"e": eng, "fn": fn, "rd": rd, "wr": wr, "sem": sem, "inc": inc, "cost": cost, "late": late, "after": after})
 
     def vec(fn, out, ins, k=1.0):
         if out[2] < 0:
-            return add("D", fn, keys(*ins) + out[5][1], out[4][1], 50 - CY * SCA * out[2])
+            return add("D", fn, keys(*ins) + out[5][1], out[4][1], dict(ns=50, sca=-out[2]))
         a = ins[0] if ins else out
         if a[2] < 0:
-            return add("D", fn, keys(*ins), keys(out), 50 + CY * GAT * out[2])
+            return add("D", fn, keys(*ins), keys(out), dict(ns=50, gat=out[2]))
         half = out[3] and all(x[3] for x in ins if isinstance(x, tuple) and x[2] > 1)
-        add("D", fn, keys(*ins), keys(out), DF + CY * max(64, k * out[2] * (0.5 if half else 1.0)))
+        add("D", fn, keys(*ins), keys(out), dict(dve=1, cy=max(64, k * out[2] * (0.5 if half else 1.0))))
 
     def cp(out, in_):
         vec(lambda: g.vector.tensor_copy(out[0], in_[0]), out, [in_])
@@ -124,59 +129,77 @@ def rank_program(g, core, T, topo):
         vec(lambda: g.vector.memset(out[0], c), out, [])
 
     def act(out, a, func=AF.Copy, bias=0.0, scale=1.0):
-        cost = 65 + CY * GAT * out[2] if a[2] < 0 else AFX + CY * max(64, out[2])
-        if not table:
-            table.append(len(ops))
-            cost += 1300
+        cost = dict(ns=65, gat=out[2]) if a[2] < 0 else dict(act=1, cy=max(64, out[2]))
         add("A", lambda: g.scalar.activation(out[0], a[0], func, bias=val(bias), scale=val(scale)), keys(a, bias, scale), keys(out),
-            cost, after=table[0] if table[0] < len(ops) else None)
+            cost)
 
     def mm(out, lhsT, rhs, start=True, stop=True):
         add("P", lambda: g.tensor.matmul(out[0], lhsT[0], rhs[0], start, stop), keys(lhsT, rhs), keys(out),
-            PE * max(min(64, lhsT[2]), rhs[2]) * (1 if lhsT[3] else 4))
+            dict(pe=max(min(64, lhsT[2]), rhs[2]) * (1 if lhsT[3] else 4)))
+
+    def fuse(k):
+        part = ops[-k:]
+        del ops[-k:]
+        add("P", lambda: [o["fn"]() for o in part][-1], [x for o in part for x in o["rd"]], part[0]["wr"],
+            dict(pe=sum(o["cost"]["pe"] for o in part)))
 
     def group(out, terms):
         for j, (lhsT, rhs) in enumerate(terms):
             mm(out, lhsT, rhs, j == 0, j == len(terms) - 1)
 
+    def wrap(out, row, c0, more=()):
+        group(out, [(S("dg", 15 - r, 143 - r), S(row, c0 + r, c0 + 16 * out[2], 16)) for r in range(16)] + list(more))
+        fuse(16 + len(more))
+
     def iota(out, pattern, base, mult=0):
         if SCRATCH[out[1][0][0]][2] == I32:
-            add("G", lambda: g.iota(out[0], pattern, base, mult), [], keys(out), 130 + 2 * CY * out[2])
+            add("G", lambda: g.iota(out[0], pattern, base, mult), [], keys(out), dict(ns=130, cy=2 * out[2]))
         else:
             add("G", lambda: g.iota(out[0], pattern, base, mult, allow_small_or_imprecise_dtypes=True), [], keys(out),
-                130 + 2 * CY * out[2])
+                dict(ns=130, cy=2 * out[2]))
 
     def pick(out, in_, pattern, base, mult=1):
         add("G", lambda: g.affine_select(out[0], in_[0], pattern, OP.is_equal, 0.0, base, mult), keys(in_), keys(out),
-            170 + 2 * CY * out[2])
+            dict(ns=170, cy=2 * out[2], pool=mult == 0))
+
+    def copy(out, in_):
+        pick(out, in_, [[0, out[2]]], 0, 0)
+
+    def diag(out, c):
+        zero = S("hi", 2 * HS, 2 * HS + 128)
+        add("G", lambda: g.affine_select(out[0], zero[0], [[-1, 128]], OP.not_equal, c, 0, 1), keys(zero), keys(out),
+            dict(ns=170, cy=256))
 
     moved = [0]
 
     def dma(q, out, in_, sem, nbytes):
         eng = {"S": g.sync, "A": g.scalar, "G": g}[q]
         moved[0] = moved[0] + nbytes if sem[0] == "l" else nbytes
-        add(q, lambda: eng.dma_start(val(out), val(in_)), keys(in_), keys(out), 60, sem, 16, DMA + moved[0] / RATE)
+        add(q, lambda: eng.dma_start(val(out), val(in_)), keys(in_), keys(out), dict(ns=60), sem, 16,
+            dict(dma=1, byte=moved[0]))
 
     dma("S", S("obi"), T.ob[:], "l_ob", 8192)
-    dma("A", S("shi", p=(0, 8)), T.shp[:], "l_sh", 32 * V)
-    dma("S", S("reci"), T.rec[:], "l_rec", 512 * V)
-    dma("A", S("v0"), T.tv[:], "l_tv", 65536)
-    dma("S", S("boxw", 0, NB), T.box[:], "l_box", 256 * NB)
     dma("A", S("drb", 0, 3), T.dr[:], "l_dr", 4096)
+    dma("A", S("shi", p=(0, 16)), T.shp[:], "l_sh", 32 * V)
+    dma("S", S("v0"), T.tv[:], "l_tv", 65536)
+    dma("S", S("reci"), T.rec[:], "l_rec", 512 * V)
+    dma("S", S("boxw", 0, NB), T.box[:], "l_box", 256 * NB)
     dma("S", S("bdi"), T.bound[:], "l_bd", 512 * S0)
 
-    pc = [col("pc", j) for j in range(14)]
+    pc = [col("pc", j) for j in range(16)]
     QM = S("kk", 32, 40)
     iota(S("pi", 0, 1), [[0, 1]], 0, 1)
     ms(S("one"), 1.0)
+    ms(S("hi", HS, 432), 0.0)
     pick(S("idb"), S("one"), [[-1, 128]], 0)
     iota(S("bo"), [[1, 8], [0, 16]], 0)
+    for h in range(2):
+        pick(H("eq", h), S("one"), [[-2, 8], [0, 16]], -h)
     iota(S("io", 0, 256), [[1, 256]], 0)
     iota(S("iw"), [[16, 16]], 0)
     iota(S("em"), [[1, 32], [0, 16]], 0)
     iota(S("hi", 0, HS), [[-34, 8], [0, SEG]], 239)
     iota(S("lo"), [[0, 8], [1, SEG]], -17)
-    iota(S("fk"), [[0, 8], [1, SEG]], -4097, 16)
     iota(S("fc", 1, HS + 1), [[16, 8], [1, SEG]], -1)
     iota(S("fd", 1, HS + 1), [[16, 8], [1, SEG]], -1)
     iota(S("fc", 0, HS + 1, SEG), [[0, 9]], -5)
@@ -186,112 +209,95 @@ def rank_program(g, core, T, topo):
     iota(S("thb"), [[-34, 8], [0, 16]], 239)
     iota(S("jm"), [[0, 8], [1, 16]], 0)
     iota(S("lli"), [[SEG, 8]], SEG - 1)
-    iota(S("dh", 0, 256), [[-1, 16], [0, 16]], 15)
-    iota(S("dl", 0, 256), [[0, 16], [-1, 16]], 15)
-    for k in ("tb", "dh", "dl"):
-        iota(S(k, 256, 257), [[0, 1]], 0)
-    iota(S("dh", 257, 513), [[1, 16], [0, 16]], 0)
-    iota(S("dl", 257, 513), [[0, 16], [1, 16]], 0)
+    iota(S("dh", 0, 256), [[1, 16], [0, 16]], 0)
+    iota(S("dl", 0, 256), [[0, 16], [1, 16]], 0)
     ts(col("pi", 1), col("pi", 0), 15, OP.bitwise_and)
     ts(col("pi", 2), col("pi", 0), 4, OP.arith_shift_right)
     ts(col("pi", 3), col("pi", 0), 31, OP.bitwise_and)
     cp(S("pc", 0, 4), S("pi", 0, 4))
-    ts(S("bom"), S("bo"), pc[0], OP.is_equal)
     ts(S("bo"), S("bo"), pc[2], OP.is_equal)
     ts(S("em"), S("em"), pc[3], OP.is_equal, -1.0, OP.mult)
-    for j, sc in enumerate((32.0, 2.0 ** 21, 1.0)):
-        ts(H("g24", j, 8), S("io", 0, 8), pc[2], OP.is_equal, sc, OP.mult)
     ts(QM, S("io", 0, 8), pc[2], OP.is_equal)
+    for j, sc in enumerate((32.0, 2.0 ** 21, 1.0)):
+        act(H("g24", j, 8), QM, scale=sc)
     ms(S("dg"), 0.0)
     cp(S("dg", 15, 143, 16), QM)
     ts(S("iw"), S("iw"), pc[1], OP.add)
-    ts(S("rev"), S("iw"), -1.0, OP.mult, 255.0, OP.add)
-    top = 108 * math.log(2.0)
-    for h in range(2):
-        act(col("ww", 16 + h), pc[0], AF.Exp, bias=top - 128 * h * math.log(RHO), scale=-math.log(RHO))
-    act(S("ww", 0, 16), S("iw"), AF.Exp, bias=top, scale=-math.log(RHO))
-    act(S("thrn"), S("io", 0, 256), AF.Exp, bias=top + math.log(2.5), scale=-math.log(RHO))
-    ts(S("thrn"), S("thrn"), -1.0, OP.mult)
-    act(S("ww", 18, 20), S("ww", 16, 18), scale=-5.0)
-    ts(S("sh1", p=(0, 8)), S("shi", p=(0, 8)), 1.0, OP.add)
+    ms(S("cb"), RATIO)
+    scan(S("thrn"), S("cb"), S("hi", 2 * HS - 112, 3 * HS), -2.0 ** 94, OP.mult, OP.min)
+    wrap(S("pn", 0, 16), "thrn", 0)
+    for h in halves:
+        mm(S("pn", 16 + h, 17 + h), H("thrn", h), S("one", 0, 1))
+    act(S("ww", 0, 16), S("pn", 0, 16), scale=-8 / 2.5)
+    act(S("ww", 16, 18), S("pn", 16, 18), scale=-1 / 2.5)
+    act(S("ww", 18, 20), S("pn", 16, 18), scale=2.0)
+    ts(S("sh1", p=(0, 16)), S("shi", p=(0, 16)), -1.0, OP.mult, 256.0, OP.add)
     for h, bank in enumerate(("py", "pz")):
-        mm(S(bank, 0, 448), S("bom", p=(0, 8)), S("sh1", 448 * h, 448 * h + 448, p=(0, 8)))
+        mm(S(bank, 0, 448), S("eq", 128 * h, 128 * h + 128, p=(0, 16)), S("sh1", p=(0, 16)))
         act(H("shb", h, 448), S(bank, 0, 448))
     act(pc[4], pc[2], AF.Identity, bias=7.0 * OFF, scale=-float(OFF))
-    act(pc[5], pc[0], AF.Identity, bias=-2040.0, scale=16.0)
+    act(pc[5], pc[0], AF.Identity, bias=-2040.0 - 2.0 ** 22, scale=16.0)
     act(pc[11], pc[0], AF.Identity, bias=-4096.0, scale=16.0)
-    ms(S("hi", HS, 432), 0.0)
-    ts(S("hi", 0, HS), S("hi", 0, HS), 4096.0, OP.mult)
-    tt(S("fk"), S("fk"), S("hi", 0, HS), OP.add)
-    ts(S("fk", SEG - 1, HS, SEG), S("fk", SEG - 1, HS, SEG), 2039.0, OP.add)
-    ms(S("fk", 0, HS, SEG), 2.0 ** 22)
+    act(pc[14], pc[0], AF.Identity, bias=-4080.0, scale=16.0)
+    act(S("hi", 0, HS), S("hi", 0, HS), scale=4096.0)
     ms(S("hi", 0, HS, SEG), 2.0 ** 22)
+    group(S("pn", 0, HS), [(S("idb"), S("hi", 0, HS)), (S("idb"), S("lo"))])
+    act(S("fk"), S("pn", 0, HS), AF.Identity, bias=pc[14])
+    ts(S("fk", SEG - 1, HS, SEG), S("fk", SEG - 1, HS, SEG), 2039.0, OP.add)
     ms(S("hi", HS + SEG - 1, 2 * HS, SEG), 2.0 ** 21)
     ms(S("lo", SEG - 1, HS, SEG), 2.0 ** 22)
     act(S("thb"), S("thb"), scale=4096.0)
     ts(S("dm"), S("jm"), pc[1], OP.is_equal)
-    act(S("dmx"), S("thb"), AF.Identity, bias=pc[5])
-    tt(S("dmx"), S("dmx"), S("dm"), OP.mult)
     ts(S("vqx", 0, HS + 1), S("fc", 0, HS + 1), pc[0], OP.is_equal, -2.0 ** 21, OP.mult)
     ts(S("e1", 1, HS + 2), S("fd", 1, HS + 2), pc[0], OP.is_equal, 2.0 ** -12, OP.mult)
     tt(S("dmz"), S("e1", 1, HS + 1), S("e1", 2, HS + 2), OP.subtract)
     ts(W("a2", 0), S("iw"), -8.5, OP.add, 1.0 / SEG, OP.mult)
     cp(S("lei"), W("a2", 0))
-    ts(S("le"), S("lei"), float(SEG), OP.mult, SEG - 1.0, OP.add)
+    cp(S("le"), S("lei"))
     cp(S("ll"), S("lli"))
     act(H("kk", 0, 16), S("iw"), AF.Identity, bias=V / 16.0, scale=1 / 16.0)
     act(H("kk", 1, 16), S("iw"), AF.Identity, bias=-14 - TBD / 4096.0, scale=-1 / 4096.0)
-    act(S("drc", 0, 1), S("drb", 0, 1), scale=-1.0)
+    act(S("drc", 12, 15), S("drb", 0, 3), scale=-1.0)
     act(S("drc", 1, 3), S("drb", 1, 3), AF.Identity, bias=128.0, scale=-1.0)
     act(S("drc", 4, 6), S("drb", 0, 2), AF.Identity, bias=-2.0, scale=1 / 128.0)
     act(S("drc", 6, 7), S("drb", 2, 3), AF.Identity, bias=-256.0)
     act(S("drc", 8, 10), S("drb", 0, 2), AF.Identity, bias=-255.5)
     act(S("drc", 10, 11), S("drb", 2, 3), AF.Identity, bias=256.0, scale=-1.0)
-    cp(S("tb", 0, S0), IND(S("bdi"), S("rev")))
-    for a, b in ((0, 256), (256, 513)):
-        ts(S("dh", a, b), S("dh", a, b), pc[1], OP.is_equal)
-        ts(S("dl", a, b), S("dl", a, b), pc[1], OP.not_equal)
-    act(S("idf"), S("idb"))
     for a in range(256, V, 256):
         act(S("io", a, min(V, a + 256)), S("io", 0, min(V - a, 256)), AF.Identity, bias=float(a))
-    for k, sc in (("nidf", -1.0), ("nidb", -1.0), ("ip24", 2.0 ** 24), ("i64", 64.0), ("i05", 0.5), ("in23", -2.0 ** 23),
-                  ("ip22", 2.0 ** 22), ("in22", -2.0 ** 22)):
-        act(S(k), S("idb"), scale=sc)
-    for t in range(RO):
-        act(H("ib", t), S("idb"), scale=float(NB + TH * t))
-    act(H("dk", 0), S("idb"), scale=pc[0])
-    act(pc[13], pc[0], AF.Identity, bias=128.0)
-    act(H("dk", 1), S("idb"), scale=pc[13])
+    cp(S("tb", 0, S0), S("bdi"))
+    ts(S("dh", 0, 256), S("dh", 0, 256), pc[1], OP.is_equal)
+    ts(S("dl", 0, 256), S("dl", 0, 256), pc[1], OP.not_equal)
+    for k, sc in (("ip22", 2.0 ** 22), ("nidf", -1.0), ("i64", 64.0), ("i05", 0.5), ("idf", 1.0), ("idh", 1.0)):
+        diag(S(k), sc)
+    diag(H("ib", 0), float(NB))
+    group(S("pn", 0, 128), [(S("idb"), S("thb")), (S("ip22"), S("dm"))])
+    act(S("dmx"), S("pn", 0, 128), AF.Relu, bias=pc[5])
+    act(S("pc", 12, 14), S("io", 0, 129, 128), AF.Identity, bias=pc[0])
+    for h in halves:
+        act(H("dk", h), S("idb"), scale=pc[12 + h])
     ts(S("idbig"), S("idb"), 2.0 ** 99, OP.mult, 2.0 ** 13, OP.mult)
     act(S("bo8k"), S("bo"), scale=8192.0)
     act(S("bom"), S("bo"), AF.Identity, bias=-1.0)
-    ms(S("mh", 0, 128), -0.5)
-    ms(S("mh", 128, 136), -0.3125)
-    ms(S("none"), -1.0)
-    ms(S("cst"), 2.0 ** 20 - 7 * 4096.0)
-    for h in range(2):
+    act(S("mh", 0, 128), S("one"), scale=-0.5)
+    act(S("mh", 128, 136), S("one", 0, 8), scale=-0.3125)
+    act(S("none"), S("one"), scale=-1.0)
+    act(S("cst"), S("one"), scale=-53 * 512.0)
+    for h in halves:
         act(H("dw", h), S("idb"), scale=col("ww", 18 + h))
     ts(pc[6], pc[1], 0.0, OP.is_equal, -2.0 ** 21, OP.mult)
     ts(pc[8], pc[1], 15.0, OP.is_equal, 2.0 ** 21, OP.mult)
     act(pc[7], pc[6], AF.Identity, bias=-2.0 ** 32, scale=2.0 ** 11)
     act(pc[9], pc[8], AF.Identity, bias=-2.0 ** 20, scale=0.5)
-    act(pc[12], pc[8], AF.Identity, bias=-0.5, scale=-1019.5 * 2.0 ** -21)
+    act(pc[15], pc[8], AF.Identity, bias=-0.5, scale=-1019.5 * 2.0 ** -21)
     ts(pc[10], pc[6], -2.0 ** -17, OP.mult, pc[0], OP.add)
-    act(S("kr"), S("idb"), scale=pc[12])
+    act(S("kr"), S("idb"), scale=pc[15])
     for j in range(2):
         ts(H("kpa", j, HS), S("fc", 1, HS + 1), pc[0], OP.is_equal, pc[6 + j], OP.mult)
         ts(H("kpb", j, HS), S("fc", 0, HS), pc[0], OP.is_equal, pc[8 + j], OP.mult)
+    tt(S("kpa"), S("kpa"), S("kpb"), OP.add)
     tt(S("hq"), S("vqx", 0, HS), S("vqx", 1, HS + 1), OP.subtract)
     ts(S("rm"), S("io", 1, 129), pc[10], OP.is_equal)
-
-    def vhalf(t, h):
-        return H("v0", h) if t == 0 else S3("rcv%d" % (t - 1), 4 * h, 4 * h + 4, 0, 32)
-
-    def vblock(t, u):
-        return H("v0", u, 32) if t == 0 else S3("rcv%d" % (t - 1), u, u + 1, 0, 32)
-
-    def wrap(out, row, c0, more=()):
-        group(out, [(S("dg", 15 - r, 143 - r), S(row, c0 + r, c0 + 16 * out[2], 16)) for r in range(16)] + list(more))
 
     def place(h, what):
         first = dict(dif=("pr", 0), box=("pz", 440), ref=("pr", 152), new=("pr", 160), one=("py", 0), turn=("py", 0))
@@ -302,22 +308,24 @@ def rank_program(g, core, T, topo):
 
     def pre(t, h):
         if t == 0:
+            v = H("v0", h)
             cp(WH("ow", 0, h), H("obi", h, 8))
             ts(H("ci", h), IND(S("reci"), WH("ow", 0, h)), 4095, OP.bitwise_and)
         else:
             r = "rcv%d" % (t - 1)
-            tt(WH("owi", t, h), S3(r, 4 * h, 4 * h + 4, 32, 34), S3(r, 4 * h, 4 * h + 4, 34, 36), OP.add)
-            cp(WH("ow", t, h), WH("owi", t, h))
-            cp(H("ci", h), IND(S("rf", 0, V), WH("ow", t, h)))
+            v = S3(r, 4 * h, 4 * h + 4, 0, 32)
+            cp(WH("ow", t, h), S3(r, 4 * h, 4 * h + 4, 32, 34))
+        act(H("xd", 2 * h), IND(S("rf", 0, V), WH("ow", t, h)))
+        if t:
+            cp(H("ci", h), H("xd", 2 * h) if h == own else IND(S("rf", 0, V), WH("ow", t, h)))
             ts(H("ci", h), H("ci", h), 4095, OP.bitwise_and)
         cp(H("cu", h), H("ci", h))
-        act(H("xd", 2 * h), IND(S("rf", 0, V), WH("ow", t, h)))
-        for k in range(4):
-            mm(S("pz", 128 * h, 128 * h + 128, p=(32 * k, 32 * k + 32)), vblock(t, 4 * h + k), S("idb"))
         if t:
-            act(H("vt", h), H("pz", h), AF.Identity, bias=128.0, scale=128.0)
+            ts(H("vd", h), v, 128.0, OP.mult, col("drc", t), OP.add)
         else:
-            act(H("vt", h), H("pz", h))
+            act(H("vd", h), v, AF.Identity, bias=col("drc", 12))
+        mm(H("pz", h), H("vd" if t else "v0", h), S("idb"))
+        act(H("vt", h), H("pz", h))
 
     def chunk(t, h, k, j):
         src = IND(S("boxw", 0, NB + TH * t), H("cu", 4 * h + k, 32))
@@ -327,69 +335,69 @@ def rank_program(g, core, T, topo):
         else:
             act(dst, src)
         rows = (32 * k, 32 * k + 32)
-        group(S(BANKS[j]), [(S("idb"), dst), (S("vt", 128 * h, 128 * h + 128, p=rows), S("em", p=rows))])
-        act(H("bd", 8 * h + 4 + k, 512), S(BANKS[j]), AF.Abs)
+        group(S(BANKS[j]), [(S("vt", 128 * h, 128 * h + 128, p=rows), S("em", p=rows)), (S("idb"), dst)])
+        act(H("bd", 8 * h + 4 + k, 512), S(BANKS[j]), AF.Abs, bias=col("drc", 12 + t) if t else 0.0)
 
     def red(t, h):
         q, o, n = "pq%d" % h, 4096 * h + 2048, 17 if t else 16
         for u in range(n):
             mm(S(q, 1 + u, 432, SEG), S("bd", o + u % 16, o + 2048, 16), S("g24"), False, u == n - 1)
+        fuse(n)
+        put = cp if h == own else copy
         if t:
-            cp(S("bd", o + 7, o + 2048, 16), S("bd", o - 2048, o, 16))
-        act(S("bd", o + 8, o + 2048, 16), vhalf(t, h), AF.Identity, bias=col("drc", t), scale=128.0 if t else 1.0)
+            put(S("bd", o + 7, o + 2048, 16), S("bd", o - 2048, o, 16))
+        put(S("bd", o + 8, o + 2048, 16), H("vd", h))
 
-    def shapes(t, h):
-        P = H("pr", 60 + h, 8) if t == 0 or h != own else S("pz", 416, 424)
-        act(H("sr", 2 * t + h), IND(S("shb", 0, V), WH("ow", t, h)))
-        wrap(P, "sr", TH * t + 128 * h)
-        ts(H("sl", h, 8), P, -1 / 16.0, OP.mult, 256.0, OP.add)
-        if t == 2:
-            ts(H("sn", h, 8), P, 1 / 16.0, OP.mult)
-        entry = IND(S("tb", 0, 256 if t < 2 else 513), H("sl", h, 8))
-        act(H("hv", h), entry)
+    def shapes(t, h, n):
+        P = S("pr", 480 + 8 * h, 480 + 8 * (h + n)) if n == 2 or h != own else S("pz", 416, 424)
+        a, b = 128 * h, 128 * (h + n)
+        act(S("sr", TH * t + a, TH * t + b), IND(S("shb", 0, V), W("ow", t, a // 16, b // 16)))
+        wrap(P, "sr", TH * t + a)
+        ts(S("sl", a // 16, b // 16), P, -1 / 16.0, OP.mult, 256.0, OP.add)
+        if t == 0:
+            act(S("sk"), P, AF.Identity, bias=-1 / 16.0, scale=2.0 ** -16)
+        entry = IND(S("tb", 0, 256 if t < 2 else 512), S("sl", a // 16, b // 16))
+        act(S("hv", a, b), entry)
         if t:
-            act(H("hr", h), entry, AF.Relu, bias=-4096.0)
-            act(H("rn", h), entry, AF.Sign, bias=4090.0, scale=-1.0)
+            act(S("hr", a, b), entry, AF.Relu, bias=-4096.0)
+            act(S("rn", a, b), entry, AF.Sign, bias=4090.0, scale=-1.0)
 
-    def keys_init(t, h):
+    def bounds(t, h):
         q = "pq%d" % h
         mm(S(q, 0, 432), S("idb"), S("hi"), True, False)
         mm(H(q, 0, HS), S("idb"), S("lo"), False, False)
         if t:
-            for k in ("kpa", "kpb"):
-                mm(S(q, 0, 2 * HS), S("none"), S(k), False, False)
-
-    def bounds(t, h):
-        q = "pq%d" % h
+            mm(S(q, 0, 2 * HS), S("none"), S("kpa"), False, False)
         mm(H(q, 1, HS), H("hv", h), S("vqx", 1, HS + 1), False, False)
         if t:
             mm(H(q, 1, HS), H("hr", h), S("hq"), False, False)
-            for k in ("kpa", "kpb"):
-                mm(S(q, 0, 2 * HS), H("rn", h), S(k), False, False)
+            mm(S(q, 0, 2 * HS), H("rn", h), S("kpa"), False, False)
 
     def seen(t, h):
         cp(H("xd", 2 * h + 1), H("ci", h))
         if t:
             bank = place(h, "turn")[1][0][0]
+            group(H(bank, 0), [(S("ip22"), S("none")), (S("ip22"), H("rn", h))])
             for j in range(2):
-                mm(H(bank, j), S("ip22"), H("rn", h), j == 0, False)
-            mm(H(bank, 0, 256), S("idf"), H("xd", h, 256), False, True)
-            act(S("xa"), H(bank, 0, 256), AF.Identity, bias=-2.0 ** 22)
+                tt(H("xa", j), H(bank, 0), H("xd", 2 * h + j), OP.add)
             for j in range(2):
                 mm(H(bank, 2 + j), S("in23"), H("rn", h), j == 0, False)
             mm(H(bank, 1, 256), S("rm"), S("xa"), False, True)
             tt(H("xs", h, 256), H(bank, 1, 256), S("xa"), OP.max)
 
     def fields(t, h):
-        if t or h == halves[0]:
-            P = S("pz", 288, 416)
-            group(P, [(S("idb"), S("thb")), (S("idb"), S("jm"))] + [(S("none"), S("kr")), (H("rn", h), S("kr"))] * (t > 0))
-            act(H("p16", h), P, AF.Identity, bias=pc[11])
+        P = S("pz", 288, 416)
+        if t:
+            mm(P, H("rn", h), S("kr"))
+            tt(H("p16", h), P, H("p16", 2), OP.add)
+        else:
+            group(P, [(S("idb"), S("thb")), (S("idb"), S("jm"))] + [(S("none"), S("kr"))] * (h == own))
+            act(H("p16", 2 if h == own else h), P, AF.Identity, bias=pc[11])
 
     def objects(t):
-        cp(W("owf", t), S("obi") if t == 0 else W("owi", t))
+        cp(W("owf", t), W("ow", t))
         cp(S("oru"), IND(S("io"), W("ow", t)))
-        mm(S("pn", 0, 256), S("idb"), S("thrn"), True, False)
+        mm(S("pn", 0, 256), S("one"), S("thrn"), True, False)
         for q in range(16):
             e = S("eq", 272 * q, 256 * q + 256)
             ts(e, S("oru", 16 * q, TH), W("owf", t, q, q + 1), OP.is_equal, col("ww", q), OP.mult)
@@ -401,17 +409,15 @@ def rank_program(g, core, T, topo):
         cp(S("oo"), W("a2", 1))
 
     def digits(t):
-        n = 256 if t < 2 else 513
-        if t == 0:
-            act(S("sk"), S("pr", 480, 496), AF.Identity, bias=-1 / 16.0, scale=2.0 ** -16)
+        n = 256 if t < 2 else 512
         if t == 2:
-            act(S("na"), IND(S("tb", 256, 513), S("sn")), AF.Sign, bias=-4090.0)
+            act(S("na"), IND(S("tb", 256, 768), S("sl")), AF.Sign, bias=-4090.0)
         act(S("ha"), IND(S("dh", 0, n), S("sl")))
         act(S("hn"), IND(S("dl", 0, n), S("sl")))
-        for h in range(2):
+        for h in halves:
             mm(H("py", h), H("ha", h), S("idb"))
-            group(H("py", 2 + h), [(S("idb"), S("thb")), (H("hn", h), S("ip24"))] + [(H("na", h), S("bo8k"))] * (t == 2))
-        for h in range(2):
+            group(H("py", 2 + h), [(S("idb"), S("thb")), (H("hn", h), S("ip22"))] + [(H("na", h), S("bo8k"))] * (t == 2))
+        for h in halves:
             act(H("hta", h), H("py", h), scale=col("ww", 16 + h))
         act(S("t2"), S("py", 256, 512), AF.Identity, bias=-8.0 + (2.0 ** 17 if t == 2 else 0.0))
 
@@ -420,13 +426,12 @@ def rank_program(g, core, T, topo):
         if t < 2:
             mm(place(h, "dif"), H("xd", 2 * h), S("dmz"))
         tt(H("tt", h, HS), H(q, 1, HS), S("fk"), OP.max)
-        for out in (M, H("me", h, HS))[:1 + (t < 2)]:
-            scan(out, H("tt", h, HS), H(q, 0, HS), 2.0 ** 23, OP.min, OP.min)
+        scan(M, H("tt", h, HS), H(q, 0, HS), 2.0 ** 23, OP.min, OP.min)
         tt(H("lq", h), IND(M, S("ll")), S("dmx"), OP.min)
         P = place(h, "box")
         mm(P, H("lq", h), QM)
         ts(H("ox", h, 8), P, pc[4], OP.subtract)
-        act(S3("e3", 8 * h, 8 * h + 8), H(q, 2, HS))
+        act(S3("e3", 8 * h, 8 * h + 8), H(q, 2, HS), AF.Identity, bias=-2048.0)
         X = IND(H("bd", h, 4096), H("ox", h, 8))
         act(H("yy", h), X, AF.Identity, bias=col("drc", 4 + t), scale=1 / 128.0 if t < 2 else 1.0)
         if t == 2:
@@ -434,14 +439,14 @@ def rank_program(g, core, T, topo):
             tt(H("vout", h), H("yy", h), H("ys", h), OP.add)
             return
         act(H("ys", h), X, AF.Sign, bias=col("drc", 8 + t))
-        tt(H("ff", h, HS), IND(H("me", h, HS), S("le", 0, 9)), M, OP.is_equal)
+        cp(H("me", h, 8), S("mm", HS * h + SEG - 1, HS * h + HS, SEG))
+        tt(H("ff", h, HS), IND(H("me", h, 8), S("le", 0, 9)), M, OP.is_equal)
         scan(H("s2", h, HS), place(h, "dif"), H("ff", h, HS), 0.0, OP.add, OP.mult)
         tt(H("lq", 2 + h), IND(H("s2", h, HS), S("ll")), S("dm"), OP.mult)
         P = place(h, "ref")
         group(P, [(S("idb"), S("mh", 128, 136)), (H("lq", 2 + h), QM)])
         s = "snd%d" % t
-        cp(S3(s, 4 * h, 4 * h + 4, 32, 34), P)
-        tt(S3(s, 4 * h, 4 * h + 4, 34, 36), P, S3(s, 4 * h, 4 * h + 4, 32, 34), OP.subtract)
+        ts(S3(s, 4 * h, 4 * h + 4, 32, 34), P, MAGIC, OP.add, MAGIC, OP.subtract)
         tt(S3(s, 4 * h, 4 * h + 4, 0, 32), H("yy", h), H("ys", h), OP.subtract)
 
     def send(t, h):
@@ -457,12 +462,12 @@ def rank_program(g, core, T, topo):
             trs.append(RemoteDMATransfer(dst_ids=[DstId(rid=rid, pnc=pid)], dma_engine_mask=sum(1 << e for e in es),
                                          remote_sem=T.sem[sem], src=T[s][:, cores.index(d), 0:SENT], dst=T[r][:, rank, 0:SENT]))
         add("G", lambda: g.remote_dma_fused(trs, local_sem=T.sem.sent), keys(S3(s, 4 * h, 4 * h + 4, 0, SENT)), [],
-            800 + FIRST * (t + late == 0), "sent", -sum(len(m) for m in mk.values()))
+            dict(call=1, first=t + late == 0), "sent", -sum(len(m) for m in mk.values()))
         srcs = [q for q in range(4 * h, 4 * h + 4) if q != rank]
         n = sum(len(plan(cores[q], own)[core]) for q in srcs)
-        add("X", None, [], [(r, q * SLOT, q * SLOT + SLOT) for q in srcs], 0, sem, -n, DEAL, len(ops) - 1)
+        add("X", None, [], [(r, q * SLOT, q * SLOT + SLOT) for q in srcs], {}, sem, -n, dict(deal=1), len(ops) - 1)
         if late:
-            act(S3(r, rank, rank + 1, 0, SENT), S3(s, rank, rank + 1, 0, SENT))
+            cp(S3(r, rank, rank + 1, 0, SENT), S3(s, rank, rank + 1, 0, SENT))
 
     def record(t, h):
         x = "xs" if t else "xd"
@@ -472,42 +477,44 @@ def rank_program(g, core, T, topo):
         tt(IND(S("rf"), H("oo", h, 8)), H(x, 2 * h), H("mc", h), OP.add)
 
     def newbox(t, h):
-        P, o = place(h, "new"), 4096 * h + 2056
-        group(P, [(S("i05"), S("mh", 0, 128)), (S("i05"), S("bd", o, o + 2040, 16)), (S("i64"), H("yy", h))])
-        ts(H("boxw", 14 + 2 * t + h), P, MAGIC + 128, OP.add, MAGIC, OP.subtract)
+        P = place(h, "new")
+        group(P, [(S("i05"), S("mh", 0, 128)), (S("i05"), H("vd", h)), (S("i64"), H("yy", h))])
+        act(H("lq", h), P, AF.Identity, bias=MAGIC + 128)
+        act(H("boxw", 14 + 2 * t + h), H("lq", h), AF.Identity, bias=-MAGIC)
 
     def askers(t, h):
         tt(H("hw", h), IND(H("mm", h, HS), S("ll")), H("t2", h), OP.is_ge)
         for j in range(1 + (t > 0)):
-            if h == own and j == 0:
-                act(H("es", 2 * j + h), S3("e3", 8 * h, 8 * h + 8, 1 + j, 17 + j))
+            part = (H("es", 2 * j + h), S3("e3", 8 * h, 8 * h + 8, 1 + j, 17 + j))
+            if h == own and j == 0 and t == 2:
+                cp(*part)
             else:
-                pick(H("es", 2 * j + h), S3("e3", 8 * h, 8 * h + 8, 1 + j, 17 + j), [[0, 128]], 0, 0)
+                copy(*part)
 
     def makers(t):
         group(H("pn", 0), [(S("idbig"), S("bom"))] + [(H("hta", h), H("hw", h)) for h in halves])
         act(S("hm"), H("pn", 0), AF.Relu)
         P = S("pn", 256, 512)
         mm(P, S("idbig"), S("hn"), True, False)
-        for h in range(2):
+        for h in halves:
             mm(H("pn", 2 + h), H("hw", h), H("dw", h), False, False)
-        mm(P, S("nidb"), S("thrn"), False, False)
+        mm(P, S("none"), S("thrn"), False, False)
         mm(P, S("hm"), S("ha"), False, True)
         act(S("flu"), P, AF.Sign, scale=-1.0)
         for j in range(1 + (t > 0)):
             q = "pq%d" % ((own + j) % 2)
-            for h in range(2):
-                mm(H(q, h), H("es", 2 * j + h), S("idf"), h == 0, False)
+            for h in halves:
+                mm(H(q, h), H("es", 2 * j + h), S("idh"), h != own, False)
             if t:
-                mm(S(q, 0, 256), S(("ip22", "in22")[j]), S("rn"), False, False)
+                mm(S(q, 0, 256), S(("ip22", "in13")[j]), S("rn"), False, False)
             if j:
                 mm(S(q, 0, 256), S("cst"), S("em", 0, 256), False, False)
             mm(S(q, 0, 256), S("bo8k"), S("flu"), False, True)
         if t:
-            act(S("ea"), S("pq%d" % own, 0, 256), AF.Relu, bias=14 * 8192.0 - 2.0 ** 22)
+            act(S("ea"), S("pq%d" % own, 0, 256), AF.Relu, bias=14 * 8192.0 + 2048 - 2.0 ** 22)
             tt(H("yhs", t, TH), S("pq%d" % (1 - own), 0, 256), S("ea"), OP.max)
         else:
-            act(H("yhs", t, TH), S(q, 0, 256), AF.Relu, bias=14 * 8192.0)
+            act(H("yhs", t, TH), S(q, 0, 256), AF.Relu, bias=14 * 8192.0 + 2048)
         dma("S", T.yh[:, TH * t:TH * t + TH], H("yhs", t, TH), "o_h%d" % t, 512 * TH)
         if t == 2:
             return
@@ -517,17 +524,22 @@ def rank_program(g, core, T, topo):
         ts(S("osa"), W("a2", 3), -4096.0, OP.mult, -14 * 4096.0, OP.add)
         ts(IND(S("tb"), S("osa")), H("yhs", t, TH), 1.0, OP.mult, 4097.0, OP.add)
         if t == 0:
-            act(S("tb", 257, 513), IND(S("tb", 0, 256), S("rev")), AF.Relu, bias=-4097.0)
+            act(S("tb", 256, 512), S("tb", 0, 256), AF.Relu, bias=-4097.0)
+            iota(S("tb", 512, 768), [[0, 256]], 0)
+            for k in ("dh", "dl"):
+                copy(S(k, 256, 512), S(k, 0, 256))
 
     cp(S("rf", 0, V), S("reci"))
     for t in range(RO):
         for h in halves:
             pre(t, h)
-            shapes(t, h)
-            keys_init(t, h)
+            if t:
+                shapes(t, h, 1)
+        if t == 0:
+            shapes(t, 0, 2)
+        for h in halves:
             bounds(t, h)
         seen(t, halves[0])
-        digits(t)
         objects(t)
         for j, h in enumerate(halves):
             for k in range(4):
@@ -535,7 +547,8 @@ def rank_program(g, core, T, topo):
             red(t, h)
             fields(t, h)
         if t == 1:
-            tt(S("vis"), H("sr", 1, TH), S("rn"), OP.mult)
+            group(S("pz", 0, 256), [(S("idb"), H("sr", 1, TH)), (S("i64"), S("rn")), (S("i64"), S("rn"))])
+            act(S("vis"), S("pz", 0, 256), AF.Identity, bias=-128.0)
             wrap(S("pz", 424, 440), "vis", 0)
             act(S("sk"), S("pz", 424, 440), AF.Identity, bias=-1 / 16.0, scale=2.0 ** -16)
             cp(IND(S("shb"), S("oo")), S("vis"))
@@ -544,21 +557,50 @@ def rank_program(g, core, T, topo):
             if h != own:
                 seen(t, own)
             record(t, h)
+            if h != own:
+                digits(t)
+            askers(t, h)
             if t < 2:
                 send(t, h)
                 newbox(t, h)
-            askers(t, h)
         if t == 2:
             dma("S", T.yr[:], S("rf", 0, V), "o_yr", 512 * V)
             dma("S", T.yv[:], S("vout"), "o_yv", 65536)
+        for h in range(2 * (t == 0)):
+            diag(S(("in13", "in23")[h]), -2.0 ** (13 + 10 * h))
+            diag(H("ib", 1 + h), float(NB + TH * (1 + h)))
         makers(t)
 
-    emit(g, T, order(ops, psum, own))
+    emit(g, T, order(ops, psum))
 
 
 def schedule(ops):
     n = len(ops)
-    lag = [{j: (HOP + ops[j]["late"] if j in o["deps"] else 0) for j in o["pred"]} for o in ops]
+    cases = []
+    for case in CASES:
+        ns = dict(zip(TERMS, case))
+        cost, late = ([sum(ns[k] * x for k, x in o[key].items()) for o in ops] for key in ("cost", "late"))
+        cases.append((cost, late, [[(j, ns["hop"] + late[j] if j in o["deps"] else 0) for j in o["pred"]] for o in ops]))
+    cost, late, lag = cases[0][0], cases[0][1], [dict(x) for x in cases[0][2]]
+
+    eng = [o["e"] for o in ops]
+    outs = [i for i, o in enumerate(ops) if o["sem"] and o["sem"][0] == "o"]
+
+    def judge(line, at=0, known=None):
+        span, ends = 0.0, []
+        for c, (cost, late, need) in enumerate(cases):
+            end = list(known[c]) if at else [0.0] * n
+            free = {eng[i]: end[i] for i in line[:at]}
+            for i in line[at:]:
+                s = free.get(eng[i], 0.0)
+                for j, x in need[i]:
+                    if end[j] + x > s:
+                        s = end[j] + x
+                end[i] = free[eng[i]] = s + cost[i]
+            span += WEIGHTS[c] * max(end[i] + late[i] for i in outs)
+            ends.append(end)
+        return span / sum(WEIGHTS), ends
+
     back = [{} for _ in ops]
     for i in range(n):
         for j, x in lag[i].items():
@@ -572,7 +614,7 @@ def schedule(ops):
         while pool:
             i = pool.pop()[1]
             row = busy.setdefault(ops[i]["e"], [])
-            s, c, at = ready[i], ops[i]["cost"], 0
+            s, c, at = ready[i], cost[i], 0
             for a, b in row:
                 if a >= s + c:
                     break
@@ -588,47 +630,95 @@ def schedule(ops):
             pool.sort()
         return end
 
-    late = [o["late"] for o in ops]
-    end = [float(i) for i in range(n)]
     seed = SEED
-    best = None
-    for _ in range(ROUNDS):
+    best = now = None
+    for turn in range(STARTS * SHORT + ROUNDS):
+        if turn <= STARTS * SHORT and turn % SHORT == 0:
+            now = best[2] if turn == STARTS * SHORT else None
+            end = now[1] if now else [float(i) for i in range(n)]
         shake = []
         for x in end:
             seed = (seed * 1103515245 + 12345) % 2147483648
-            shake.append(-x - SHAKE * seed / 2147483648)
+            shake.append(-x - SHAKE * (1 + turn % 4) * seed / 2147483648)
         rev = place(back, lag, shake, late)
         end = place(lag, back, [-x for x in rev], [0.0] * n)
-        span = max(e + x for e, x in zip(end, late))
+        line = sorted(range(n), key=lambda i: (end[i] - cost[i], end[i], i))
+        span = judge(line)[0]
         if best is None or span < best[0]:
-            best = (span, sorted(range(n), key=lambda i: (end[i] - ops[i]["cost"], end[i], i)), end)
-        end = best[2]
+            best = (span, line, (span, end))
+        if now is None or span < now[0] + SLACK * (1 - turn / (STARTS * SHORT + ROUNDS)):
+            now = (span, end)
+        end = now[1]
+
+    def neighbours(line, end, cost, late, need):
+        prev, last = [-1] * n, {}
+        for i in line:
+            prev[i] = last.get(eng[i], -1)
+            last[eng[i]] = i
+        i, arcs = max(outs, key=lambda k: end[k] + late[k]), []
+        while i >= 0:
+            ways = [(end[j] + x, j) for j, x in need[i]] + [(end[prev[i]] if prev[i] >= 0 else -1.0, prev[i])]
+            j = max(ways)[1]
+            if j == prev[i] >= 0 and j not in lag[i]:
+                arcs.append((j, i))
+            i = j
+        return arcs
+
+    line = best[1]
+    now, ends = judge(line)
+    for turn in range(SWAPS):
+        seed = (seed * 1103515245 + 12345) % 2147483648
+        if turn % 8 == 0:
+            c = turn // 8 % len(cases)
+            arcs = neighbours(line, ends[c], *cases[c])
+        u, v = arcs[(seed >> 8) % len(arcs)]
+        a, b = line.index(u), line.index(v)
+        ahead, wanted, queues = [v], set(lag[v]), {eng[v]}
+        for i in line[b - 1:a:-1]:
+            if i in wanted or eng[i] in queues:
+                ahead.append(i)
+                wanted.update(lag[i])
+                queues.add(eng[i])
+        if a > b or u in wanted:
+            continue
+        moved = set(ahead)
+        trial = line[:a] + ahead[::-1] + [i for i in line[a:b] if i not in moved] + line[b + 1:]
+        span, new = judge(trial, a, ends)
+        if span <= now + STEP * (1 - turn / SWAPS):
+            now, line, ends = span, trial, new
+            if now < best[0]:
+                best = (now, line)
     return best[1]
 
 
-def order(ops, psum, kind):
-    seen = {}
+def order(ops, psum):
+    seen, runs = {}, {}
     for i, o in enumerate(ops):
         deps, soft = set(), set()
         for mode, ks in (("r", o["rd"]), ("w", o["wr"])):
             for name, lo, hi in ks:
+                if name in psum:
+                    run, before = runs.setdefault(name, ([], []))
+                    if run and ops[run[-1]]["e"] != o["e"]:
+                        run, before = runs[name] = ([], run)
+                    if o["e"] == "P" and run:
+                        soft.add(run[-1])
+                    else:
+                        deps.update(before[-1:] if before and ops[before[0]]["e"] == "P" else before)
+                    run.append(i)
+                    continue
                 hist = seen.setdefault(name, [])
-                for j, m, l2, h2 in hist:
-                    if j == i:
-                        continue
-                    clash = (mode == "w" or m == "w") and l2 < hi and lo < h2
-                    if name in psum and ops[j]["e"] == o["e"] == "P":
-                        soft.add(j)
-                    elif clash or (name in psum and ops[j]["e"] != o["e"]):
-                        deps.add(j)
+                deps.update(j for j, m, l2, h2 in hist if j != i and (mode == "w" or m == "w") and l2 < hi and lo < h2)
                 if mode == "w":
-                    hist[:] = [x for x in hist if not (lo <= x[2] and x[3] <= hi) or name in psum and x[0] > i - 400]
+                    hist[:] = [x for x in hist if not (lo <= x[2] and x[3] <= hi)]
                 hist.append((i, mode, lo, hi))
         if o["after"] is not None:
             soft.add(o["after"])
         if o["e"] in "SG" or o["sem"]:
-            soft |= {j for j in range(i) if ops[j]["e"] == o["e"] and (ops[j]["sem"] or o["e"] == "G")}
+            soft |= set([j for j in range(i) if ops[j]["e"] == o["e"] and (ops[j]["sem"] or o["e"] == "G")][-1:])
+        soft.discard(i)
         o["deps"], o["pred"] = deps, deps | soft
+    kind = tuple(tuple(sorted(o["pred"])) for o in ops)
     if kind not in ORDERS:
         ORDERS[kind] = schedule(ops)
     out = ORDERS[kind]

from concourse.bass import DstId, RemoteDMATransfer
from concourse.mybir import AluOpType as OP, ActivationFunctionType as AF

N, V, NB, S0, TH, RO = 8, 896, 1792, 256, 256, 3
F32, BF, F16, I32, U16 = "float32", "bfloat16", "float16", "int32", "uint16"
SLOT, SENT = 40, 34
SEG = 18
HS = 8 * SEG
OFF = 34 * 4096
RATIO = 0.5546875
MAGIC = 12582912.0
TBD = 768
WIDTHS = {
    I32: dict(obi=16, reci=V, shi=448, bdi=S0, pi=8, lei=16, lli=8, ci=TH),
    U16: dict(le=16, ll=8, ow=48, cu=TH, oru=TH, sl=16, ox=16, oo=16, osa=16),
    BF: dict(sh1=448, shb=V + TH, boxw=NB + 2 * TH, v0=TH, drb=8, dg=144, one=128, none=128, em=512, idb=128, bo=128,
             bom=128, bo8k=128, idbig=128, dw=256, dk=256, ib=384, in23=128, ip22=128, in13=128, i64=128, i05=128,
             cst=128, kr=128, mh=144, g24=24, hi=432, lo=HS, thb=128, jm=128, dm=128, fc=160, fd=160, kpa=2 * HS,
             kpb=2 * HS, vt=256, vd=256, bd=8192, eq=4096, dh=512, dl=512, ha=TH, hn=TH, hta=TH, hw=TH, hm=128, flu=TH,
             thrn=TH, cb=TH, sr=3 * TH, rn=TH, na=TH, vis=TH, oh=256, ff=2 * HS, yy=TH, ys=TH, vout=TH),
    F16: dict(idh=128, es=512),
    F32: dict(rf=V + TH, tb=TBD + TH, drc=16, io=V, pc=16, idf=128, nidf=128, rm=128, vqx=160, hq=HS, e1=160, dmz=HS, fk=HS,
              p16=384, dmx=128, iw=16, kk=40, ww=24, me=16, owf=48, xd=512, xa=256, xs=512, sk=16, hv=TH, hr=TH,
              t2=256, tt=2 * HS, mm=2 * HS, s2=2 * HS, lq=512, a2=64, mc=TH, ea=TH, yhs=3 * TH),
}
SCRATCH = {k: ("sbuf", [128, n], d) for d, w in WIDTHS.items() for k, n in w.items()}
SCRATCH.update({k: ("sbuf", [128, 8, SLOT], F16) for k in ("snd0", "snd1", "rcv0", "rcv1")})
SCRATCH["e3"] = ("sbuf", [128, 16, SEG], F32)
SCRATCH.update({k: ("psum", [128, 512], F32) for k in ("pq0", "pq1", "pz", "pr", "pu0", "pu1", "pn", "py")})
SEMAPHORES = ["sD", "sA", "sP", "sG", "arr00", "arr01", "arr10", "arr11", "sent", "l_ob", "l_rec", "l_box", "l_tv", "l_dr",
              "l_bd", "l_sh", "o_yr", "o_yv", "o_h0", "o_h1", "o_h2"]

MODES = ["DADADADD", "AADDADDD", "AADDADDD"]
BANKS = ["pu0", "pu1", "pr", "pu0", "pu1", "pu0", "pu1", "pu0"]
STARTS, SHORT, ROUNDS, SEED, SHAKE, SLACK, SWAPS, STEP = 20, 25, 100, 5, 200, 250, 26000, 150
TERMS = ("ns", "cy", "gat", "sca", "pe", "dve", "act", "pool", "dma", "byte", "call", "deal", "first", "hop")
CASES = [(1, 0.83, 1.3, 3.15, 0.42, 25, 45, 100, 1600, 0.0045, 1000, 1900, 1500, 165),
         (1, 1.08, 2.0, 5.0, 0.54, 25, 45, 0, 1800, 0.005, 700, 2200, 2000, 190),
         (1, 0.83, 1.1, 2.1, 0.40, 35, 55, 400, 1500, 0.004, 1600, 2500, 2500, 230),
         (1, 0.83, 1.1, 2.1, 0.42, 20, 40, 0, 1550, 0.004, 700, 1500, 1000, 180)]
WEIGHTS = (1.2, 0.4, 0.5, 0.4)
ORDERS = {}


def masks_of(src, dsts, topo):
    far = [c for c in dsts if c not in topo.cores_of(src)]
    pool = [e for e in topo.engines(src, far[0]) if all(e in topo.engines(src, c) for c in far)]
    k = len(pool) // len(far)
    out = {c: pool[k * j:k * j + k] for j, c in enumerate(far)}
    for c in dsts:
        if c not in far:
            out[c] = [e for e in topo.engines(src, c) if e not in pool][:k]
    return out


def rank_program(g, core, T, topo):
    rank = T.rank_of(core)
    if rank is None:
        return
    cores = list(T.cores)
    ops = []
    psum = {k for k, s in SCRATCH.items() if s[0] == "psum"}
    own = rank // 4
    halves = (1 - own, own)

    def S(name, lo=None, hi=None, step=1, p=None):
        n = SCRATCH[name][1][1]
        lo = 0 if lo is None else lo
        hi = n if hi is None else hi
        rows = slice(None) if p is None else slice(p[0], p[1])
        ap = T[name][rows, lo:hi:step] if step != 1 else T[name][rows, lo:hi]
        return (ap, [(name, lo, hi)], len(range(lo, hi, step)), SCRATCH[name][2] in (BF, F16, U16))

    def S3(name, q0, q1, c0=0, c1=SEG):
        w = SCRATCH[name][1][2]
        ap = T[name][:, q0, c0:c1] if q1 == q0 + 1 else T[name][:, q0:q1, c0:c1]
        return (ap, [(name, q * w + c0, q * w + c1) for q in range(q0, q1)], (q1 - q0) * (c1 - c0), SCRATCH[name][2] != F32)

    def H(name, h, w=128):
        return S(name, w * h, w * h + w)

    def W(name, t, a=0, b=16):
        return S(name, 16 * t + a, 16 * t + b)

    def WH(name, t, h):
        return W(name, t, 8 * h, 8 * h + 8)

    def col(name, j):
        return S(name, j, j + 1)

    def IND(win, off):
        return (win[0].indirect(off[0]), win[1] + off[1], -16 * off[2], False, win, off)

    def val(x):
        return x[0] if isinstance(x, tuple) else x

    def keys(*xs):
        return [k for x in xs if isinstance(x, tuple) for k in x[1]]

    def add(eng, fn, rd, wr, cost, sem=None, inc=None, late={}, after=None):
        ops.append({"e": eng, "fn": fn, "rd": rd, "wr": wr, "sem": sem, "inc": inc, "cost": cost, "late": late, "after": after})

    def vec(fn, out, ins, k=1.0):
        if out[2] < 0:
            return add("D", fn, keys(*ins) + out[5][1], out[4][1], dict(ns=50, sca=-out[2]))
        a = ins[0] if ins else out
        if a[2] < 0:
            return add("D", fn, keys(*ins), keys(out), dict(ns=50, gat=out[2]))
        half = out[3] and all(x[3] for x in ins if isinstance(x, tuple) and x[2] > 1)
        add("D", fn, keys(*ins), keys(out), dict(dve=1, cy=max(64, k * out[2] * (0.5 if half else 1.0))))

    def cp(out, in_):
        vec(lambda: g.vector.tensor_copy(out[0], in_[0]), out, [in_])

    def tt(out, a, b, op):
        k = 1.0 if a[1][0][0] in psum or b[1][0][0] in psum else 2.0
        vec(lambda: g.vector.tensor_tensor(out[0], a[0], b[0], op), out, [a, b], k)

    def ts(out, a, s1, op0, s2=None, op1=None):
        if op1 is None:
            vec(lambda: g.vector.tensor_scalar(out[0], a[0], val(s1), None, op0), out, [a, s1])
        else:
            vec(lambda: g.vector.tensor_scalar(out[0], a[0], val(s1), val(s2), op0, op1), out, [a, s1, s2])

    def scan(out, d0, d1, init, op0, op1):
        vec(lambda: g.vector.tensor_tensor_scan(out[0], d0[0], d1[0], init, op0, op1), out, [d0, d1])

    def ms(out, c):
        vec(lambda: g.vector.memset(out[0], c), out, [])

    def act(out, a, func=AF.Copy, bias=0.0, scale=1.0):
        cost = dict(ns=65, gat=out[2]) if a[2] < 0 else dict(act=1, cy=max(64, out[2]))
        add("A", lambda: g.scalar.activation(out[0], a[0], func, bias=val(bias), scale=val(scale)), keys(a, bias, scale), keys(out),
            cost)

    def mm(out, lhsT, rhs, start=True, stop=True):
        add("P", lambda: g.tensor.matmul(out[0], lhsT[0], rhs[0], start, stop), keys(lhsT, rhs), keys(out),
            dict(pe=max(min(64, lhsT[2]), rhs[2]) * (1 if lhsT[3] else 4)))

    def fuse(k):
        part = ops[-k:]
        del ops[-k:]
        add("P", lambda: [o["fn"]() for o in part][-1], [x for o in part for x in o["rd"]], part[0]["wr"],
            dict(pe=sum(o["cost"]["pe"] for o in part)))

    def group(out, terms):
        for j, (lhsT, rhs) in enumerate(terms):
            mm(out, lhsT, rhs, j == 0, j == len(terms) - 1)

    def wrap(out, row, c0, more=()):
        group(out, [(S("dg", 15 - r, 143 - r), S(row, c0 + r, c0 + 16 * out[2], 16)) for r in range(16)] + list(more))
        fuse(16 + len(more))

    def iota(out, pattern, base, mult=0):
        if SCRATCH[out[1][0][0]][2] == I32:
            add("G", lambda: g.iota(out[0], pattern, base, mult), [], keys(out), dict(ns=130, cy=2 * out[2]))
        else:
            add("G", lambda: g.iota(out[0], pattern, base, mult, allow_small_or_imprecise_dtypes=True), [], keys(out),
                dict(ns=130, cy=2 * out[2]))

    def pick(out, in_, pattern, base, mult=1):
        add("G", lambda: g.affine_select(out[0], in_[0], pattern, OP.is_equal, 0.0, base, mult), keys(in_), keys(out),
            dict(ns=170, cy=2 * out[2], pool=mult == 0))

    def copy(out, in_):
        pick(out, in_, [[0, out[2]]], 0, 0)

    def diag(out, c):
        zero = S("hi", 2 * HS, 2 * HS + 128)
        add("G", lambda: g.affine_select(out[0], zero[0], [[-1, 128]], OP.not_equal, c, 0, 1), keys(zero), keys(out),
            dict(ns=170, cy=256))

    moved = [0]

    def dma(q, out, in_, sem, nbytes):
        eng = {"S": g.sync, "A": g.scalar, "G": g}[q]
        moved[0] = moved[0] + nbytes if sem[0] == "l" else nbytes
        add(q, lambda: eng.dma_start(val(out), val(in_)), keys(in_), keys(out), dict(ns=60), sem, 16,
            dict(dma=1, byte=moved[0]))

    dma("S", S("obi"), T.ob[:], "l_ob", 8192)
    dma("A", S("drb", 0, 3), T.dr[:], "l_dr", 4096)
    dma("A", S("shi", p=(0, 16)), T.shp[:], "l_sh", 32 * V)
    dma("S", S("v0"), T.tv[:], "l_tv", 65536)
    dma("S", S("reci"), T.rec[:], "l_rec", 512 * V)
    dma("S", S("boxw", 0, NB), T.box[:], "l_box", 256 * NB)
    dma("S", S("bdi"), T.bound[:], "l_bd", 512 * S0)

    pc = [col("pc", j) for j in range(16)]
    QM = S("kk", 32, 40)
    iota(S("pi", 0, 1), [[0, 1]], 0, 1)
    ms(S("one"), 1.0)
    ms(S("hi", HS, 432), 0.0)
    pick(S("idb"), S("one"), [[-1, 128]], 0)
    iota(S("bo"), [[1, 8], [0, 16]], 0)
    for h in range(2):
        pick(H("eq", h), S("one"), [[-2, 8], [0, 16]], -h)
    iota(S("io", 0, 256), [[1, 256]], 0)
    iota(S("iw"), [[16, 16]], 0)
    iota(S("em"), [[1, 32], [0, 16]], 0)
    iota(S("hi", 0, HS), [[-34, 8], [0, SEG]], 239)
    iota(S("lo"), [[0, 8], [1, SEG]], -17)
    iota(S("fc", 1, HS + 1), [[16, 8], [1, SEG]], -1)
    iota(S("fd", 1, HS + 1), [[16, 8], [1, SEG]], -1)
    iota(S("fc", 0, HS + 1, SEG), [[0, 9]], -5)
    iota(S("fd", SEG, HS + 1, SEG), [[16, 8]], 0)
    for k in ("fc", "fd"):
        iota(S(k, 1, HS + 2, SEG), [[0, 9]], -5)
    iota(S("thb"), [[-34, 8], [0, 16]], 239)
    iota(S("jm"), [[0, 8], [1, 16]], 0)
    iota(S("lli"), [[SEG, 8]], SEG - 1)
    iota(S("dh", 0, 256), [[1, 16], [0, 16]], 0)
    iota(S("dl", 0, 256), [[0, 16], [1, 16]], 0)
    ts(col("pi", 1), col("pi", 0), 15, OP.bitwise_and)
    ts(col("pi", 2), col("pi", 0), 4, OP.arith_shift_right)
    ts(col("pi", 3), col("pi", 0), 31, OP.bitwise_and)
    cp(S("pc", 0, 4), S("pi", 0, 4))
    ts(S("bo"), S("bo"), pc[2], OP.is_equal)
    ts(S("em"), S("em"), pc[3], OP.is_equal, -1.0, OP.mult)
    ts(QM, S("io", 0, 8), pc[2], OP.is_equal)
    for j, sc in enumerate((32.0, 2.0 ** 21, 1.0)):
        act(H("g24", j, 8), QM, scale=sc)
    ms(S("dg"), 0.0)
    cp(S("dg", 15, 143, 16), QM)
    ts(S("iw"), S("iw"), pc[1], OP.add)
    ms(S("cb"), RATIO)
    scan(S("thrn"), S("cb"), S("hi", 2 * HS - 112, 3 * HS), -2.0 ** 94, OP.mult, OP.min)
    wrap(S("pn", 0, 16), "thrn", 0)
    for h in halves:
        mm(S("pn", 16 + h, 17 + h), H("thrn", h), S("one", 0, 1))
    act(S("ww", 0, 16), S("pn", 0, 16), scale=-8 / 2.5)
    act(S("ww", 16, 18), S("pn", 16, 18), scale=-1 / 2.5)
    act(S("ww", 18, 20), S("pn", 16, 18), scale=2.0)
    ts(S("sh1", p=(0, 16)), S("shi", p=(0, 16)), -1.0, OP.mult, 256.0, OP.add)
    for h, bank in enumerate(("py", "pz")):
        mm(S(bank, 0, 448), S("eq", 128 * h, 128 * h + 128, p=(0, 16)), S("sh1", p=(0, 16)))
        act(H("shb", h, 448), S(bank, 0, 448))
    act(pc[4], pc[2], AF.Identity, bias=7.0 * OFF, scale=-float(OFF))
    act(pc[5], pc[0], AF.Identity, bias=-2040.0 - 2.0 ** 22, scale=16.0)
    act(pc[11], pc[0], AF.Identity, bias=-4096.0, scale=16.0)
    act(pc[14], pc[0], AF.Identity, bias=-4080.0, scale=16.0)
    act(S("hi", 0, HS), S("hi", 0, HS), scale=4096.0)
    ms(S("hi", 0, HS, SEG), 2.0 ** 22)
    group(S("pn", 0, HS), [(S("idb"), S("hi", 0, HS)), (S("idb"), S("lo"))])
    act(S("fk"), S("pn", 0, HS), AF.Identity, bias=pc[14])
    ts(S("fk", SEG - 1, HS, SEG), S("fk", SEG - 1, HS, SEG), 2039.0, OP.add)
    ms(S("hi", HS + SEG - 1, 2 * HS, SEG), 2.0 ** 21)
    ms(S("lo", SEG - 1, HS, SEG), 2.0 ** 22)
    act(S("thb"), S("thb"), scale=4096.0)
    ts(S("dm"), S("jm"), pc[1], OP.is_equal)
    ts(S("vqx", 0, HS + 1), S("fc", 0, HS + 1), pc[0], OP.is_equal, -2.0 ** 21, OP.mult)
    ts(S("e1", 1, HS + 2), S("fd", 1, HS + 2), pc[0], OP.is_equal, 2.0 ** -12, OP.mult)
    tt(S("dmz"), S("e1", 1, HS + 1), S("e1", 2, HS + 2), OP.subtract)
    ts(W("a2", 0), S("iw"), -8.5, OP.add, 1.0 / SEG, OP.mult)
    cp(S("lei"), W("a2", 0))
    cp(S("le"), S("lei"))
    cp(S("ll"), S("lli"))
    act(H("kk", 0, 16), S("iw"), AF.Identity, bias=V / 16.0, scale=1 / 16.0)
    act(H("kk", 1, 16), S("iw"), AF.Identity, bias=-14 - TBD / 4096.0, scale=-1 / 4096.0)
    act(S("drc", 12, 15), S("drb", 0, 3), scale=-1.0)
    act(S("drc", 1, 3), S("drb", 1, 3), AF.Identity, bias=128.0, scale=-1.0)
    act(S("drc", 4, 6), S("drb", 0, 2), AF.Identity, bias=-2.0, scale=1 / 128.0)
    act(S("drc", 6, 7), S("drb", 2, 3), AF.Identity, bias=-256.0)
    act(S("drc", 8, 10), S("drb", 0, 2), AF.Identity, bias=-255.5)
    act(S("drc", 10, 11), S("drb", 2, 3), AF.Identity, bias=256.0, scale=-1.0)
    for a in range(256, V, 256):
        act(S("io", a, min(V, a + 256)), S("io", 0, min(V - a, 256)), AF.Identity, bias=float(a))
    cp(S("tb", 0, S0), S("bdi"))
    ts(S("dh", 0, 256), S("dh", 0, 256), pc[1], OP.is_equal)
    ts(S("dl", 0, 256), S("dl", 0, 256), pc[1], OP.not_equal)
    for k, sc in (("ip22", 2.0 ** 22), ("nidf", -1.0), ("i64", 64.0), ("i05", 0.5), ("idf", 1.0), ("idh", 1.0)):
        diag(S(k), sc)
    diag(H("ib", 0), float(NB))
    group(S("pn", 0, 128), [(S("idb"), S("thb")), (S("ip22"), S("dm"))])
    act(S("dmx"), S("pn", 0, 128), AF.Relu, bias=pc[5])
    act(S("pc", 12, 14), S("io", 0, 129, 128), AF.Identity, bias=pc[0])
    for h in halves:
        act(H("dk", h), S("idb"), scale=pc[12 + h])
    ts(S("idbig"), S("idb"), 2.0 ** 99, OP.mult, 2.0 ** 13, OP.mult)
    act(S("bo8k"), S("bo"), scale=8192.0)
    act(S("bom"), S("bo"), AF.Identity, bias=-1.0)
    act(S("mh", 0, 128), S("one"), scale=-0.5)
    act(S("mh", 128, 136), S("one", 0, 8), scale=-0.3125)
    act(S("none"), S("one"), scale=-1.0)
    act(S("cst"), S("one"), scale=-53 * 512.0)
    for h in halves:
        act(H("dw", h), S("idb"), scale=col("ww", 18 + h))
    ts(pc[6], pc[1], 0.0, OP.is_equal, -2.0 ** 21, OP.mult)
    ts(pc[8], pc[1], 15.0, OP.is_equal, 2.0 ** 21, OP.mult)
    act(pc[7], pc[6], AF.Identity, bias=-2.0 ** 32, scale=2.0 ** 11)
    act(pc[9], pc[8], AF.Identity, bias=-2.0 ** 20, scale=0.5)
    act(pc[15], pc[8], AF.Identity, bias=-0.5, scale=-1019.5 * 2.0 ** -21)
    ts(pc[10], pc[6], -2.0 ** -17, OP.mult, pc[0], OP.add)
    act(S("kr"), S("idb"), scale=pc[15])
    for j in range(2):
        ts(H("kpa", j, HS), S("fc", 1, HS + 1), pc[0], OP.is_equal, pc[6 + j], OP.mult)
        ts(H("kpb", j, HS), S("fc", 0, HS), pc[0], OP.is_equal, pc[8 + j], OP.mult)
    tt(S("kpa"), S("kpa"), S("kpb"), OP.add)
    tt(S("hq"), S("vqx", 0, HS), S("vqx", 1, HS + 1), OP.subtract)
    ts(S("rm"), S("io", 1, 129), pc[10], OP.is_equal)

    def place(h, what):
        first = dict(dif=("pr", 0), box=("pz", 440), ref=("pr", 152), new=("pr", 160), one=("py", 0), turn=("py", 0))
        last = dict(dif=("pu0", 0), box=("pz", 448), ref=("pu0", 152), new=("pu0", 160), one=("pu1", 0),
                    turn=("pq%d" % halves[0], 0))
        bank, o = (first if h == halves[0] else last)[what]
        return S(bank, o, o + dict(dif=HS, box=8, ref=8, new=128, one=128, turn=256)[what])

    def pre(t, h):
        if t == 0:
            v = H("v0", h)
            cp(WH("ow", 0, h), H("obi", h, 8))
            ts(H("ci", h), IND(S("reci"), WH("ow", 0, h)), 4095, OP.bitwise_and)
        else:
            r = "rcv%d" % (t - 1)
            v = S3(r, 4 * h, 4 * h + 4, 0, 32)
            cp(WH("ow", t, h), S3(r, 4 * h, 4 * h + 4, 32, 34))
        act(H("xd", 2 * h), IND(S("rf", 0, V), WH("ow", t, h)))
        if t:
            cp(H("ci", h), H("xd", 2 * h) if h == own else IND(S("rf", 0, V), WH("ow", t, h)))
            ts(H("ci", h), H("ci", h), 4095, OP.bitwise_and)
        cp(H("cu", h), H("ci", h))
        if t:
            ts(H("vd", h), v, 128.0, OP.mult, col("drc", t), OP.add)
        else:
            act(H("vd", h), v, AF.Identity, bias=col("drc", 12))
        mm(H("pz", h), H("vd" if t else "v0", h), S("idb"))
        act(H("vt", h), H("pz", h))

    def chunk(t, h, k, j):
        src = IND(S("boxw", 0, NB + TH * t), H("cu", 4 * h + k, 32))
        dst = H("bd", 8 * h + k, 512)
        if MODES[t][j] == "D":
            cp(dst, src)
        else:
            act(dst, src)
        rows = (32 * k, 32 * k + 32)
        group(S(BANKS[j]), [(S("vt", 128 * h, 128 * h + 128, p=rows), S("em", p=rows)), (S("idb"), dst)])
        act(H("bd", 8 * h + 4 + k, 512), S(BANKS[j]), AF.Abs, bias=col("drc", 12 + t) if t else 0.0)

    def red(t, h):
        q, o, n = "pq%d" % h, 4096 * h + 2048, 17 if t else 16
        for u in range(n):
            mm(S(q, 1 + u, 432, SEG), S("bd", o + u % 16, o + 2048, 16), S("g24"), False, u == n - 1)
        fuse(n)
        put = cp if h == own else copy
        if t:
            put(S("bd", o + 7, o + 2048, 16), S("bd", o - 2048, o, 16))
        put(S("bd", o + 8, o + 2048, 16), H("vd", h))

    def shapes(t, h, n):
        P = S("pr", 480 + 8 * h, 480 + 8 * (h + n)) if n == 2 or h != own else S("pz", 416, 424)
        a, b = 128 * h, 128 * (h + n)
        act(S("sr", TH * t + a, TH * t + b), IND(S("shb", 0, V), W("ow", t, a // 16, b // 16)))
        wrap(P, "sr", TH * t + a)
        ts(S("sl", a // 16, b // 16), P, -1 / 16.0, OP.mult, 256.0, OP.add)
        if t == 0:
            act(S("sk"), P, AF.Identity, bias=-1 / 16.0, scale=2.0 ** -16)
        entry = IND(S("tb", 0, 256 if t < 2 else 512), S("sl", a // 16, b // 16))
        act(S("hv", a, b), entry)
        if t:
            act(S("hr", a, b), entry, AF.Relu, bias=-4096.0)
            act(S("rn", a, b), entry, AF.Sign, bias=4090.0, scale=-1.0)

    def bounds(t, h):
        q = "pq%d" % h
        mm(S(q, 0, 432), S("idb"), S("hi"), True, False)
        mm(H(q, 0, HS), S("idb"), S("lo"), False, False)
        if t:
            mm(S(q, 0, 2 * HS), S("none"), S("kpa"), False, False)
        mm(H(q, 1, HS), H("hv", h), S("vqx", 1, HS + 1), False, False)
        if t:
            mm(H(q, 1, HS), H("hr", h), S("hq"), False, False)
            mm(S(q, 0, 2 * HS), H("rn", h), S("kpa"), False, False)

    def seen(t, h):
        cp(H("xd", 2 * h + 1), H("ci", h))
        if t:
            bank = place(h, "turn")[1][0][0]
            group(H(bank, 0), [(S("ip22"), S("none")), (S("ip22"), H("rn", h))])
            for j in range(2):
                tt(H("xa", j), H(bank, 0), H("xd", 2 * h + j), OP.add)
            for j in range(2):
                mm(H(bank, 2 + j), S("in23"), H("rn", h), j == 0, False)
            mm(H(bank, 1, 256), S("rm"), S("xa"), False, True)
            tt(H("xs", h, 256), H(bank, 1, 256), S("xa"), OP.max)

    def fields(t, h):
        P = S("pz", 288, 416)
        if t:
            mm(P, H("rn", h), S("kr"))
            tt(H("p16", h), P, H("p16", 2), OP.add)
        else:
            group(P, [(S("idb"), S("thb")), (S("idb"), S("jm"))] + [(S("none"), S("kr"))] * (h == own))
            act(H("p16", 2 if h == own else h), P, AF.Identity, bias=pc[11])

    def objects(t):
        cp(W("owf", t), W("ow", t))
        cp(S("oru"), IND(S("io"), W("ow", t)))
        mm(S("pn", 0, 256), S("one"), S("thrn"), True, False)
        for q in range(16):
            e = S("eq", 272 * q, 256 * q + 256)
            ts(e, S("oru", 16 * q, TH), W("owf", t, q, q + 1), OP.is_equal, col("ww", q), OP.mult)
            mm(S("pn", 16 * q, 256), S("bo"), e, False, q == 15)
        act(S("cb"), S("pn", 0, 256), AF.Sign)
        wrap(S("pn", 256, 272), "cb", 0)
        tt(W("a2", 1), S("pn", 256, 272), H("kk", 0, 16), OP.mult)
        tt(W("a2", 1), W("a2", 1), W("owf", t), OP.max)
        cp(S("oo"), W("a2", 1))

    def digits(t):
        n = 256 if t < 2 else 512
        if t == 2:
            act(S("na"), IND(S("tb", 256, 768), S("sl")), AF.Sign, bias=-4090.0)
        act(S("ha"), IND(S("dh", 0, n), S("sl")))
        act(S("hn"), IND(S("dl", 0, n), S("sl")))
        for h in halves:
            mm(H("py", h), H("ha", h), S("idb"))
            group(H("py", 2 + h), [(S("idb"), S("thb")), (H("hn", h), S("ip22"))] + [(H("na", h), S("bo8k"))] * (t == 2))
        for h in halves:
            act(H("hta", h), H("py", h), scale=col("ww", 16 + h))
        act(S("t2"), S("py", 256, 512), AF.Identity, bias=-8.0 + (2.0 ** 17 if t == 2 else 0.0))

    def choose(t, h):
        q, M = "pq%d" % h, H("mm", h, HS)
        if t < 2:
            mm(place(h, "dif"), H("xd", 2 * h), S("dmz"))
        tt(H("tt", h, HS), H(q, 1, HS), S("fk"), OP.max)
        scan(M, H("tt", h, HS), H(q, 0, HS), 2.0 ** 23, OP.min, OP.min)
        tt(H("lq", h), IND(M, S("ll")), S("dmx"), OP.min)
        P = place(h, "box")
        mm(P, H("lq", h), QM)
        ts(H("ox", h, 8), P, pc[4], OP.subtract)
        act(S3("e3", 8 * h, 8 * h + 8), H(q, 2, HS), AF.Identity, bias=-2048.0)
        X = IND(H("bd", h, 4096), H("ox", h, 8))
        act(H("yy", h), X, AF.Identity, bias=col("drc", 4 + t), scale=1 / 128.0 if t < 2 else 1.0)
        if t == 2:
            ts(H("ys", h), X, col("drc", 10), OP.is_lt, 256.0, OP.mult)
            tt(H("vout", h), H("yy", h), H("ys", h), OP.add)
            return
        act(H("ys", h), X, AF.Sign, bias=col("drc", 8 + t))
        cp(H("me", h, 8), S("mm", HS * h + SEG - 1, HS * h + HS, SEG))
        tt(H("ff", h, HS), IND(H("me", h, 8), S("le", 0, 9)), M, OP.is_equal)
        scan(H("s2", h, HS), place(h, "dif"), H("ff", h, HS), 0.0, OP.add, OP.mult)
        tt(H("lq", 2 + h), IND(H("s2", h, HS), S("ll")), S("dm"), OP.mult)
        P = place(h, "ref")
        group(P, [(S("idb"), S("mh", 128, 136)), (H("lq", 2 + h), QM)])
        s = "snd%d" % t
        ts(S3(s, 4 * h, 4 * h + 4, 32, 34), P, MAGIC, OP.add, MAGIC, OP.subtract)
        tt(S3(s, 4 * h, 4 * h + 4, 0, 32), H("yy", h), H("ys", h), OP.subtract)

    def send(t, h):
        s, r, late = "snd%d" % t, "rcv%d" % t, int(h == own)
        sem = "arr%d%d" % (t, late)

        def plan(c, half):
            return masks_of(c, [d for d in cores[4 * half:4 * half + 4] if d != c], topo)
        mk = plan(core, h)
        trs = []
        for d, es in mk.items():
            rid, pid = topo.addr(d, core)
            trs.append(RemoteDMATransfer(dst_ids=[DstId(rid=rid, pnc=pid)], dma_engine_mask=sum(1 << e for e in es),
                                         remote_sem=T.sem[sem], src=T[s][:, cores.index(d), 0:SENT], dst=T[r][:, rank, 0:SENT]))
        add("G", lambda: g.remote_dma_fused(trs, local_sem=T.sem.sent), keys(S3(s, 4 * h, 4 * h + 4, 0, SENT)), [],
            dict(call=1, first=t + late == 0), "sent", -sum(len(m) for m in mk.values()))
        srcs = [q for q in range(4 * h, 4 * h + 4) if q != rank]
        n = sum(len(plan(cores[q], own)[core]) for q in srcs)
        add("X", None, [], [(r, q * SLOT, q * SLOT + SLOT) for q in srcs], {}, sem, -n, dict(deal=1), len(ops) - 1)
        if late:
            cp(S3(r, rank, rank + 1, 0, SENT), S3(s, rank, rank + 1, 0, SENT))

    def record(t, h):
        x = "xs" if t else "xd"
        tt(H("oh", h), IND(H("mm", h, HS), S("ll")), H("p16", h if t else halves[0]), OP.is_equal)
        group(place(h, "one"), [(S("nidf"), H(x, 2 * h + 1)), (H("oh", h), H("dk", h)), (H("oh", h), H("ib", t))])
        act(H("mc", h), place(h, "one"), AF.Relu)
        tt(IND(S("rf"), H("oo", h, 8)), H(x, 2 * h), H("mc", h), OP.add)

    def newbox(t, h):
        P = place(h, "new")
        group(P, [(S("i05"), S("mh", 0, 128)), (S("i05"), H("vd", h)), (S("i64"), H("yy", h))])
        act(H("lq", h), P, AF.Identity, bias=MAGIC + 128)
        act(H("boxw", 14 + 2 * t + h), H("lq", h), AF.Identity, bias=-MAGIC)

    def askers(t, h):
        tt(H("hw", h), IND(H("mm", h, HS), S("ll")), H("t2", h), OP.is_ge)
        for j in range(1 + (t > 0)):
            part = (H("es", 2 * j + h), S3("e3", 8 * h, 8 * h + 8, 1 + j, 17 + j))
            if h == own and j == 0 and t == 2:
                cp(*part)
            else:
                copy(*part)

    def makers(t):
        group(H("pn", 0), [(S("idbig"), S("bom"))] + [(H("hta", h), H("hw", h)) for h in halves])
        act(S("hm"), H("pn", 0), AF.Relu)
        P = S("pn", 256, 512)
        mm(P, S("idbig"), S("hn"), True, False)
        for h in halves:
            mm(H("pn", 2 + h), H("hw", h), H("dw", h), False, False)
        mm(P, S("none"), S("thrn"), False, False)
        mm(P, S("hm"), S("ha"), False, True)
        act(S("flu"), P, AF.Sign, scale=-1.0)
        for j in range(1 + (t > 0)):
            q = "pq%d" % ((own + j) % 2)
            for h in halves:
                mm(H(q, h), H("es", 2 * j + h), S("idh"), h != own, False)
            if t:
                mm(S(q, 0, 256), S(("ip22", "in13")[j]), S("rn"), False, False)
            if j:
                mm(S(q, 0, 256), S("cst"), S("em", 0, 256), False, False)
            mm(S(q, 0, 256), S("bo8k"), S("flu"), False, True)
        if t:
            act(S("ea"), S("pq%d" % own, 0, 256), AF.Relu, bias=14 * 8192.0 + 2048 - 2.0 ** 22)
            tt(H("yhs", t, TH), S("pq%d" % (1 - own), 0, 256), S("ea"), OP.max)
        else:
            act(H("yhs", t, TH), S(q, 0, 256), AF.Relu, bias=14 * 8192.0 + 2048)
        dma("S", T.yh[:, TH * t:TH * t + TH], H("yhs", t, TH), "o_h%d" % t, 512 * TH)
        if t == 2:
            return
        P = S("pn", 0, 16)
        wrap(P, "flu", 0, [(S("idf"), S("sk"))])
        tt(W("a2", 3), P, H("kk", 1, 16), OP.max)
        ts(S("osa"), W("a2", 3), -4096.0, OP.mult, -14 * 4096.0, OP.add)
        ts(IND(S("tb"), S("osa")), H("yhs", t, TH), 1.0, OP.mult, 4097.0, OP.add)
        if t == 0:
            act(S("tb", 256, 512), S("tb", 0, 256), AF.Relu, bias=-4097.0)
            iota(S("tb", 512, 768), [[0, 256]], 0)
            for k in ("dh", "dl"):
                copy(S(k, 256, 512), S(k, 0, 256))

    cp(S("rf", 0, V), S("reci"))
    for t in range(RO):
        for h in halves:
            pre(t, h)
            if t:
                shapes(t, h, 1)
        if t == 0:
            shapes(t, 0, 2)
        for h in halves:
            bounds(t, h)
        seen(t, halves[0])
        objects(t)
        for j, h in enumerate(halves):
            for k in range(4):
                chunk(t, h, k, 4 * j + k)
            red(t, h)
            fields(t, h)
        if t == 1:
            group(S("pz", 0, 256), [(S("idb"), H("sr", 1, TH)), (S("i64"), S("rn")), (S("i64"), S("rn"))])
            act(S("vis"), S("pz", 0, 256), AF.Identity, bias=-128.0)
            wrap(S("pz", 424, 440), "vis", 0)
            act(S("sk"), S("pz", 424, 440), AF.Identity, bias=-1 / 16.0, scale=2.0 ** -16)
            cp(IND(S("shb"), S("oo")), S("vis"))
        for h in halves:
            choose(t, h)
            if h != own:
                seen(t, own)
            record(t, h)
            if h != own:
                digits(t)
            askers(t, h)
            if t < 2:
                send(t, h)
                newbox(t, h)
        if t == 2:
            dma("S", T.yr[:], S("rf", 0, V), "o_yr", 512 * V)
            dma("S", T.yv[:], S("vout"), "o_yv", 65536)
        for h in range(2 * (t == 0)):
            diag(S(("in13", "in23")[h]), -2.0 ** (13 + 10 * h))
            diag(H("ib", 1 + h), float(NB + TH * (1 + h)))
        makers(t)

    emit(g, T, order(ops, psum))


def schedule(ops):
    n = len(ops)
    cases = []
    for case in CASES:
        ns = dict(zip(TERMS, case))
        cost, late = ([sum(ns[k] * x for k, x in o[key].items()) for o in ops] for key in ("cost", "late"))
        cases.append((cost, late, [[(j, ns["hop"] + late[j] if j in o["deps"] else 0) for j in o["pred"]] for o in ops]))
    cost, late, lag = cases[0][0], cases[0][1], [dict(x) for x in cases[0][2]]

    eng = [o["e"] for o in ops]
    outs = [i for i, o in enumerate(ops) if o["sem"] and o["sem"][0] == "o"]

    def judge(line, at=0, known=None):
        span, ends = 0.0, []
        for c, (cost, late, need) in enumerate(cases):
            end = list(known[c]) if at else [0.0] * n
            free = {eng[i]: end[i] for i in line[:at]}
            for i in line[at:]:
                s = free.get(eng[i], 0.0)
                for j, x in need[i]:
                    if end[j] + x > s:
                        s = end[j] + x
                end[i] = free[eng[i]] = s + cost[i]
            span += WEIGHTS[c] * max(end[i] + late[i] for i in outs)
            ends.append(end)
        return span / sum(WEIGHTS), ends

    back = [{} for _ in ops]
    for i in range(n):
        for j, x in lag[i].items():
            back[j][i] = x

    def place(before, after, rank, tail):
        left = [len(b) for b in before]
        ready = list(tail)
        pool = sorted((-rank[i], i) for i in range(n) if not left[i])
        busy, end = {}, [0.0] * n
        while pool:
            i = pool.pop()[1]
            row = busy.setdefault(ops[i]["e"], [])
            s, c, at = ready[i], cost[i], 0
            for a, b in row:
                if a >= s + c:
                    break
                s = max(s, b)
                at += 1
            row.insert(at, (s, s + c))
            end[i] = s + c
            for k, x in after[i].items():
                ready[k] = max(ready[k], end[i] + x)
                left[k] -= 1
                if not left[k]:
                    pool.append((-rank[k], k))
            pool.sort()
        return end

    seed = SEED
    best = now = None
    for turn in range(STARTS * SHORT + ROUNDS):
        if turn <= STARTS * SHORT and turn % SHORT == 0:
            now = best[2] if turn == STARTS * SHORT else None
            end = now[1] if now else [float(i) for i in range(n)]
        shake = []
        for x in end:
            seed = (seed * 1103515245 + 12345) % 2147483648
            shake.append(-x - SHAKE * (1 + turn % 4) * seed / 2147483648)
        rev = place(back, lag, shake, late)
        end = place(lag, back, [-x for x in rev], [0.0] * n)
        line = sorted(range(n), key=lambda i: (end[i] - cost[i], end[i], i))
        span = judge(line)[0]
        if best is None or span < best[0]:
            best = (span, line, (span, end))
        if now is None or span < now[0] + SLACK * (1 - turn / (STARTS * SHORT + ROUNDS)):
            now = (span, end)
        end = now[1]

    def neighbours(line, end, cost, late, need):
        prev, last = [-1] * n, {}
        for i in line:
            prev[i] = last.get(eng[i], -1)
            last[eng[i]] = i
        i, arcs = max(outs, key=lambda k: end[k] + late[k]), []
        while i >= 0:
            ways = [(end[j] + x, j) for j, x in need[i]] + [(end[prev[i]] if prev[i] >= 0 else -1.0, prev[i])]
            j = max(ways)[1]
            if j == prev[i] >= 0 and j not in lag[i]:
                arcs.append((j, i))
            i = j
        return arcs

    line = best[1]
    now, ends = judge(line)
    for turn in range(SWAPS):
        seed = (seed * 1103515245 + 12345) % 2147483648
        if turn % 8 == 0:
            c = turn // 8 % len(cases)
            arcs = neighbours(line, ends[c], *cases[c])
        u, v = arcs[(seed >> 8) % len(arcs)]
        a, b = line.index(u), line.index(v)
        ahead, wanted, queues = [v], set(lag[v]), {eng[v]}
        for i in line[b - 1:a:-1]:
            if i in wanted or eng[i] in queues:
                ahead.append(i)
                wanted.update(lag[i])
                queues.add(eng[i])
        if a > b or u in wanted:
            continue
        moved = set(ahead)
        trial = line[:a] + ahead[::-1] + [i for i in line[a:b] if i not in moved] + line[b + 1:]
        span, new = judge(trial, a, ends)
        if span <= now + STEP * (1 - turn / SWAPS):
            now, line, ends = span, trial, new
            if now < best[0]:
                best = (now, line)
    return best[1]


def order(ops, psum):
    seen, runs = {}, {}
    for i, o in enumerate(ops):
        deps, soft = set(), set()
        for mode, ks in (("r", o["rd"]), ("w", o["wr"])):
            for name, lo, hi in ks:
                if name in psum:
                    run, before = runs.setdefault(name, ([], []))
                    if run and ops[run[-1]]["e"] != o["e"]:
                        run, before = runs[name] = ([], run)
                    if o["e"] == "P" and run:
                        soft.add(run[-1])
                    else:
                        deps.update(before[-1:] if before and ops[before[0]]["e"] == "P" else before)
                    run.append(i)
                    continue
                hist = seen.setdefault(name, [])
                deps.update(j for j, m, l2, h2 in hist if j != i and (mode == "w" or m == "w") and l2 < hi and lo < h2)
                if mode == "w":
                    hist[:] = [x for x in hist if not (lo <= x[2] and x[3] <= hi)]
                hist.append((i, mode, lo, hi))
        if o["after"] is not None:
            soft.add(o["after"])
        if o["e"] in "SG" or o["sem"]:
            soft |= set([j for j in range(i) if ops[j]["e"] == o["e"] and (ops[j]["sem"] or o["e"] == "G")][-1:])
        soft.discard(i)
        o["deps"], o["pred"] = deps, deps | soft
    kind = tuple(tuple(sorted(o["pred"])) for o in ops)
    if kind not in ORDERS:
        ORDERS[kind] = schedule(ops)
    out = ORDERS[kind]
    place = {i: k for k, i in enumerate(out)}
    for o in ops:
        o["deps"] = {place[j] for j in o["deps"]}
    return [ops[i] for i in out]


def emit(g, T, ops):
    queue = {"D": g.vector, "A": g.scalar, "P": g.tensor, "G": g, "S": g.sync}
    total = {}
    for o in ops:
        if o["sem"]:
            total[o["sem"]] = total.get(o["sem"], 0) + abs(o["inc"])
    known = {e: {} for e in queue}
    for o in ops:
        o["waits"] = []
        if o["e"] == "X":
            continue
        need = {}
        for j in o["deps"]:
            k = ops[j]["sem"] or ops[j]["e"]
            need[k] = max(need.get(k, -1), j)
        kn = known[o["e"]]
        for k, j in sorted(need.items(), key=lambda x: -x[1]):
            if kn.get(k, -1) < j:
                o["waits"].append(j)
                ops[j]["mark"] = True
                for k2, j2 in ops[j].get("clock", {}).items():
                    kn[k2] = max(kn.get(k2, -1), j2)
                kn[k] = len(ops) if ops[j]["sem"] else j
        o["clock"] = dict(kn)
    count = {e: 0 for e in queue}
    waited = set()
    for o in ops:
        if o["e"] == "X":
            continue
        q = queue[o["e"]]
        for j in o["waits"]:
            d = ops[j]
            if d["sem"]:
                q.wait_ge(T.sem[d["sem"]], total[d["sem"]])
                waited.add(d["sem"])
            else:
                q.wait_ge(T.sem["s" + d["e"]], d["n"])
        ins = o["fn"]()
        if o["sem"]:
            if o["inc"] > 0:
                ins.then_inc(T.sem[o["sem"]], o["inc"])
        elif o.get("mark"):
            count[o["e"]] += 1
            o["n"] = count[o["e"]]
            ins.then_inc(T.sem["s" + o["e"]], 1)
    for s, n in total.items():
        if s not in waited:
            g.wait_ge(T.sem[s], n)
